import numpy as np
import ml_dtypes


def mxq(x, axis, fmt="e4m3"):
    dtype, down = {"e4m3": (ml_dtypes.float8_e4m3fn, 7), "e5m2": (ml_dtypes.float8_e5m2, 14)}[fmt]
    v = np.moveaxis(np.asarray(x, np.float32).astype(ml_dtypes.bfloat16).astype(np.float64), axis, -1)
    blocks = v.reshape(v.shape[:-1] + (-1, 32))
    amax = np.abs(blocks).max(-1, keepdims=True)
    byte = np.maximum(np.where(amax > 0, np.frexp(amax)[1] - 1 + 127, 0) - down, 1)
    scale = np.exp2(byte - 127.0)
    codes = (blocks / scale).astype(np.float32).astype(dtype).astype(np.float64)
    return np.moveaxis((codes * scale).reshape(v.shape), -1, axis)


WIDE = False


def mx_kscale(k):
    if not WIDE:
        return np.ones(k)
    levels = np.array([10, -10, 5, -5, 0])
    if k % 512:
        return np.exp2(np.random.permutation(np.resize(levels, k // 32))).repeat(32)
    a = np.empty((k // 512, 16))
    for p in range(k // 512):
        a[p, :8] = np.random.permutation(np.resize(levels, 8))
        for g in range(8):
            far = levels[np.abs(levels - a[p, g]) >= 10]
            a[p, g + 8] = far[np.random.randint(len(far))]
    return np.exp2(a.ravel()).repeat(32)


BF16 = ml_dtypes.bfloat16


def bf(x):
    return np.asarray(x, np.float32).astype(BF16)


def f64(x):
    return np.asarray(x).astype(np.float64)


E2M1 = np.array([0.0, 0.5, 1.0, 1.5, 2.0, 3.0, 4.0, 6.0, -0.0, -0.5, -1.0, -1.5, -2.0, -3.0, -4.0, -6.0])


def pack_weight(w, fmt):
    k, n = w.shape
    w = f64(bf(w)).reshape(k // 32, 32, n)
    amax = np.abs(w).max(1)
    if fmt == "e4m3":
        byte = np.frexp(amax)[1] - 1 + 127 - 7
    else:
        mant, ex = np.frexp(amax / 6.0)
        byte = np.where(mant > 0.5, ex, ex - 1) + 127
    byte = np.clip(np.where(amax > 0, byte, 1), 1, 254)
    scaled = (w * np.exp2(127.0 - byte)[:, None, :]).reshape(k, n).astype(np.float32)
    by_word = np.ascontiguousarray(scaled.reshape(k // 512, 128, 4, n).transpose(0, 1, 3, 2))
    if fmt == "e4m3":
        words = by_word.astype(ml_dtypes.float8_e4m3fn).view(np.uint8)
    else:
        c = by_word.astype(ml_dtypes.float4_e2m1fn).view(np.uint8) & 0xF
        words = c[..., 0::2] | (c[..., 1::2] << 4)
    return np.ascontiguousarray(words), np.ascontiguousarray(byte.astype(np.uint8).reshape(k // 512, 16, n))


def unpack_weight(words, scales, fmt):
    g, p, n, _ = words.shape
    if fmt == "e4m3":
        vals = np.ascontiguousarray(words).view(ml_dtypes.float8_e4m3fn).astype(np.float64)
    else:
        nib = np.empty((g, p, n, 4), np.uint8)
        nib[..., 0::2] = words & 0xF
        nib[..., 1::2] = words >> 4
        vals = E2M1[nib]
    vals = vals * np.repeat(np.exp2(scales.astype(np.float64) - 127.0), 8, axis=1)[..., None]
    return vals.transpose(0, 1, 3, 2).reshape(g * 512, n)
def pack4(w):
    words, scales = pack_weight(w, "e2m1")
    return words.reshape(words.shape[0], 128, -1), scales


def unpack4(words, scales):
    return unpack_weight(words.reshape(words.shape[0], 128, -1, 2), scales, "e2m1")


T, C, N, R = 2048, 1024, 1024, 1024


def draw0():
    s = mx_kscale(C)
    u = mx_kscale(T)
    echo = np.random.standard_normal((T, C)) * s * u[:, None]
    steer = np.random.standard_normal((C, N)) / np.sqrt(C) / s[:, None]
    stored = np.random.standard_normal((T, R)) / np.sqrt(T) / u[:, None]
    ref_words, ref_scales = pack4(stored)
    return {
        "echo": bf(echo),
        "steer": bf(steer),
        "ref_words": ref_words,
        "ref_scales": ref_scales,
        "col_gain": bf(1 + 0.1 * np.random.standard_normal(N)),
        "row_gain": bf(1 + 0.1 * np.random.standard_normal(R)),
    }


def core(echo, steer, ref_words, ref_scales, col_gain, row_gain):
    y = mxq(f64(echo), 1, "e4m3") @ mxq(f64(steer), 0, "e4m3")
    d = y * f64(col_gain)[None, :]
    stored = unpack4(ref_words, ref_scales)
    c = stored.T @ mxq(d, 0, "e4m3")
    e = c * f64(row_gain)[:, None]
    return np.square(e)


def e4m3fn_bytes(y):
    return np.clip(np.asarray(y, np.float64), -448.0, 448.0).astype(np.float32).astype(ml_dtypes.float8_e4m3fn).view(np.uint8)


def e4m3fn_values(b):
    return np.asarray(b, np.uint8).view(ml_dtypes.float8_e4m3fn).astype(np.float64)


def setup_inputs():
    d = draw0()
    x0 = np.asarray(d['steer']).astype(np.float64)
    s = (np.max(np.abs(x0), axis=(1,), keepdims=True) / 448.0).astype(np.float32)
    out = {}
    for k, v in d.items():
        if k == 'steer':
            out['steer_bytes'] = e4m3fn_bytes(x0 / s.astype(np.float64))
            out['steer_scale'] = s
        else:
            out[k] = v
    return out


def reference(echo, steer_bytes, steer_scale, ref_words, ref_scales, col_gain, row_gain):
    return core(echo, e4m3fn_values(steer_bytes) * steer_scale.astype(np.float64), ref_words, ref_scales, col_gain, row_gain)

@@ -1,0 +1,380 @@
+from contextlib import ExitStack
+
+import concourse.mybir as mybir
+from concourse.masks import make_identity
+
+T, C, N, R = 2048, 1024, 1024, 1024
+FLOPS = 2 * T * C * N + 2 * T * R * N
+
+F32 = mybir.dt.float32
+BF16 = mybir.dt.bfloat16
+U32 = mybir.dt.uint32
+I32 = mybir.dt.int32
+U8 = mybir.dt.uint8
+FP8 = mybir.dt.float8_e4m3fn
+FP8X4 = mybir.dt.float8_e4m3fn_x4
+FP4X4 = mybir.dt.float4_e2m1fn_x4
+COPY = mybir.ActivationFunctionType.Copy
+SQUARE = mybir.ActivationFunctionType.Square
+MULT = mybir.AluOpType.mult
+
+P = 128
+G = T // 512
+CP = C // 512
+HALF = 512
+SORTED = (2, 3)
+HEAT = 16
+
+
+def tile_sonar_ping_coherence_s13_kernel(tc, echo, steer_bytes, steer_scale, ref_words, ref_scales, col_gain, row_gain, out):
+    nc = tc.nc
+    with ExitStack() as ctx:
+        keep = ctx.enter_context(tc.tile_pool(name="keep", bufs=1))
+        ring = ctx.enter_context(tc.tile_pool(name="ring", bufs=4))
+        stage = ctx.enter_context(tc.tile_pool(name="stage", bufs=8))
+        lift = ctx.enter_context(tc.tile_pool(name="lift", bufs=2))
+        psum = ctx.enter_context(tc.psum_pool(name="psum", bufs=4))
+        ctx.enter_context(tc.manual_schedule())
+
+        eraw = [keep.tile([P, 4, C], BF16, name="eraw%d" % g, align_bytes=256) for g in range(G)]
+        egrp = {}
+        ecod = [keep.tile([P, 4 * CP * P], U32, name="ecod%d" % g, align_bytes=256) for g in range(G)]
+        escl = [keep.tile([P, 4 * CP * P], U8, name="escl%d" % g, align_bytes=256) for g in range(G)]
+        esort = {g: keep.tile([P, 4, C // 2], F32, name="esort%d" % g, align_bytes=256) for g in SORTED}
+        sraw = keep.tile([P, CP, 4, N], U8, name="sraw", align_bytes=256)
+        sscl = keep.tile([P, CP, 4], F32, name="sscl", align_bytes=256)
+        swide = [keep.tile([P, 4, HALF], BF16, name="swide%d" % j, align_bytes=256) for j in range(2 * CP)]
+        sgrp = [keep.tile([P, HALF, 4], BF16, name="sgrp%d" % j, align_bytes=256) for j in range(2 * CP)]
+        scod = [keep.tile([P, N], U32, name="scod%d" % c, align_bytes=256) for c in range(CP)]
+        sqsc = [keep.tile([P, N], U8, name="sqsc%d" % c, align_bytes=256) for c in range(CP)]
+        dcod = [keep.tile([P, N], U32, name="dcod%d" % g, align_bytes=256) for g in range(G)]
+        dscl = [keep.tile([P, N], U8, name="dscl%d" % g, align_bytes=256) for g in range(G)]
+        pcod = keep.tile([P, G, 2 * R], U8, name="pcod", align_bytes=256)
+        pscl = keep.tile([P, G, R], U8, name="pscl", align_bytes=256)
+        gains = keep.tile([P, HALF + P], BF16, name="gains", align_bytes=256)
+        ones = keep.tile([P, P], BF16, name="ones", align_bytes=256)
+        idf = keep.tile([P, P], F32, name="idf", align_bytes=256)
+        idb = keep.tile([P, P], BF16, name="idb", align_bytes=256)
+        cgain1 = keep.tile([P, HALF], BF16, name="cgain1", align_bytes=256)
+        cgain = keep.tile([P, HALF], F32, name="cgain", align_bytes=256)
+        rgain = keep.tile([P, R // P], F32, name="rgain", align_bytes=256)
+
+        def bank(tag):
+            return psum.tile([P, 512], F32, name="bank_" + tag, tag=tag)
+
+        nc.vector.memset(ones[:], 1.0)
+        nc.vector.memset(gains[:], 0.0)
+        make_identity(nc, idf[:])
+        nc.vector.memset(pscl[:].rearrange("p g n -> p (g n)").bitcast(I32), 0)
+        nc.gpsimd.tensor_copy(out=idb[:], in_=idf[:])
+
+        echo_g = echo.rearrange("(g p t) k -> g p t k", p=P, t=4)
+        steer_c = steer_bytes.rearrange("(c p t) n -> c p t n", p=P, t=4)
+
+        def load_echo(g, t0, t1):
+            nc.sync.dma_start(out=eraw[g][:, t0:t1, :], in_=echo_g[g][:, t0:t1, :])
+
+        def load_steer(c, h):
+            cols = slice(h * HALF, (h + 1) * HALF)
+            nc.sync.dma_start(out=sraw[:, c, :, cols], in_=steer_c[c][:, :, cols])
+
+        nc.scalar.dma_start(out=sscl[:], in_=steer_scale.rearrange("(c p t) o -> p c (t o)", p=P, t=4))
+        load_steer(0, 0)
+        load_steer(1, 0)
+        for t in range(4):
+            load_echo(0, t, t + 1)
+        nc.scalar.dma_start(out=gains[0:1, 0:HALF], in_=col_gain[0:HALF].unsqueeze(0))
+        nc.scalar.dma_start(out=gains[0 : R // P, HALF : HALF + P], in_=row_gain.rearrange("(c m) -> c m", m=P))
+        for t in range(4):
+            load_echo(1, t, t + 1)
+        for g in range(2, G):
+            load_echo(g, 0, 2)
+            load_echo(g, 2, 4)
+        def load_words(g):
+            nc.sync.dma_start(out=pcod[:, g, :].bitcast(I32), in_=ref_words[g].bitcast(I32))
+
+        load_words(0)
+        for q4 in range(4):
+            nc.sync.dma_start(
+                out=pscl[32 * q4 : 32 * q4 + 4, :, :].bitcast(I32),
+                in_=ref_scales[:, 4 * q4 : 4 * q4 + 4, :].rearrange("g r n -> r g n").bitcast(I32),
+            )
+        load_words(1)
+        load_steer(0, 1)
+        load_steer(1, 1)
+        nc.sync.dma_start(out=cgain1[:], in_=col_gain[HALF:N].partition_broadcast(P))
+        load_words(2)
+        load_words(3)
+
+        def widen(c, h, ts, on_vector):
+            dst = swide[2 * c + h]
+            for t in ts:
+                src = sraw[:, c, t, h * HALF : (h + 1) * HALF].bitcast(FP8)
+                if on_vector:
+                    nc.vector.tensor_scalar(out=dst[:, t, :], in0=src, scalar1=sscl[:, c, t : t + 1], scalar2=None, op0=MULT)
+                else:
+                    nc.scalar.activation(out=dst[:, t, :], in_=src, func=COPY, scale=sscl[:, c, t : t + 1])
+
+        def interleave(c, h, on_vector):
+            src = swide[2 * c + h][:].rearrange("p t (n i) -> p n t i", i=4)
+            dst = sgrp[2 * c + h][:].rearrange("p (n i) t -> p n t i", i=4)
+            if on_vector:
+                nc.vector.tensor_copy(out=dst, in_=src)
+            else:
+                nc.scalar.copy(out=dst, in_=src)
+
+        def quant_steer(c, h):
+            cols = slice(h * HALF, (h + 1) * HALF)
+            nc.vector.quantize_mx(out=scod[c][:, cols].bitcast(FP8X4), scales=sqsc[c][:, cols], in_=sgrp[2 * c + h][:].rearrange("p n t -> p (n t)"))
+
+        def sort_words(g, t, on_vector=False):
+            if g in SORTED:
+                words = eraw[g][:, t, :].bitcast(F32)
+                copy = nc.vector.tensor_copy if on_vector else nc.scalar.copy
+                copy(out=esort[g][:, t, :].rearrange("p (c u m) -> p c u m", c=CP, u=2), in_=words.rearrange("p (c m u) -> p c u m", c=CP, u=2))
+
+        def turn(g, t):
+            xt = bank("a")
+            words = eraw[g][:, t, :].bitcast(F32)
+            for c in range(CP):
+                for u in range(2):
+                    j = 2 * c + u
+                    src = esort[g][:, t, j * P : (j + 1) * P] if g in SORTED else words[:, 256 * c + u : 256 * (c + 1) : 2]
+                    nc.tensor.transpose(xt[:, j * P : (j + 1) * P], src, idf[:])
+            if t % 2 == 0:
+                egrp[2 * g + t // 2] = ring.tile([P, 2, C], BF16, name="egrp", tag="egrp", align_bytes=256)
+            dst = egrp[2 * g + t // 2][:, t % 2, :].bitcast(F32)
+            nc.scalar.copy(out=dst.rearrange("p (c r u) -> p c r u", c=CP, u=2), in_=xt[:].rearrange("p (c u r) -> p c r u", c=CP, u=2))
+
+        def quant_echo(g, half):
+            cols = slice(half * 512, (half + 1) * 512)
+            nc.vector.quantize_mx(out=ecod[g][:, cols].bitcast(FP8X4), scales=escl[g][:, cols], in_=egrp[2 * g + half][:].rearrange("p t k -> p (t k)"))
+
+        ybank = {}
+        dgrp = {}
+
+        def first(g, b):
+            y = bank("b")
+            ybank[(g, b)] = y
+            ncols = slice(b * P, (b + 1) * P)
+            for t in range(4):
+                for c in range(CP):
+                    ecols = slice((t * CP + c) * P, (t * CP + c + 1) * P)
+                    nc.tensor.matmul_mx(
+                        out=y[:, t * P : (t + 1) * P],
+                        lhsT=ecod[g][:, ecols].bitcast(FP8X4),
+                        lhsT_scale=escl[g][:, ecols],
+                        rhs=scod[c][:, ncols].bitcast(FP8X4),
+                        rhs_scale=sqsc[c][:, ncols],
+                        start=(c == 0),
+                        stop=(c == CP - 1),
+                    )
+
+        def gain(g, b):
+            if b % 2 == 0:
+                dgrp[(g, b // 2)] = ring.tile([P, 2, P, 4], BF16, name="dgrp", tag="dgrp", align_bytes=256)
+            d = dgrp[(g, b // 2)]
+            nc.vector.tensor_tensor(
+                out=d[:, b % 2, :, :],
+                in0=ybank[(g, b)][:].rearrange("p (t n) -> p n t", t=4),
+                in1=cgain[:, b * P : (b + 1) * P].unsqueeze(2).to_broadcast([P, P, 4]),
+                op=MULT,
+            )
+
+        def quant_d(g, b2):
+            cols = slice(b2 * 2 * P, (b2 + 1) * 2 * P)
+            nc.vector.quantize_mx(out=dcod[g][:, cols].bitcast(FP8X4), scales=dscl[g][:, cols], in_=dgrp[(g, b2)][:].rearrange("p b n t -> p (b n t)"))
+
+        lifted = {}
+
+        def first_wide(g):
+            lifted[g] = lift.tile([P, 4, HALF], F32, name="lifted", tag="lifted", align_bytes=256)
+            for t in range(4):
+                yb = bank("b")
+                for c in range(CP):
+                    ecols = slice((t * CP + c) * P, (t * CP + c + 1) * P)
+                    nc.tensor.matmul_mx(
+                        out=yb[:],
+                        lhsT=ecod[g][:, ecols].bitcast(FP8X4),
+                        lhsT_scale=escl[g][:, ecols],
+                        rhs=scod[c][:, HALF:N].bitcast(FP8X4),
+                        rhs_scale=sqsc[c][:, HALF:N],
+                        start=(c == 0),
+                        stop=(c == CP - 1),
+                    )
+                nc.scalar.copy(out=lifted[g][:, t, :], in_=yb[:])
+
+        def gain_wide(g, b2):
+            d = ring.tile([P, 2, P, 4], BF16, name="dgrp", tag="dgrp", align_bytes=256)
+            dgrp[(g, b2)] = d
+            n0 = (b2 - 2) * 256
+            nc.vector.tensor_tensor(
+                out=d[:].rearrange("p b (n i) t -> p (b n) t i", i=4),
+                in0=lifted[g][:, :, n0 : n0 + 256].rearrange("p t (n i) -> p n t i", i=4),
+                in1=cgain1[:, n0 : n0 + 256].rearrange("p (n i) -> p n i", i=4).unsqueeze(2).to_broadcast([P, 64, 4, 4]),
+                op=MULT,
+            )
+
+        acc = {}
+
+        def second(i, h, g):
+            if g == 0:
+                acc[(i, h)] = bank("a")
+            ncols = slice(h * HALF, (h + 1) * HALF)
+            nc.tensor.matmul_mx(
+                out=acc[(i, h)][:],
+                lhsT=pcod[:, g, i * 2 * P : (i + 1) * 2 * P].bitcast(FP4X4),
+                lhsT_scale=pscl[:, g, i * P : (i + 1) * P],
+                rhs=dcod[g][:, ncols].bitcast(FP8X4),
+                rhs_scale=dscl[g][:, ncols],
+                start=(g == 0),
+                stop=(g == G - 1),
+            )
+
+        def finish(i, h):
+            o = stage.tile([P, HALF], F32, name="o", tag="o")
+            nc.scalar.activation(out=o[:], in_=acc[(i, h)][:], func=SQUARE, scale=rgain[:, i : i + 1])
+            nc.sync.dma_start(out=out[i * P : (i + 1) * P, h * HALF : (h + 1) * HALF], in_=o[:])
+
+        def last_tile():
+            i = R // P - 1
+            for j in range(4):
+                part = bank("b")
+                ncols = slice(HALF + j * P, HALF + (j + 1) * P)
+                for g in range(G):
+                    nc.tensor.matmul_mx(
+                        out=part[:, 0:P],
+                        lhsT=pcod[:, g, i * 2 * P : (i + 1) * 2 * P].bitcast(FP4X4),
+                        lhsT_scale=pscl[:, g, i * P : (i + 1) * P],
+                        rhs=dcod[g][:, ncols].bitcast(FP8X4),
+                        rhs_scale=dscl[g][:, ncols],
+                        start=(g == 0),
+                        stop=(g == G - 1),
+                    )
+                o = stage.tile([P, P], F32, name="olast", tag="olast")
+                nc.scalar.activation(out=o[:], in_=part[:, 0:P], func=SQUARE, scale=rgain[:, i : i + 1])
+                nc.sync.dma_start(out=out[i * P : (i + 1) * P, ncols], in_=o[:])
+
+        def heat(n, width):
+            w = bank("b")
+            for j in range(n):
+                nc.tensor.matmul(out=w[:, 0:width], lhsT=ones[:], rhs=ones[:, 0:width], start=True, stop=True)
+
+        def spread_gain(j):
+            pg = bank("b")
+            nc.tensor.matmul(out=pg[:], lhsT=ones[:], rhs=gains[:, 0:HALF], start=True, stop=True)
+            return pg
+
+        def row_gains():
+            pr = bank("b")
+            nc.tensor.matmul(out=pr[:, 0 : R // P], lhsT=gains[:, HALF : HALF + P], rhs=idb[:, 0 : R // P], start=True, stop=True)
+            nc.scalar.copy(out=rgain[:], in_=pr[:, 0 : R // P])
+
+        q = []
+
+        def y(g, b):
+            first(g, b)
+            gain(g, b)
+            while q:
+                quant_d(*q.pop())
+            if b % 2 == 1:
+                q.append((g, b // 2))
+
+        def flush():
+            while q:
+                quant_d(*q.pop())
+
+        def partial(g, n=4):
+            for i in range(n):
+                second(i, 0, g)
+
+        def whole(i, h):
+            for g in range(G):
+                second(i, h, g)
+            finish(i, h)
+
+        heat(HEAT, P)
+        widen(0, 0, (0, 1), True)
+        widen(0, 0, (2, 3), False)
+        widen(1, 0, (0, 1), True)
+        widen(1, 0, (2, 3), False)
+        interleave(0, 0, True)
+        interleave(1, 0, True)
+        for t in range(4):
+            turn(0, t)
+        pg = spread_gain(0)
+        quant_steer(0, 0)
+        quant_echo(0, 0)
+        quant_steer(1, 0)
+        quant_echo(0, 1)
+        turn(1, 0)
+        turn(1, 1)
+        nc.scalar.copy(out=cgain[:], in_=pg[:])
+        turn(1, 2)
+        turn(1, 3)
+        for t in range(4):
+            sort_words(2, t)
+        quant_echo(1, 0)
+        y(0, 0)
+        y(0, 1)
+        quant_echo(1, 1)
+        y(0, 2)
+        y(0, 3)
+        for t in range(4):
+            turn(2, t)
+        sort_words(3, 0, True)
+        sort_words(3, 1, True)
+        sort_words(3, 2)
+        sort_words(3, 3)
+        y(1, 0)
+        y(1, 1)
+        quant_echo(2, 0)
+        y(1, 2)
+        quant_echo(2, 1)
+        y(1, 3)
+        for t in range(4):
+            turn(3, t)
+        row_gains()
+        widen(0, 1, range(4), False)
+        widen(1, 1, range(4), False)
+        flush()
+        quant_echo(3, 0)
+        quant_echo(3, 1)
+        for b in range(2):
+            y(2, b)
+        partial(0)
+        for b in range(2, 4):
+            y(2, b)
+        for b in range(2):
+            y(3, b)
+        partial(1)
+        for b in range(2, 4):
+            y(3, b)
+        partial(2)
+        flush()
+        interleave(0, 1, False)
+        interleave(1, 1, True)
+        quant_steer(0, 1)
+        quant_steer(1, 1)
+        partial(3)
+        for i in range(4):
+            finish(i, 0)
+        for g in range(G):
+            if g != 1:
+                whole(4 + max(0, g - 1), 0)
+            first_wide(g)
+            if g > 0:
+                quant_d(g - 1, 3)
+            gain_wide(g, 2)
+            gain_wide(g, 3)
+            quant_d(g, 2)
+        quant_d(G - 1, 3)
+        whole(7, 0)
+        for g in range(G):
+            for i in range(4):
+                second(i, 1, g)
+        for i in range(4):
+            finish(i, 1)
+        for i in range(4, 7):
+            whole(i, 1)
+        last_tile()

@@ -22,8 +22,7 @@ P = 128
 G = T // 512
 CP = C // 512
 HALF = 512
-SORTED = (2, 3)
-HEAT = 16
+QUART = 256
 
 
 def tile_sonar_ping_coherence_s13_kernel(tc, echo, steer_bytes, steer_scale, ref_words, ref_scales, col_gain, row_gain, out):
@@ -36,27 +35,34 @@ def tile_sonar_ping_coherence_s13_kernel(tc, echo, steer_bytes, steer_scale, ref
         psum = ctx.enter_context(tc.psum_pool(name="psum", bufs=4))
         ctx.enter_context(tc.manual_schedule())
 
-        eraw = [keep.tile([P, 4, C], BF16, name="eraw%d" % g, align_bytes=256) for g in range(G)]
+        pieces = {0: 1, 1: 1, 2: 2, 3: 2}
+        etile = {}
+        for g in range(G):
+            for t0 in range(0, 4, pieces[g]):
+                etile[(g, t0)] = keep.tile([P, pieces[g], C], BF16, name="eraw%d_%d" % (g, t0), align_bytes=256)
+
+        def eraw(g, t):
+            return etile[(g, t - t % pieces[g])][:, t % pieces[g], :]
+
         egrp = {}
+        esort = {}
         ecod = [keep.tile([P, 4 * CP * P], U32, name="ecod%d" % g, align_bytes=256) for g in range(G)]
         escl = [keep.tile([P, 4 * CP * P], U8, name="escl%d" % g, align_bytes=256) for g in range(G)]
-        esort = {g: keep.tile([P, 4, C // 2], F32, name="esort%d" % g, align_bytes=256) for g in SORTED}
-        sraw = keep.tile([P, CP, 4, N], U8, name="sraw", align_bytes=256)
+        sraw = {(c, h): keep.tile([P, 4, HALF], U8, name="sraw%d_%d" % (c, h), align_bytes=256) for c in range(CP) for h in range(2)}
         sscl = keep.tile([P, CP, 4], F32, name="sscl", align_bytes=256)
-        swide = [keep.tile([P, 4, HALF], BF16, name="swide%d" % j, align_bytes=256) for j in range(2 * CP)]
-        sgrp = [keep.tile([P, HALF, 4], BF16, name="sgrp%d" % j, align_bytes=256) for j in range(2 * CP)]
+        swide = {(c, q): keep.tile([P, 4, QUART], BF16, name="swide%d_%d" % (c, q), align_bytes=256) for c in range(CP) for q in range(4)}
+        sgrp = {(c, q): keep.tile([P, QUART, 4], BF16, name="sgrp%d_%d" % (c, q), align_bytes=256) for c in range(CP) for q in range(4)}
         scod = [keep.tile([P, N], U32, name="scod%d" % c, align_bytes=256) for c in range(CP)]
         sqsc = [keep.tile([P, N], U8, name="sqsc%d" % c, align_bytes=256) for c in range(CP)]
         dcod = [keep.tile([P, N], U32, name="dcod%d" % g, align_bytes=256) for g in range(G)]
         dscl = [keep.tile([P, N], U8, name="dscl%d" % g, align_bytes=256) for g in range(G)]
         pcod = keep.tile([P, G, 2 * R], U8, name="pcod", align_bytes=256)
         pscl = keep.tile([P, G, R], U8, name="pscl", align_bytes=256)
-        gains = keep.tile([P, HALF + P], BF16, name="gains", align_bytes=256)
-        ones = keep.tile([P, P], BF16, name="ones", align_bytes=256)
+        gains = keep.tile([P, N + P], BF16, name="gains", align_bytes=256)
+        ones = keep.tile([P, HALF], BF16, name="ones", align_bytes=256)
         idf = keep.tile([P, P], F32, name="idf", align_bytes=256)
         idb = keep.tile([P, P], BF16, name="idb", align_bytes=256)
-        cgain1 = keep.tile([P, HALF], BF16, name="cgain1", align_bytes=256)
-        cgain = keep.tile([P, HALF], F32, name="cgain", align_bytes=256)
+        cgain = keep.tile([P, N], BF16, name="cgain", align_bytes=256)
         rgain = keep.tile([P, R // P], F32, name="rgain", align_bytes=256)
 
         def bank(tag):
@@ -71,28 +77,27 @@ def tile_sonar_ping_coherence_s13_kernel(tc, echo, steer_bytes, steer_scale, ref
         echo_g = echo.rearrange("(g p t) k -> g p t k", p=P, t=4)
         steer_c = steer_bytes.rearrange("(c p t) n -> c p t n", p=P, t=4)
 
-        def load_echo(g, t0, t1):
-            nc.sync.dma_start(out=eraw[g][:, t0:t1, :], in_=echo_g[g][:, t0:t1, :])
+        def load_echo(g):
+            for t0 in range(0, 4, pieces[g]):
+                nc.sync.dma_start(out=etile[(g, t0)][:], in_=echo_g[g][:, t0 : t0 + pieces[g], :])
 
         def load_steer(c, h):
-            cols = slice(h * HALF, (h + 1) * HALF)
-            nc.sync.dma_start(out=sraw[:, c, :, cols], in_=steer_c[c][:, :, cols])
+            nc.sync.dma_start(out=sraw[(c, h)][:], in_=steer_c[c][:, :, h * HALF : (h + 1) * HALF])
+
+        def load_words(g):
+            nc.sync.dma_start(out=pcod[:, g, :].bitcast(I32), in_=ref_words[g].bitcast(I32))
 
         nc.scalar.dma_start(out=sscl[:], in_=steer_scale.rearrange("(c p t) o -> p c (t o)", p=P, t=4))
         load_steer(0, 0)
         load_steer(1, 0)
-        for t in range(4):
-            load_echo(0, t, t + 1)
-        nc.scalar.dma_start(out=gains[0:1, 0:HALF], in_=col_gain[0:HALF].unsqueeze(0))
-        nc.scalar.dma_start(out=gains[0 : R // P, HALF : HALF + P], in_=row_gain.rearrange("(c m) -> c m", m=P))
-        for t in range(4):
-            load_echo(1, t, t + 1)
-        for g in range(2, G):
-            load_echo(g, 0, 2)
-            load_echo(g, 2, 4)
-        def load_words(g):
-            nc.sync.dma_start(out=pcod[:, g, :].bitcast(I32), in_=ref_words[g].bitcast(I32))
-
+        load_echo(0)
+        nc.sync.dma_start(out=gains[0:1, 0:N], in_=col_gain.unsqueeze(0))
+        load_echo(1)
+        nc.sync.dma_start(out=gains[0 : R // P, N : N + P], in_=row_gain.rearrange("(c m) -> c m", m=P))
+        load_echo(2)
+        load_echo(3)
+        load_steer(0, 1)
+        load_steer(1, 1)
         load_words(0)
         for q4 in range(4):
             nc.sync.dma_start(
@@ -100,75 +105,85 @@ def tile_sonar_ping_coherence_s13_kernel(tc, echo, steer_bytes, steer_scale, ref
                 in_=ref_scales[:, 4 * q4 : 4 * q4 + 4, :].rearrange("g r n -> r g n").bitcast(I32),
             )
         load_words(1)
-        load_steer(0, 1)
-        load_steer(1, 1)
-        nc.sync.dma_start(out=cgain1[:], in_=col_gain[HALF:N].partition_broadcast(P))
         load_words(2)
         load_words(3)
 
-        def widen(c, h, ts, on_vector):
-            dst = swide[2 * c + h]
-            for t in ts:
-                src = sraw[:, c, t, h * HALF : (h + 1) * HALF].bitcast(FP8)
+        def widen(c, q, on_vector):
+            dst = swide[(c, q)]
+            n0 = (q % 2) * QUART
+            for t in range(4):
+                src = sraw[(c, q // 2)][:, t, n0 : n0 + QUART].bitcast(FP8)
                 if on_vector:
                     nc.vector.tensor_scalar(out=dst[:, t, :], in0=src, scalar1=sscl[:, c, t : t + 1], scalar2=None, op0=MULT)
                 else:
                     nc.scalar.activation(out=dst[:, t, :], in_=src, func=COPY, scale=sscl[:, c, t : t + 1])
 
-        def interleave(c, h, on_vector):
-            src = swide[2 * c + h][:].rearrange("p t (n i) -> p n t i", i=4)
-            dst = sgrp[2 * c + h][:].rearrange("p (n i) t -> p n t i", i=4)
+        def interleave(c, q, on_vector):
+            src = swide[(c, q)][:].rearrange("p t (n i) -> p n t i", i=4)
+            dst = sgrp[(c, q)][:].rearrange("p (n i) t -> p n t i", i=4)
             if on_vector:
                 nc.vector.tensor_copy(out=dst, in_=src)
             else:
                 nc.scalar.copy(out=dst, in_=src)
 
-        def quant_steer(c, h):
-            cols = slice(h * HALF, (h + 1) * HALF)
-            nc.vector.quantize_mx(out=scod[c][:, cols].bitcast(FP8X4), scales=sqsc[c][:, cols], in_=sgrp[2 * c + h][:].rearrange("p n t -> p (n t)"))
+        def quant_steer(c, q):
+            cols = slice(q * QUART, (q + 1) * QUART)
+            nc.vector.quantize_mx(out=scod[c][:, cols].bitcast(FP8X4), scales=sqsc[c][:, cols], in_=sgrp[(c, q)][:].rearrange("p n t -> p (n t)"))
 
-        def sort_words(g, t, on_vector=False):
-            if g in SORTED:
-                words = eraw[g][:, t, :].bitcast(F32)
-                copy = nc.vector.tensor_copy if on_vector else nc.scalar.copy
-                copy(out=esort[g][:, t, :].rearrange("p (c u m) -> p c u m", c=CP, u=2), in_=words.rearrange("p (c m u) -> p c u m", c=CP, u=2))
+        def sort_words(g, t, on_vector):
+            words = eraw(g, t).bitcast(F32)
+            esort[(g, t)] = ring.tile([P, C // 2], F32, name="esort", tag="esort", align_bytes=256)
+            copy = nc.vector.tensor_copy if on_vector else nc.scalar.copy
+            copy(out=esort[(g, t)][:].rearrange("p (c u m) -> p c u m", c=CP, u=2), in_=words.rearrange("p (c m u) -> p c u m", c=CP, u=2))
+
+        xbank = {}
 
         def turn(g, t):
             xt = bank("a")
-            words = eraw[g][:, t, :].bitcast(F32)
+            xbank[(g, t)] = xt
+            words = eraw(g, t).bitcast(F32)
             for c in range(CP):
                 for u in range(2):
                     j = 2 * c + u
-                    src = esort[g][:, t, j * P : (j + 1) * P] if g in SORTED else words[:, 256 * c + u : 256 * (c + 1) : 2]
+                    src = esort[(g, t)][:, j * P : (j + 1) * P] if (g, t) in esort else words[:, 256 * c + u : 256 * (c + 1) : 2]
                     nc.tensor.transpose(xt[:, j * P : (j + 1) * P], src, idf[:])
+
+        def empty(g, t):
             if t % 2 == 0:
                 egrp[2 * g + t // 2] = ring.tile([P, 2, C], BF16, name="egrp", tag="egrp", align_bytes=256)
             dst = egrp[2 * g + t // 2][:, t % 2, :].bitcast(F32)
-            nc.scalar.copy(out=dst.rearrange("p (c r u) -> p c r u", c=CP, u=2), in_=xt[:].rearrange("p (c u r) -> p c r u", c=CP, u=2))
+            nc.scalar.copy(out=dst.rearrange("p (c r u) -> p c r u", c=CP, u=2), in_=xbank[(g, t)][:].rearrange("p (c u r) -> p c r u", c=CP, u=2))
 
         def quant_echo(g, half):
             cols = slice(half * 512, (half + 1) * 512)
             nc.vector.quantize_mx(out=ecod[g][:, cols].bitcast(FP8X4), scales=escl[g][:, cols], in_=egrp[2 * g + half][:].rearrange("p t k -> p (t k)"))
 
+        def quant_echo_slot(g, t):
+            cols = slice(t * 256, (t + 1) * 256)
+            nc.vector.quantize_mx(out=ecod[g][:, cols].bitcast(FP8X4), scales=escl[g][:, cols], in_=egrp[2 * g + t // 2][:, t % 2, :])
+
         ybank = {}
         dgrp = {}
 
-        def first(g, b):
-            y = bank("b")
-            ybank[(g, b)] = y
+        def first_slot(g, b, t):
+            if t == 0:
+                ybank[(g, b)] = bank("b")
             ncols = slice(b * P, (b + 1) * P)
+            for c in range(CP):
+                ecols = slice((t * CP + c) * P, (t * CP + c + 1) * P)
+                nc.tensor.matmul_mx(
+                    out=ybank[(g, b)][:, t * P : (t + 1) * P],
+                    lhsT=ecod[g][:, ecols].bitcast(FP8X4),
+                    lhsT_scale=escl[g][:, ecols],
+                    rhs=scod[c][:, ncols].bitcast(FP8X4),
+                    rhs_scale=sqsc[c][:, ncols],
+                    start=(c == 0),
+                    stop=(c == CP - 1),
+                )
+
+        def first(g, b):
             for t in range(4):
-                for c in range(CP):
-                    ecols = slice((t * CP + c) * P, (t * CP + c + 1) * P)
-                    nc.tensor.matmul_mx(
-                        out=y[:, t * P : (t + 1) * P],
-                        lhsT=ecod[g][:, ecols].bitcast(FP8X4),
-                        lhsT_scale=escl[g][:, ecols],
-                        rhs=scod[c][:, ncols].bitcast(FP8X4),
-                        rhs_scale=sqsc[c][:, ncols],
-                        start=(c == 0),
-                        stop=(c == CP - 1),
-                    )
+                first_slot(g, b, t)
 
         def gain(g, b):
             if b % 2 == 0:
@@ -211,7 +226,7 @@ def tile_sonar_ping_coherence_s13_kernel(tc, echo, steer_bytes, steer_scale, ref
             nc.vector.tensor_tensor(
                 out=d[:].rearrange("p b (n i) t -> p (b n) t i", i=4),
                 in0=lifted[g][:, :, n0 : n0 + 256].rearrange("p t (n i) -> p n t i", i=4),
-                in1=cgain1[:, n0 : n0 + 256].rearrange("p (n i) -> p n i", i=4).unsqueeze(2).to_broadcast([P, 64, 4, 4]),
+                in1=cgain[:, HALF + n0 : HALF + n0 + 256].rearrange("p (n i) -> p n i", i=4).unsqueeze(2).to_broadcast([P, 64, 4, 4]),
                 op=MULT,
             )
 
@@ -255,124 +270,139 @@ def tile_sonar_ping_coherence_s13_kernel(tc, echo, steer_bytes, steer_scale, ref
                 nc.scalar.activation(out=o[:], in_=part[:, 0:P], func=SQUARE, scale=rgain[:, i : i + 1])
                 nc.sync.dma_start(out=out[i * P : (i + 1) * P, ncols], in_=o[:])
 
-        def heat(n, width):
+        def warm(n):
             w = bank("b")
             for j in range(n):
-                nc.tensor.matmul(out=w[:, 0:width], lhsT=ones[:], rhs=ones[:, 0:width], start=True, stop=True)
+                nc.tensor.matmul(out=w[:], lhsT=ones[:, 0:P], rhs=ones[:], start=True, stop=True)
 
-        def spread_gain(j):
-            pg = bank("b")
-            nc.tensor.matmul(out=pg[:], lhsT=ones[:], rhs=gains[:, 0:HALF], start=True, stop=True)
+        def spread_gain():
+            pg = psum.tile([P, N], BF16, name="bank_b", tag="b")
+            for h in range(2):
+                nc.tensor.matmul(out=pg[:, h * HALF : (h + 1) * HALF], lhsT=ones[:, 0:P], rhs=gains[:, h * HALF : (h + 1) * HALF], start=True, stop=True)
             return pg
 
         def row_gains():
             pr = bank("b")
-            nc.tensor.matmul(out=pr[:, 0 : R // P], lhsT=gains[:, HALF : HALF + P], rhs=idb[:, 0 : R // P], start=True, stop=True)
+            nc.tensor.matmul(out=pr[:, 0 : R // P], lhsT=gains[:, N : N + P], rhs=idb[:, 0 : R // P], start=True, stop=True)
             nc.scalar.copy(out=rgain[:], in_=pr[:, 0 : R // P])
 
-        q = []
-
-        def y(g, b):
-            first(g, b)
-            gain(g, b)
-            while q:
-                quant_d(*q.pop())
-            if b % 2 == 1:
-                q.append((g, b // 2))
-
-        def flush():
-            while q:
-                quant_d(*q.pop())
-
-        def partial(g, n=4):
-            for i in range(n):
-                second(i, 0, g)
+        def partial(h, g, bands):
+            for i in bands:
+                second(i, h, g)
 
         def whole(i, h):
             for g in range(G):
                 second(i, h, g)
             finish(i, h)
 
-        heat(HEAT, P)
-        widen(0, 0, (0, 1), True)
-        widen(0, 0, (2, 3), False)
-        widen(1, 0, (0, 1), True)
-        widen(1, 0, (2, 3), False)
+
+        warm(6)
+        widen(0, 0, True)
+        widen(1, 0, False)
+        widen(0, 1, True)
         interleave(0, 0, True)
         interleave(1, 0, True)
+        quant_steer(0, 0)
+        quant_steer(1, 0)
         for t in range(4):
             turn(0, t)
-        pg = spread_gain(0)
-        quant_steer(0, 0)
+            empty(0, t)
+        pg = spread_gain()
         quant_echo(0, 0)
-        quant_steer(1, 0)
-        quant_echo(0, 1)
-        turn(1, 0)
-        turn(1, 1)
-        nc.scalar.copy(out=cgain[:], in_=pg[:])
-        turn(1, 2)
-        turn(1, 3)
-        for t in range(4):
-            sort_words(2, t)
-        quant_echo(1, 0)
-        y(0, 0)
-        y(0, 1)
-        quant_echo(1, 1)
-        y(0, 2)
-        y(0, 3)
-        for t in range(4):
-            turn(2, t)
-        sort_words(3, 0, True)
-        sort_words(3, 1, True)
-        sort_words(3, 2)
-        sort_words(3, 3)
-        y(1, 0)
-        y(1, 1)
-        quant_echo(2, 0)
-        y(1, 2)
-        quant_echo(2, 1)
-        y(1, 3)
-        for t in range(4):
-            turn(3, t)
-        row_gains()
-        widen(0, 1, range(4), False)
-        widen(1, 1, range(4), False)
-        flush()
-        quant_echo(3, 0)
-        quant_echo(3, 1)
-        for b in range(2):
-            y(2, b)
-        partial(0)
-        for b in range(2, 4):
-            y(2, b)
-        for b in range(2):
-            y(3, b)
-        partial(1)
-        for b in range(2, 4):
-            y(3, b)
-        partial(2)
-        flush()
-        interleave(0, 1, False)
+        widen(1, 1, True)
+        quant_echo_slot(0, 2)
+        interleave(0, 1, True)
+        quant_echo_slot(0, 3)
         interleave(1, 1, True)
         quant_steer(0, 1)
         quant_steer(1, 1)
-        partial(3)
+        turn(1, 0)
+        empty(1, 0)
+        for t in range(4):
+            first_slot(0, 0, t)
+            first_slot(0, 1, t)
+        nc.scalar.copy(out=cgain[:], in_=pg[:])
+        for t in range(1, 4):
+            turn(1, t)
+            if t < 3:
+                sort_words(2, t - 1, False)
+            empty(1, t)
+        first(0, 2)
+        first(0, 3)
+
+        for t in range(4):
+            turn(2, t)
+            empty(2, t)
+        for t in range(4):
+            sort_words(3, t, False)
+        gain(0, 0)
+        quant_echo(1, 0)
+        gain(0, 1)
+        quant_echo(1, 1)
+        first(1, 0)
+        first(1, 1)
+        gain(0, 2)
+        quant_d(0, 0)
+        gain(0, 3)
+        first(1, 2)
+        first(1, 3)
+        for t in range(4):
+            turn(3, t)
+            empty(3, t)
+        row_gains()
+        for c in range(CP):
+            widen(c, 2, False)
+            widen(c, 3, False)
+        for g in range(1, G):
+            nxt = g + 1
+            gain(g, 0)
+            quant_d(g - 1, 1)
+            gain(g, 1)
+            if nxt < G:
+                quant_echo(nxt, 0)
+                quant_echo(nxt, 1)
+            if g == 2:
+                partial(0, 0, range(4))
+            if nxt < G:
+                first(nxt, 0)
+                first(nxt, 1)
+            gain(g, 2)
+            quant_d(g, 0)
+            gain(g, 3)
+            if nxt < G:
+                first(nxt, 2)
+                first(nxt, 3)
+        partial(0, 1, range(4))
+        partial(0, 2, range(4))
+        quant_d(3, 1)
+        interleave(0, 2, False)
+        interleave(0, 3, False)
+        interleave(1, 2, True)
+        interleave(1, 3, True)
+        quant_steer(0, 2)
+        quant_steer(1, 2)
+        quant_steer(0, 3)
+        quant_steer(1, 3)
+
+        partial(0, 3, range(4))
         for i in range(4):
             finish(i, 0)
-        for g in range(G):
-            if g != 1:
-                whole(4 + max(0, g - 1), 0)
+        whole(4, 0)
+        for b in range(4, 8):
+            first(0, b)
+            gain(0, b)
+            if b == 6:
+                quant_d(0, 2)
+        for g in range(1, G):
             first_wide(g)
-            if g > 0:
-                quant_d(g - 1, 3)
+            quant_d(g - 1, 3)
+            whole(4 + g, 0)
             gain_wide(g, 2)
             gain_wide(g, 3)
             quant_d(g, 2)
         quant_d(G - 1, 3)
-        whole(7, 0)
         for g in range(G):
-            for i in range(4):
-                second(i, 1, g)
+            partial(1, g, range(4))
         for i in range(4):
             finish(i, 1)
         for i in range(4, 7):

@@ -190,9 +190,9 @@ def tile_sonar_ping_coherence_s13_kernel(tc, echo, steer_bytes, steer_scale, ref
                 dgrp[(g, b // 2)] = ring.tile([P, 2, P, 4], BF16, name="dgrp", tag="dgrp", align_bytes=256)
             d = dgrp[(g, b // 2)]
             nc.vector.tensor_tensor(
-                out=d[:, b % 2, :, :],
-                in0=ybank[(g, b)][:].rearrange("p (t n) -> p n t", t=4),
-                in1=cgain[:, b * P : (b + 1) * P].unsqueeze(2).to_broadcast([P, P, 4]),
+                out=d[:, b % 2, :, :].rearrange("p (n i) t -> p n t i", i=4),
+                in0=ybank[(g, b)][:].rearrange("p (t n i) -> p n t i", t=4, i=4),
+                in1=cgain[:, b * P : (b + 1) * P].rearrange("p (n i) -> p n i", i=4).unsqueeze(2).to_broadcast([P, P // 4, 4, 4]),
                 op=MULT,
             )
 

@@ -50,26 +50,26 @@ def tile_sonar_ping_coherence_s13_kernel(tc, echo, steer_bytes, steer_scale, ref
         escl = [keep.tile([P, 4 * CP * P], U8, name="escl%d" % g, align_bytes=256) for g in range(G)]
         sraw = {(c, h): keep.tile([P, 4, HALF], U8, name="sraw%d_%d" % (c, h), align_bytes=256) for c in range(CP) for h in range(2)}
         sscl = keep.tile([P, CP, 4], F32, name="sscl", align_bytes=256)
-        swide = {(c, q): keep.tile([P, 4, QUART], BF16, name="swide%d_%d" % (c, q), align_bytes=256) for c in range(CP) for q in range(4)}
-        sgrp = {(c, q): keep.tile([P, QUART, 4], BF16, name="sgrp%d_%d" % (c, q), align_bytes=256) for c in range(CP) for q in range(4)}
+        swide = {(c, h): keep.tile([P, 4, HALF], BF16, name="swide%d_%d" % (c, h), align_bytes=256) for c in range(CP) for h in range(2)}
+        sgrp = [keep.tile([P, N, 4], BF16, name="sgrp%d" % c, align_bytes=256) for c in range(CP)]
         scod = [keep.tile([P, N], U32, name="scod%d" % c, align_bytes=256) for c in range(CP)]
         sqsc = [keep.tile([P, N], U8, name="sqsc%d" % c, align_bytes=256) for c in range(CP)]
         dcod = [keep.tile([P, N], U32, name="dcod%d" % g, align_bytes=256) for g in range(G)]
         dscl = [keep.tile([P, N], U8, name="dscl%d" % g, align_bytes=256) for g in range(G)]
         pcod = keep.tile([P, G, 2 * R], U8, name="pcod", align_bytes=256)
         pscl = keep.tile([P, G, R], U8, name="pscl", align_bytes=256)
-        gains = keep.tile([P, N + P], BF16, name="gains", align_bytes=256)
+        gains = keep.tile([P, HALF + P], BF16, name="gains", align_bytes=256)
         ones = keep.tile([P, HALF], BF16, name="ones", align_bytes=256)
         idf = keep.tile([P, P], F32, name="idf", align_bytes=256)
         idb = keep.tile([P, P], BF16, name="idb", align_bytes=256)
-        cgain = keep.tile([P, N], BF16, name="cgain", align_bytes=256)
+        cgain = [keep.tile([P, HALF], BF16, name="cgain%d" % h, align_bytes=256) for h in range(2)]
         rgain = keep.tile([P, R // P], F32, name="rgain", align_bytes=256)
 
         def bank(tag):
             return psum.tile([P, 512], F32, name="bank_" + tag, tag=tag)
 
-        nc.vector.memset(ones[:], 1.0)
         nc.vector.memset(gains[:], 0.0)
+        nc.vector.memset(ones[:], 1.0)
         make_identity(nc, idf[:])
         nc.vector.memset(pscl[:].rearrange("p g n -> p (g n)").bitcast(I32), 0)
         nc.gpsimd.tensor_copy(out=idb[:], in_=idf[:])
@@ -88,12 +88,12 @@ def tile_sonar_ping_coherence_s13_kernel(tc, echo, steer_bytes, steer_scale, ref
             nc.sync.dma_start(out=pcod[:, g, :].bitcast(I32), in_=ref_words[g].bitcast(I32))
 
         nc.scalar.dma_start(out=sscl[:], in_=steer_scale.rearrange("(c p t) o -> p c (t o)", p=P, t=4))
+        nc.scalar.dma_start(out=gains[0:1, 0:HALF], in_=col_gain[0:HALF].unsqueeze(0))
+        nc.scalar.dma_start(out=gains[0 : R // P, HALF : HALF + P], in_=row_gain.rearrange("(c m) -> c m", m=P))
         load_steer(0, 0)
         load_steer(1, 0)
         load_echo(0)
-        nc.sync.dma_start(out=gains[0:1, 0:N], in_=col_gain.unsqueeze(0))
         load_echo(1)
-        nc.sync.dma_start(out=gains[0 : R // P, N : N + P], in_=row_gain.rearrange("(c m) -> c m", m=P))
         load_echo(2)
         load_echo(3)
         load_steer(0, 1)
@@ -107,28 +107,30 @@ def tile_sonar_ping_coherence_s13_kernel(tc, echo, steer_bytes, steer_scale, ref
         load_words(1)
         load_words(2)
         load_words(3)
+        nc.sync.dma_start(out=cgain[1][:], in_=col_gain[HALF:N].partition_broadcast(P))
 
-        def widen(c, q, on_vector):
-            dst = swide[(c, q)]
-            n0 = (q % 2) * QUART
+        def widen(c, n0, n1, on_vector):
+            h = n0 // HALF
+            cols = slice(n0 - h * HALF, n1 - h * HALF)
+            dst = swide[(c, h)]
             for t in range(4):
-                src = sraw[(c, q // 2)][:, t, n0 : n0 + QUART].bitcast(FP8)
+                src = sraw[(c, h)][:, t, cols].bitcast(FP8)
                 if on_vector:
-                    nc.vector.tensor_scalar(out=dst[:, t, :], in0=src, scalar1=sscl[:, c, t : t + 1], scalar2=None, op0=MULT)
+                    nc.vector.tensor_scalar(out=dst[:, t, cols], in0=src, scalar1=sscl[:, c, t : t + 1], scalar2=None, op0=MULT)
                 else:
-                    nc.scalar.activation(out=dst[:, t, :], in_=src, func=COPY, scale=sscl[:, c, t : t + 1])
+                    nc.scalar.activation(out=dst[:, t, cols], in_=src, func=COPY, scale=sscl[:, c, t : t + 1])
 
-        def interleave(c, q, on_vector):
-            src = swide[(c, q)][:].rearrange("p t (n i) -> p n t i", i=4)
-            dst = sgrp[(c, q)][:].rearrange("p (n i) t -> p n t i", i=4)
+        def interleave(c, n0, n1, on_vector):
+            h = n0 // HALF
+            src = swide[(c, h)][:, :, n0 - h * HALF : n1 - h * HALF].rearrange("p t (n i) -> p n t i", i=4)
+            dst = sgrp[c][:, n0:n1, :].rearrange("p (n i) t -> p n t i", i=4)
             if on_vector:
                 nc.vector.tensor_copy(out=dst, in_=src)
             else:
                 nc.scalar.copy(out=dst, in_=src)
 
-        def quant_steer(c, q):
-            cols = slice(q * QUART, (q + 1) * QUART)
-            nc.vector.quantize_mx(out=scod[c][:, cols].bitcast(FP8X4), scales=sqsc[c][:, cols], in_=sgrp[(c, q)][:].rearrange("p n t -> p (n t)"))
+        def quant_steer(c, n0, n1):
+            nc.vector.quantize_mx(out=scod[c][:, n0:n1].bitcast(FP8X4), scales=sqsc[c][:, n0:n1], in_=sgrp[c][:, n0:n1, :].rearrange("p n t -> p (n t)"))
 
         def sort_words(g, t, on_vector):
             words = eraw(g, t).bitcast(F32)
@@ -149,18 +151,14 @@ def tile_sonar_ping_coherence_s13_kernel(tc, echo, steer_bytes, steer_scale, ref
                     nc.tensor.transpose(xt[:, j * P : (j + 1) * P], src, idf[:])
 
         def empty(g, t):
-            if t % 2 == 0:
-                egrp[2 * g + t // 2] = ring.tile([P, 2, C], BF16, name="egrp", tag="egrp", align_bytes=256)
-            dst = egrp[2 * g + t // 2][:, t % 2, :].bitcast(F32)
+            if t == 0:
+                egrp[g] = lift.tile([P, 4, C], BF16, name="egrp", tag="egrp", align_bytes=256)
+            dst = egrp[g][:, t, :].bitcast(F32)
             nc.scalar.copy(out=dst.rearrange("p (c r u) -> p c r u", c=CP, u=2), in_=xbank[(g, t)][:].rearrange("p (c u r) -> p c r u", c=CP, u=2))
 
-        def quant_echo(g, half):
-            cols = slice(half * 512, (half + 1) * 512)
-            nc.vector.quantize_mx(out=ecod[g][:, cols].bitcast(FP8X4), scales=escl[g][:, cols], in_=egrp[2 * g + half][:].rearrange("p t k -> p (t k)"))
-
-        def quant_echo_slot(g, t):
-            cols = slice(t * 256, (t + 1) * 256)
-            nc.vector.quantize_mx(out=ecod[g][:, cols].bitcast(FP8X4), scales=escl[g][:, cols], in_=egrp[2 * g + t // 2][:, t % 2, :])
+        def quant_echo(g, t0, t1):
+            cols = slice(t0 * CP * P, t1 * CP * P)
+            nc.vector.quantize_mx(out=ecod[g][:, cols].bitcast(FP8X4), scales=escl[g][:, cols], in_=egrp[g][:, t0:t1, :].rearrange("p t k -> p (t k)"))
 
         ybank = {}
         dgrp = {}
@@ -186,19 +184,20 @@ def tile_sonar_ping_coherence_s13_kernel(tc, echo, steer_bytes, steer_scale, ref
                 first_slot(g, b, t)
 
         def gain(g, b):
-            if b % 2 == 0:
-                dgrp[(g, b // 2)] = ring.tile([P, 2, P, 4], BF16, name="dgrp", tag="dgrp", align_bytes=256)
-            d = dgrp[(g, b // 2)]
+            if b % 4 == 0:
+                dgrp[(g, b // 4)] = ring.tile([P, HALF, 4], BF16, name="dgrp", tag="dgrp", align_bytes=256)
+            d = dgrp[(g, b // 4)][:, (b % 4) * P : (b % 4 + 1) * P, :]
             nc.vector.tensor_tensor(
-                out=d[:, b % 2, :, :].rearrange("p (n i) t -> p n t i", i=4),
+                out=d.rearrange("p (n i) t -> p n t i", i=4),
                 in0=ybank[(g, b)][:].rearrange("p (t n i) -> p n t i", t=4, i=4),
-                in1=cgain[:, b * P : (b + 1) * P].rearrange("p (n i) -> p n i", i=4).unsqueeze(2).to_broadcast([P, P // 4, 4, 4]),
+                in1=cgain[b // 4][:, (b % 4) * P : (b % 4 + 1) * P].rearrange("p (n i) -> p n i", i=4).unsqueeze(2).to_broadcast([P, P // 4, 4, 4]),
                 op=MULT,
             )
 
-        def quant_d(g, b2):
-            cols = slice(b2 * 2 * P, (b2 + 1) * 2 * P)
-            nc.vector.quantize_mx(out=dcod[g][:, cols].bitcast(FP8X4), scales=dscl[g][:, cols], in_=dgrp[(g, b2)][:].rearrange("p b n t -> p (b n t)"))
+        def quant_d(g, n0, n1):
+            h = n0 // HALF
+            src = dgrp[(g, h)][:, n0 - h * HALF : n1 - h * HALF, :]
+            nc.vector.quantize_mx(out=dcod[g][:, n0:n1].bitcast(FP8X4), scales=dscl[g][:, n0:n1], in_=src.rearrange("p n t -> p (n t)"))
 
         lifted = {}
 
@@ -219,14 +218,14 @@ def tile_sonar_ping_coherence_s13_kernel(tc, echo, steer_bytes, steer_scale, ref
                     )
                 nc.scalar.copy(out=lifted[g][:, t, :], in_=yb[:])
 
-        def gain_wide(g, b2):
-            d = ring.tile([P, 2, P, 4], BF16, name="dgrp", tag="dgrp", align_bytes=256)
-            dgrp[(g, b2)] = d
-            n0 = (b2 - 2) * 256
+        def gain_wide(g, q):
+            if q == 0:
+                dgrp[(g, 1)] = ring.tile([P, HALF, 4], BF16, name="dgrp", tag="dgrp", align_bytes=256)
+            cols = slice(q * QUART, (q + 1) * QUART)
             nc.vector.tensor_tensor(
-                out=d[:].rearrange("p b (n i) t -> p (b n) t i", i=4),
-                in0=lifted[g][:, :, n0 : n0 + 256].rearrange("p t (n i) -> p n t i", i=4),
-                in1=cgain[:, HALF + n0 : HALF + n0 + 256].rearrange("p (n i) -> p n i", i=4).unsqueeze(2).to_broadcast([P, 64, 4, 4]),
+                out=dgrp[(g, 1)][:, cols, :].rearrange("p (n i) t -> p n t i", i=4),
+                in0=lifted[g][:, :, cols].rearrange("p t (n i) -> p n t i", i=4),
+                in1=cgain[1][:, cols].rearrange("p (n i) -> p n i", i=4).unsqueeze(2).to_broadcast([P, QUART // 4, 4, 4]),
                 op=MULT,
             )
 
@@ -234,7 +233,7 @@ def tile_sonar_ping_coherence_s13_kernel(tc, echo, steer_bytes, steer_scale, ref
 
         def second(i, h, g):
             if g == 0:
-                acc[(i, h)] = bank("a")
+                acc[(i, h)] = bank("b" if (h == 0 and i == 4) else "a")
             ncols = slice(h * HALF, (h + 1) * HALF)
             nc.tensor.matmul_mx(
                 out=acc[(i, h)][:],
@@ -270,21 +269,21 @@ def tile_sonar_ping_coherence_s13_kernel(tc, echo, steer_bytes, steer_scale, ref
                 nc.scalar.activation(out=o[:], in_=part[:, 0:P], func=SQUARE, scale=rgain[:, i : i + 1])
                 nc.sync.dma_start(out=out[i * P : (i + 1) * P, ncols], in_=o[:])
 
+        scratch = bank("b")
+
         def warm(n):
-            w = bank("b")
             for j in range(n):
-                nc.tensor.matmul(out=w[:], lhsT=ones[:, 0:P], rhs=ones[:], start=True, stop=True)
+                nc.tensor.matmul(out=scratch[:], lhsT=ones[:, 0:P], rhs=ones[:], start=True, stop=True)
 
         def spread_gain():
-            pg = psum.tile([P, N], BF16, name="bank_b", tag="b")
-            for h in range(2):
-                nc.tensor.matmul(out=pg[:, h * HALF : (h + 1) * HALF], lhsT=ones[:, 0:P], rhs=gains[:, h * HALF : (h + 1) * HALF], start=True, stop=True)
+            pg = psum.tile([P, HALF], BF16, name="bank_b", tag="b")
+            nc.tensor.matmul(out=pg[:], lhsT=ones[:, 0:P], rhs=gains[:, 0:HALF], start=True, stop=True)
             return pg
 
         def row_gains():
             pr = bank("b")
-            nc.tensor.matmul(out=pr[:, 0 : R // P], lhsT=gains[:, N : N + P], rhs=idb[:, 0 : R // P], start=True, stop=True)
-            nc.scalar.copy(out=rgain[:], in_=pr[:, 0 : R // P])
+            nc.tensor.matmul(out=pr[:, 0 : R // P], lhsT=gains[:, HALF : HALF + P], rhs=idb[:, 0 : R // P], start=True, stop=True)
+            return pr
 
         def partial(h, g, bands):
             for i in bands:
@@ -296,111 +295,107 @@ def tile_sonar_ping_coherence_s13_kernel(tc, echo, steer_bytes, steer_scale, ref
             finish(i, h)
 
 
-        warm(6)
-        widen(0, 0, True)
-        widen(1, 0, False)
-        widen(0, 1, True)
-        interleave(0, 0, True)
-        interleave(1, 0, True)
-        quant_steer(0, 0)
-        quant_steer(1, 0)
+        warm(5)
+        pg = spread_gain()
+        pr = row_gains()
+        widen(0, 0, QUART, True)
+        widen(0, QUART, HALF, True)
+        widen(1, 0, HALF, False)
         for t in range(4):
             turn(0, t)
             empty(0, t)
-        pg = spread_gain()
-        quant_echo(0, 0)
-        widen(1, 1, True)
-        quant_echo_slot(0, 2)
-        interleave(0, 1, True)
-        quant_echo_slot(0, 3)
-        interleave(1, 1, True)
-        quant_steer(0, 1)
-        quant_steer(1, 1)
-        turn(1, 0)
-        empty(1, 0)
+        interleave(0, 0, QUART, True)
+        interleave(0, QUART, HALF, True)
+        quant_steer(0, 0, QUART)
+        interleave(1, 0, QUART, True)
+        quant_steer(0, QUART, HALF)
+        quant_steer(1, 0, QUART)
+        quant_echo(0, 0, 2)
+        interleave(1, QUART, HALF, True)
+        quant_echo(0, 2, 4)
+        quant_steer(1, QUART, HALF)
         for t in range(4):
-            first_slot(0, 0, t)
-            first_slot(0, 1, t)
-        nc.scalar.copy(out=cgain[:], in_=pg[:])
-        for t in range(1, 4):
             turn(1, t)
-            if t < 3:
-                sort_words(2, t - 1, False)
             empty(1, t)
-        first(0, 2)
-        first(0, 3)
+            if t == 9:
+                warm(2)
+            if t == 1:
+                nc.scalar.copy(out=cgain[0][:], in_=pg[:])
+                nc.scalar.copy(out=rgain[:], in_=pr[:, 0 : R // P])
+        for b in range(4):
+            first(0, b)
 
+        quant_echo(1, 0, 2)
+        for t in range(4):
+            sort_words(2, t, t < 2)
         for t in range(4):
             turn(2, t)
             empty(2, t)
-        for t in range(4):
-            sort_words(3, t, False)
         gain(0, 0)
-        quant_echo(1, 0)
+        quant_echo(1, 2, 4)
         gain(0, 1)
-        quant_echo(1, 1)
         first(1, 0)
         first(1, 1)
         gain(0, 2)
-        quant_d(0, 0)
         gain(0, 3)
+        sort_words(3, 0, True)
         first(1, 2)
         first(1, 3)
+        for t in range(1, 4):
+            sort_words(3, t, False)
         for t in range(4):
             turn(3, t)
             empty(3, t)
-        row_gains()
         for c in range(CP):
-            widen(c, 2, False)
-            widen(c, 3, False)
+            widen(c, HALF, N, False)
         for g in range(1, G):
             nxt = g + 1
+            if g == 1:
+                quant_d(0, 0, HALF)
             gain(g, 0)
-            quant_d(g - 1, 1)
             gain(g, 1)
             if nxt < G:
-                quant_echo(nxt, 0)
-                quant_echo(nxt, 1)
+                quant_echo(nxt, 0, 4)
+            if g > 1:
+                quant_d(g - 1, 0, HALF)
             if g == 2:
                 partial(0, 0, range(4))
             if nxt < G:
                 first(nxt, 0)
                 first(nxt, 1)
             gain(g, 2)
-            quant_d(g, 0)
+            if g == 3:
+                quant_d(3, 0, QUART)
             gain(g, 3)
             if nxt < G:
                 first(nxt, 2)
                 first(nxt, 3)
         partial(0, 1, range(4))
         partial(0, 2, range(4))
-        quant_d(3, 1)
-        interleave(0, 2, False)
-        interleave(0, 3, False)
-        interleave(1, 2, True)
-        interleave(1, 3, True)
-        quant_steer(0, 2)
-        quant_steer(1, 2)
-        quant_steer(0, 3)
-        quant_steer(1, 3)
+        for g in range(G - 1):
+            partial(0, g, (4,))
+        quant_d(3, QUART, HALF)
+        interleave(0, HALF, N, False)
+        interleave(1, HALF, HALF + QUART, False)
+        quant_steer(0, HALF, N)
+        interleave(1, HALF + QUART, N, True)
+        quant_steer(1, HALF, HALF + QUART)
+        quant_steer(1, HALF + QUART, N)
 
-        partial(0, 3, range(4))
-        for i in range(4):
+        partial(0, 3, (0, 4, 1, 2, 3))
+        for i in (0, 4, 1, 2, 3):
             finish(i, 0)
-        whole(4, 0)
         for b in range(4, 8):
             first(0, b)
             gain(0, b)
-            if b == 6:
-                quant_d(0, 2)
+        quant_d(0, HALF, N)
         for g in range(1, G):
             first_wide(g)
-            quant_d(g - 1, 3)
             whole(4 + g, 0)
-            gain_wide(g, 2)
-            gain_wide(g, 3)
-            quant_d(g, 2)
-        quant_d(G - 1, 3)
+            gain_wide(g, 0)
+            gain_wide(g, 1)
+            quant_d(g, HALF, HALF + QUART)
+            quant_d(g, HALF + QUART, N)
         for g in range(G):
             partial(1, g, range(4))
         for i in range(4):

@@ -68,8 +68,8 @@ def tile_sonar_ping_coherence_s13_kernel(tc, echo, steer_bytes, steer_scale, ref
         def bank(tag):
             return psum.tile([P, 512], F32, name="bank_" + tag, tag=tag)
 
-        nc.vector.memset(gains[:], 0.0)
         nc.vector.memset(ones[:], 1.0)
+        nc.vector.memset(gains[:], 0.0)
         make_identity(nc, idf[:])
         nc.vector.memset(pscl[:].rearrange("p g n -> p (g n)").bitcast(I32), 0)
         nc.gpsimd.tensor_copy(out=idb[:], in_=idf[:])
@@ -88,14 +88,14 @@ def tile_sonar_ping_coherence_s13_kernel(tc, echo, steer_bytes, steer_scale, ref
             nc.sync.dma_start(out=pcod[:, g, :].bitcast(I32), in_=ref_words[g].bitcast(I32))
 
         nc.scalar.dma_start(out=sscl[:], in_=steer_scale.rearrange("(c p t) o -> p c (t o)", p=P, t=4))
-        nc.scalar.dma_start(out=gains[0:1, 0:HALF], in_=col_gain[0:HALF].unsqueeze(0))
-        nc.scalar.dma_start(out=gains[0 : R // P, HALF : HALF + P], in_=row_gain.rearrange("(c m) -> c m", m=P))
         load_steer(0, 0)
         load_steer(1, 0)
         load_echo(0)
+        nc.sync.dma_start(out=gains[0:1, 0:HALF], in_=col_gain[0:HALF].unsqueeze(0))
         load_echo(1)
         load_echo(2)
         load_echo(3)
+        nc.sync.dma_start(out=gains[0 : R // P, HALF : HALF + P], in_=row_gain.rearrange("(c m) -> c m", m=P))
         load_steer(0, 1)
         load_steer(1, 1)
         load_words(0)
@@ -296,8 +296,6 @@ def tile_sonar_ping_coherence_s13_kernel(tc, echo, steer_bytes, steer_scale, ref
 
 
         warm(5)
-        pg = spread_gain()
-        pr = row_gains()
         widen(0, 0, QUART, True)
         widen(0, QUART, HALF, True)
         widen(1, 0, HALF, False)
@@ -317,11 +315,8 @@ def tile_sonar_ping_coherence_s13_kernel(tc, echo, steer_bytes, steer_scale, ref
         for t in range(4):
             turn(1, t)
             empty(1, t)
-            if t == 9:
-                warm(2)
-            if t == 1:
-                nc.scalar.copy(out=cgain[0][:], in_=pg[:])
-                nc.scalar.copy(out=rgain[:], in_=pr[:, 0 : R // P])
+        pg = spread_gain()
+        nc.scalar.copy(out=cgain[0][:], in_=pg[:])
         for b in range(4):
             first(0, b)
 
@@ -346,6 +341,8 @@ def tile_sonar_ping_coherence_s13_kernel(tc, echo, steer_bytes, steer_scale, ref
         for t in range(4):
             turn(3, t)
             empty(3, t)
+        pr = row_gains()
+        nc.scalar.copy(out=rgain[:], in_=pr[:, 0 : R // P])
         for c in range(CP):
             widen(c, HALF, N, False)
         for g in range(1, G):

@@ -63,13 +63,17 @@ def tile_sonar_ping_coherence_s13_kernel(tc, echo, steer_bytes, steer_scale, ref
         idf = keep.tile([P, P], F32, name="idf", align_bytes=256)
         idb = keep.tile([P, P], BF16, name="idb", align_bytes=256)
         cgain = [keep.tile([P, HALF], BF16, name="cgain%d" % h, align_bytes=256) for h in range(2)]
+        table_warm = keep.tile([P, 1], F32, name="table_warm", align_bytes=256)
         rgain = keep.tile([P, R // P], F32, name="rgain", align_bytes=256)
 
         def bank(tag):
             return psum.tile([P, 512], F32, name="bank_" + tag, tag=tag)
 
+        nc.scalar.dma_start(out=sscl[:], in_=steer_scale.rearrange("(c p t) o -> p c (t o)", p=P, t=4))
+
         nc.vector.memset(ones[:], 1.0)
         nc.vector.memset(gains[:], 0.0)
+        nc.scalar.activation(out=table_warm[:], in_=ones[:, 0:1], func=SQUARE)
         make_identity(nc, idf[:])
         nc.vector.memset(pscl[:].rearrange("p g n -> p (g n)").bitcast(I32), 0)
         nc.gpsimd.tensor_copy(out=idb[:], in_=idf[:])
@@ -87,7 +91,6 @@ def tile_sonar_ping_coherence_s13_kernel(tc, echo, steer_bytes, steer_scale, ref
         def load_words(g):
             nc.sync.dma_start(out=pcod[:, g, :].bitcast(I32), in_=ref_words[g].bitcast(I32))
 
-        nc.scalar.dma_start(out=sscl[:], in_=steer_scale.rearrange("(c p t) o -> p c (t o)", p=P, t=4))
         load_steer(0, 0)
         load_steer(1, 0)
         load_echo(0)
@@ -134,14 +137,14 @@ def tile_sonar_ping_coherence_s13_kernel(tc, echo, steer_bytes, steer_scale, ref
 
         def sort_words(g, t, on_vector):
             words = eraw(g, t).bitcast(F32)
-            esort[(g, t)] = ring.tile([P, C // 2], F32, name="esort", tag="esort", align_bytes=256)
+            esort[(g, t)] = keep.tile([P, C // 2], F32, name="esort%d_%d" % (g, t), align_bytes=256)
             copy = nc.vector.tensor_copy if on_vector else nc.scalar.copy
             copy(out=esort[(g, t)][:].rearrange("p (c u m) -> p c u m", c=CP, u=2), in_=words.rearrange("p (c m u) -> p c u m", c=CP, u=2))
 
         xbank = {}
 
         def turn(g, t):
-            xt = bank("a")
+            xt = bank("b" if g == 0 else "a")
             xbank[(g, t)] = xt
             words = eraw(g, t).bitcast(F32)
             for c in range(CP):
@@ -273,7 +276,7 @@ def tile_sonar_ping_coherence_s13_kernel(tc, echo, steer_bytes, steer_scale, ref
 
         def warm(n):
             for j in range(n):
-                nc.tensor.matmul(out=scratch[:], lhsT=ones[:, 0:P], rhs=ones[:], start=True, stop=True)
+                nc.tensor.matmul(out=scratch[:], lhsT=idb[:], rhs=ones[:], start=True, stop=True)
 
         def spread_gain():
             pg = psum.tile([P, HALF], BF16, name="bank_b", tag="b")
@@ -295,37 +298,45 @@ def tile_sonar_ping_coherence_s13_kernel(tc, echo, steer_bytes, steer_scale, ref
             finish(i, h)
 
 
-        warm(5)
+        warm(4)
         widen(0, 0, QUART, True)
+        widen(1, 0, QUART, False)
         widen(0, QUART, HALF, True)
-        widen(1, 0, HALF, False)
         for t in range(4):
             turn(0, t)
             empty(0, t)
+            if t in ():
+                warm(1)
         interleave(0, 0, QUART, True)
-        interleave(0, QUART, HALF, True)
-        quant_steer(0, 0, QUART)
         interleave(1, 0, QUART, True)
-        quant_steer(0, QUART, HALF)
+        quant_steer(0, 0, QUART)
         quant_steer(1, 0, QUART)
+        widen(1, QUART, HALF, True)
         quant_echo(0, 0, 2)
-        interleave(1, QUART, HALF, True)
+        interleave(0, QUART, HALF, True)
         quant_echo(0, 2, 4)
+        interleave(1, QUART, HALF, True)
+        quant_steer(0, QUART, HALF)
         quant_steer(1, QUART, HALF)
-        for t in range(4):
+        for t in range(0, 4):
             turn(1, t)
             empty(1, t)
         pg = spread_gain()
         nc.scalar.copy(out=cgain[0][:], in_=pg[:])
-        for b in range(4):
-            first(0, b)
+        first(0, 0)
+        first(0, 1)
+        first(0, 2)
+        first(0, 3)
 
         quant_echo(1, 0, 2)
         for t in range(4):
             sort_words(2, t, t < 2)
+        for t in range(1, 3):
+            sort_words(3, t, False)
         for t in range(4):
             turn(2, t)
             empty(2, t)
+        sort_words(3, 3, False)
         gain(0, 0)
         quant_echo(1, 2, 4)
         gain(0, 1)
@@ -336,8 +347,6 @@ def tile_sonar_ping_coherence_s13_kernel(tc, echo, steer_bytes, steer_scale, ref
         sort_words(3, 0, True)
         first(1, 2)
         first(1, 3)
-        for t in range(1, 4):
-            sort_words(3, t, False)
         for t in range(4):
             turn(3, t)
             empty(3, t)
@@ -372,12 +381,11 @@ def tile_sonar_ping_coherence_s13_kernel(tc, echo, steer_bytes, steer_scale, ref
         for g in range(G - 1):
             partial(0, g, (4,))
         quant_d(3, QUART, HALF)
-        interleave(0, HALF, N, False)
-        interleave(1, HALF, HALF + QUART, False)
-        quant_steer(0, HALF, N)
-        interleave(1, HALF + QUART, N, True)
-        quant_steer(1, HALF, HALF + QUART)
-        quant_steer(1, HALF + QUART, N)
+        for n0 in (HALF, HALF + QUART):
+            interleave(0, n0, n0 + QUART, False)
+            interleave(1, n0, n0 + QUART, True)
+            quant_steer(0, n0, n0 + QUART)
+            quant_steer(1, n0, n0 + QUART)
 
         partial(0, 3, (0, 4, 1, 2, 3))
         for i in (0, 4, 1, 2, 3):

@@ -30,7 +30,7 @@ def tile_sonar_ping_coherence_s13_kernel(tc, echo, steer_bytes, steer_scale, ref
     with ExitStack() as ctx:
         keep = ctx.enter_context(tc.tile_pool(name="keep", bufs=1))
         ring = ctx.enter_context(tc.tile_pool(name="ring", bufs=4))
-        stage = ctx.enter_context(tc.tile_pool(name="stage", bufs=8))
+        stage = ctx.enter_context(tc.tile_pool(name="stage", bufs=6))
         lift = ctx.enter_context(tc.tile_pool(name="lift", bufs=2))
         psum = ctx.enter_context(tc.psum_pool(name="psum", bufs=4))
         ctx.enter_context(tc.manual_schedule())
@@ -95,10 +95,10 @@ def tile_sonar_ping_coherence_s13_kernel(tc, echo, steer_bytes, steer_scale, ref
         load_steer(1, 0)
         load_echo(0)
         nc.sync.dma_start(out=gains[0:1, 0:HALF], in_=col_gain[0:HALF].unsqueeze(0))
+        nc.sync.dma_start(out=gains[0 : R // P, HALF : HALF + P], in_=row_gain.rearrange("(c m) -> c m", m=P))
         load_echo(1)
         load_echo(2)
         load_echo(3)
-        nc.sync.dma_start(out=gains[0 : R // P, HALF : HALF + P], in_=row_gain.rearrange("(c m) -> c m", m=P))
         load_steer(0, 1)
         load_steer(1, 1)
         load_words(0)
@@ -236,7 +236,7 @@ def tile_sonar_ping_coherence_s13_kernel(tc, echo, steer_bytes, steer_scale, ref
 
         def second(i, h, g):
             if g == 0:
-                acc[(i, h)] = bank("b" if (h == 0 and i == 4) else "a")
+                acc[(i, h)] = bank("b" if (h == 0 and i in (4, 5)) else "a")
             ncols = slice(h * HALF, (h + 1) * HALF)
             nc.tensor.matmul_mx(
                 out=acc[(i, h)][:],
@@ -272,20 +272,20 @@ def tile_sonar_ping_coherence_s13_kernel(tc, echo, steer_bytes, steer_scale, ref
                 nc.scalar.activation(out=o[:], in_=part[:, 0:P], func=SQUARE, scale=rgain[:, i : i + 1])
                 nc.sync.dma_start(out=out[i * P : (i + 1) * P, ncols], in_=o[:])
 
-        scratch = bank("b")
+        scratch = bank("a")
 
         def warm(n):
             for j in range(n):
                 nc.tensor.matmul(out=scratch[:], lhsT=idb[:], rhs=ones[:], start=True, stop=True)
 
         def spread_gain():
-            pg = psum.tile([P, HALF], BF16, name="bank_b", tag="b")
-            nc.tensor.matmul(out=pg[:], lhsT=ones[:, 0:P], rhs=gains[:, 0:HALF], start=True, stop=True)
+            pg = scratch[:, 0 : HALF // 2].bitcast(BF16)
+            nc.tensor.matmul(out=pg, lhsT=ones[:, 0:P], rhs=gains[:, 0:HALF], start=True, stop=True)
             return pg
 
         def row_gains():
-            pr = bank("b")
-            nc.tensor.matmul(out=pr[:, 0 : R // P], lhsT=gains[:, HALF : HALF + P], rhs=idb[:, 0 : R // P], start=True, stop=True)
+            pr = scratch[:, HALF // 2 : HALF // 2 + R // P]
+            nc.tensor.matmul(out=pr, lhsT=gains[:, HALF : HALF + P], rhs=idb[:, 0 : R // P], start=True, stop=True)
             return pr
 
         def partial(h, g, bands):
@@ -305,44 +305,49 @@ def tile_sonar_ping_coherence_s13_kernel(tc, echo, steer_bytes, steer_scale, ref
         for t in range(4):
             turn(0, t)
             empty(0, t)
-            if t in ():
-                warm(1)
+        turn(1, 0)
         interleave(0, 0, QUART, True)
         interleave(1, 0, QUART, True)
         quant_steer(0, 0, QUART)
         quant_steer(1, 0, QUART)
-        widen(1, QUART, HALF, True)
         quant_echo(0, 0, 2)
-        interleave(0, QUART, HALF, True)
+        widen(1, QUART, HALF, True)
         quant_echo(0, 2, 4)
+        interleave(0, QUART, HALF, True)
         interleave(1, QUART, HALF, True)
         quant_steer(0, QUART, HALF)
         quant_steer(1, QUART, HALF)
-        for t in range(0, 4):
-            turn(1, t)
-            empty(1, t)
         pg = spread_gain()
-        nc.scalar.copy(out=cgain[0][:], in_=pg[:])
-        first(0, 0)
-        first(0, 1)
+        pr = row_gains()
+        nc.scalar.copy(out=cgain[0][:], in_=pg)
+        nc.scalar.copy(out=rgain[:], in_=pr)
+        for t in range(1, 4):
+            sort_words(1, t, False)
+        for t in range(4):
+            first_slot(0, 0, t)
+            first_slot(0, 1, t)
+        for t in range(4):
+            if t > 0:
+                turn(1, t)
+            empty(1, t)
         first(0, 2)
         first(0, 3)
 
+        gain(0, 0)
+        for t in range(2):
+            sort_words(2, t, True)
+        gain(0, 1)
         quant_echo(1, 0, 2)
-        for t in range(4):
-            sort_words(2, t, t < 2)
         for t in range(1, 3):
             sort_words(3, t, False)
         for t in range(4):
             turn(2, t)
             empty(2, t)
         sort_words(3, 3, False)
-        gain(0, 0)
+        gain(0, 2)
         quant_echo(1, 2, 4)
-        gain(0, 1)
         first(1, 0)
         first(1, 1)
-        gain(0, 2)
         gain(0, 3)
         sort_words(3, 0, True)
         first(1, 2)
@@ -350,8 +355,6 @@ def tile_sonar_ping_coherence_s13_kernel(tc, echo, steer_bytes, steer_scale, ref
         for t in range(4):
             turn(3, t)
             empty(3, t)
-        pr = row_gains()
-        nc.scalar.copy(out=rgain[:], in_=pr[:, 0 : R // P])
         for c in range(CP):
             widen(c, HALF, N, False)
         for g in range(1, G):
@@ -379,7 +382,7 @@ def tile_sonar_ping_coherence_s13_kernel(tc, echo, steer_bytes, steer_scale, ref
         partial(0, 1, range(4))
         partial(0, 2, range(4))
         for g in range(G - 1):
-            partial(0, g, (4,))
+            partial(0, g, (4, 5))
         quant_d(3, QUART, HALF)
         for n0 in (HALF, HALF + QUART):
             interleave(0, n0, n0 + QUART, False)
@@ -387,8 +390,8 @@ def tile_sonar_ping_coherence_s13_kernel(tc, echo, steer_bytes, steer_scale, ref
             quant_steer(0, n0, n0 + QUART)
             quant_steer(1, n0, n0 + QUART)
 
-        partial(0, 3, (0, 4, 1, 2, 3))
-        for i in (0, 4, 1, 2, 3):
+        partial(0, 3, (0, 4, 5, 1, 2, 3))
+        for i in (4, 5, 0, 1, 2, 3):
             finish(i, 0)
         for b in range(4, 8):
             first(0, b)
@@ -396,7 +399,8 @@ def tile_sonar_ping_coherence_s13_kernel(tc, echo, steer_bytes, steer_scale, ref
         quant_d(0, HALF, N)
         for g in range(1, G):
             first_wide(g)
-            whole(4 + g, 0)
+            if g > 1:
+                whole(4 + g, 0)
             gain_wide(g, 0)
             gain_wide(g, 1)
             quant_d(g, HALF, HALF + QUART)

@@ -23,6 +23,8 @@ G = T // 512
 CP = C // 512
 HALF = 512
 QUART = 256
+BANDS = R // P
+TWO_ONES = 0x3F803F80
 
 
 def tile_sonar_ping_coherence_s13_kernel(tc, echo, steer_bytes, steer_scale, ref_words, ref_scales, col_gain, row_gain, out):
@@ -30,385 +32,431 @@ def tile_sonar_ping_coherence_s13_kernel(tc, echo, steer_bytes, steer_scale, ref
     with ExitStack() as ctx:
         keep = ctx.enter_context(tc.tile_pool(name="keep", bufs=1))
         ring = ctx.enter_context(tc.tile_pool(name="ring", bufs=4))
-        stage = ctx.enter_context(tc.tile_pool(name="stage", bufs=6))
-        lift = ctx.enter_context(tc.tile_pool(name="lift", bufs=2))
-        psum = ctx.enter_context(tc.psum_pool(name="psum", bufs=4))
+        stage = ctx.enter_context(tc.tile_pool(name="stage", bufs=8))
+        psum = ctx.enter_context(tc.psum_pool(name="psum", bufs=1))
         ctx.enter_context(tc.manual_schedule())
 
-        pieces = {0: 1, 1: 1, 2: 2, 3: 2}
-        etile = {}
-        for g in range(G):
-            for t0 in range(0, 4, pieces[g]):
-                etile[(g, t0)] = keep.tile([P, pieces[g], C], BF16, name="eraw%d_%d" % (g, t0), align_bytes=256)
+        def kept(shape, dtype, name):
+            return keep.tile(shape, dtype, name=name, align_bytes=256)
 
-        def eraw(g, t):
-            return etile[(g, t - t % pieces[g])][:, t % pieces[g], :]
+        def bank(k):
+            return psum.tile([P, 512], F32, name="bank%d" % k, tag="bank%d" % k)
 
-        egrp = {}
-        esort = {}
-        ecod = [keep.tile([P, 4 * CP * P], U32, name="ecod%d" % g, align_bytes=256) for g in range(G)]
-        escl = [keep.tile([P, 4 * CP * P], U8, name="escl%d" % g, align_bytes=256) for g in range(G)]
-        sraw = {(c, h): keep.tile([P, 4, HALF], U8, name="sraw%d_%d" % (c, h), align_bytes=256) for c in range(CP) for h in range(2)}
-        sscl = keep.tile([P, CP, 4], F32, name="sscl", align_bytes=256)
-        swide = {(c, h): keep.tile([P, 4, HALF], BF16, name="swide%d_%d" % (c, h), align_bytes=256) for c in range(CP) for h in range(2)}
-        sgrp = [keep.tile([P, N, 4], BF16, name="sgrp%d" % c, align_bytes=256) for c in range(CP)]
-        scod = [keep.tile([P, N], U32, name="scod%d" % c, align_bytes=256) for c in range(CP)]
-        sqsc = [keep.tile([P, N], U8, name="sqsc%d" % c, align_bytes=256) for c in range(CP)]
-        dcod = [keep.tile([P, N], U32, name="dcod%d" % g, align_bytes=256) for g in range(G)]
-        dscl = [keep.tile([P, N], U8, name="dscl%d" % g, align_bytes=256) for g in range(G)]
-        pcod = keep.tile([P, G, 2 * R], U8, name="pcod", align_bytes=256)
-        pscl = keep.tile([P, G, R], U8, name="pscl", align_bytes=256)
-        gains = keep.tile([P, HALF + P], BF16, name="gains", align_bytes=256)
-        ones = keep.tile([P, HALF], BF16, name="ones", align_bytes=256)
-        idf = keep.tile([P, P], F32, name="idf", align_bytes=256)
-        idb = keep.tile([P, P], BF16, name="idb", align_bytes=256)
-        cgain = [keep.tile([P, HALF], BF16, name="cgain%d" % h, align_bytes=256) for h in range(2)]
-        table_warm = keep.tile([P, 1], F32, name="table_warm", align_bytes=256)
-        rgain = keep.tile([P, R // P], F32, name="rgain", align_bytes=256)
-
-        def bank(tag):
-            return psum.tile([P, 512], F32, name="bank_" + tag, tag=tag)
-
-        nc.scalar.dma_start(out=sscl[:], in_=steer_scale.rearrange("(c p t) o -> p c (t o)", p=P, t=4))
-
-        nc.vector.memset(ones[:], 1.0)
-        nc.vector.memset(gains[:], 0.0)
-        nc.scalar.activation(out=table_warm[:], in_=ones[:, 0:1], func=SQUARE)
-        make_identity(nc, idf[:])
-        nc.vector.memset(pscl[:].rearrange("p g n -> p (g n)").bitcast(I32), 0)
-        nc.gpsimd.tensor_copy(out=idb[:], in_=idf[:])
+        ecod = [kept([P, 4 * CP * P], U32, "ecod%d" % g) for g in range(G)]
+        escl = [kept([P, 4 * CP * P], U8, "escl%d" % g) for g in range(G)]
+        sscl = kept([P, CP, 4], F32, "sscl")
+        sgrp = [kept([P, N, 4], BF16, "sgrp%d" % c) for c in range(CP)]
+        scod = [kept([P, N], U32, "scod%d" % c) for c in range(CP)]
+        sqsc = [kept([P, N], U8, "sqsc%d" % c) for c in range(CP)]
+        dcod = [kept([P, N], U32, "dcod%d" % g) for g in range(G)]
+        dscl = [kept([P, N], U8, "dscl%d" % g) for g in range(G)]
+        pcod = [kept([P, 2 * R], U8, "pcod%d" % g) for g in range(G)]
+        pscl = kept([P, G, R], U8, "pscl")
+        gains = kept([P, N + P], BF16, "gains")
+        ones = kept([P, HALF], BF16, "ones")
+        idf = kept([P, P], F32, "idf")
+        idb = kept([P, P], BF16, "idb")
+        cgain = kept([P, N], BF16, "cgain")
+        table_warm = kept([P, 2], F32, "table_warm")
+        rgain = kept([P, BANDS], F32, "rgain")
 
         echo_g = echo.rearrange("(g p t) k -> g p t k", p=P, t=4)
         steer_c = steer_bytes.rearrange("(c p t) n -> c p t n", p=P, t=4)
+        eraw, esort, xbank, egrp, sraw, swide = {}, {}, {}, {}, {}, {}
+        ybank, dgrp, dtwo, acc, gbank = {}, {}, {}, {}, {}
 
-        def load_echo(g):
-            for t0 in range(0, 4, pieces[g]):
-                nc.sync.dma_start(out=etile[(g, t0)][:], in_=echo_g[g][:, t0 : t0 + pieces[g], :])
+        def load_echo(g, t0, t1):
+            tile = kept([P, t1 - t0, C], BF16, "eraw%d_%d" % (g, t0))
+            nc.sync.dma_start(out=tile[:], in_=echo_g[g][:, t0:t1, :])
+            for t in range(t0, t1):
+                eraw[(g, t)] = tile[:, t - t0, :]
 
-        def load_steer(c, h):
-            nc.sync.dma_start(out=sraw[(c, h)][:], in_=steer_c[c][:, :, h * HALF : (h + 1) * HALF])
+        def load_steer(c, n0, n1):
+            tile = kept([P, 4, n1 - n0], U8, "sraw%d_%d" % (c, n0))
+            nc.sync.dma_start(out=tile[:], in_=steer_c[c][:, :, n0:n1])
+            for b in range(n0 // P, n1 // P):
+                sraw[(c, b)] = (tile, n0)
 
         def load_words(g):
-            nc.sync.dma_start(out=pcod[:, g, :].bitcast(I32), in_=ref_words[g].bitcast(I32))
+            nc.sync.dma_start(out=pcod[g][:].bitcast(I32), in_=ref_words[g].bitcast(I32))
 
-        load_steer(0, 0)
-        load_steer(1, 0)
-        load_echo(0)
-        nc.sync.dma_start(out=gains[0:1, 0:HALF], in_=col_gain[0:HALF].unsqueeze(0))
-        nc.sync.dma_start(out=gains[0 : R // P, HALF : HALF + P], in_=row_gain.rearrange("(c m) -> c m", m=P))
-        load_echo(1)
-        load_echo(2)
-        load_echo(3)
-        load_steer(0, 1)
-        load_steer(1, 1)
-        load_words(0)
-        for q4 in range(4):
-            nc.sync.dma_start(
-                out=pscl[32 * q4 : 32 * q4 + 4, :, :].bitcast(I32),
-                in_=ref_scales[:, 4 * q4 : 4 * q4 + 4, :].rearrange("g r n -> r g n").bitcast(I32),
-            )
-        load_words(1)
-        load_words(2)
-        load_words(3)
-        nc.sync.dma_start(out=cgain[1][:], in_=col_gain[HALF:N].partition_broadcast(P))
+        def load_scales(g0, g1):
+            for q4 in range(4):
+                nc.sync.dma_start(
+                    out=pscl[32 * q4 : 32 * q4 + 4, g0:g1, :].bitcast(I32),
+                    in_=ref_scales[g0:g1, 4 * q4 : 4 * q4 + 4, :].rearrange("g r n -> r g n").bitcast(I32),
+                )
 
         def widen(c, n0, n1, on_vector):
-            h = n0 // HALF
-            cols = slice(n0 - h * HALF, n1 - h * HALF)
-            dst = swide[(c, h)]
+            raw, base = sraw[(c, n0 // P)]
+            wide = kept([P, 4, n1 - n0], BF16, "swide%d_%d" % (c, n0))
+            for b in range(n0 // P, n1 // P):
+                swide[(c, b)] = (wide, n0)
             for t in range(4):
-                src = sraw[(c, h)][:, t, cols].bitcast(FP8)
+                src = raw[:, t, n0 - base : n1 - base].bitcast(FP8)
                 if on_vector:
-                    nc.vector.tensor_scalar(out=dst[:, t, cols], in0=src, scalar1=sscl[:, c, t : t + 1], scalar2=None, op0=MULT)
+                    nc.vector.tensor_scalar(out=wide[:, t, :], in0=src, scalar1=sscl[:, c, t : t + 1], scalar2=None, op0=MULT)
                 else:
-                    nc.scalar.activation(out=dst[:, t, cols], in_=src, func=COPY, scale=sscl[:, c, t : t + 1])
+                    nc.scalar.activation(out=wide[:, t, :], in_=src, func=COPY, scale=sscl[:, c, t : t + 1])
 
         def interleave(c, n0, n1, on_vector):
-            h = n0 // HALF
-            src = swide[(c, h)][:, :, n0 - h * HALF : n1 - h * HALF].rearrange("p t (n i) -> p n t i", i=4)
-            dst = sgrp[c][:, n0:n1, :].rearrange("p (n i) t -> p n t i", i=4)
-            if on_vector:
-                nc.vector.tensor_copy(out=dst, in_=src)
-            else:
-                nc.scalar.copy(out=dst, in_=src)
+            wide, base = swide[(c, n0 // P)]
+            copy = nc.vector.tensor_copy if on_vector else nc.scalar.copy
+            copy(
+                out=sgrp[c][:, n0:n1, :].rearrange("p (n i) t -> p n t i", i=4),
+                in_=wide[:, :, n0 - base : n1 - base].rearrange("p t (n i) -> p n t i", i=4),
+            )
 
         def quant_steer(c, n0, n1):
             nc.vector.quantize_mx(out=scod[c][:, n0:n1].bitcast(FP8X4), scales=sqsc[c][:, n0:n1], in_=sgrp[c][:, n0:n1, :].rearrange("p n t -> p (n t)"))
 
         def sort_words(g, t, on_vector):
-            words = eraw(g, t).bitcast(F32)
-            esort[(g, t)] = keep.tile([P, C // 2], F32, name="esort%d_%d" % (g, t), align_bytes=256)
+            esort[(g, t)] = ring.tile([P, C // 2], F32, name="esort", tag="esort", align_bytes=256)
             copy = nc.vector.tensor_copy if on_vector else nc.scalar.copy
-            copy(out=esort[(g, t)][:].rearrange("p (c u m) -> p c u m", c=CP, u=2), in_=words.rearrange("p (c m u) -> p c u m", c=CP, u=2))
+            copy(out=esort[(g, t)][:].rearrange("p (c u m) -> p c u m", c=CP, u=2), in_=eraw[(g, t)].bitcast(F32).rearrange("p (c m u) -> p c u m", c=CP, u=2))
 
-        xbank = {}
-
-        def turn(g, t):
-            xt = bank("b" if g == 0 else "a")
-            xbank[(g, t)] = xt
-            words = eraw(g, t).bitcast(F32)
+        def turn(g, t, k):
+            xbank[(g, t)] = bank(k)
+            words = eraw[(g, t)].bitcast(F32)
             for c in range(CP):
                 for u in range(2):
                     j = 2 * c + u
                     src = esort[(g, t)][:, j * P : (j + 1) * P] if (g, t) in esort else words[:, 256 * c + u : 256 * (c + 1) : 2]
-                    nc.tensor.transpose(xt[:, j * P : (j + 1) * P], src, idf[:])
+                    nc.tensor.transpose(xbank[(g, t)][:, j * P : (j + 1) * P], src, idf[:])
 
-        def empty(g, t):
-            if t == 0:
-                egrp[g] = lift.tile([P, 4, C], BF16, name="egrp", tag="egrp", align_bytes=256)
-            dst = egrp[g][:, t, :].bitcast(F32)
-            nc.scalar.copy(out=dst.rearrange("p (c r u) -> p c r u", c=CP, u=2), in_=xbank[(g, t)][:].rearrange("p (c u r) -> p c r u", c=CP, u=2))
+        def empty(g, t, on_vector=False):
+            egrp[(g, t)] = ring.tile([P, C], BF16, name="egrp", tag="egrp", align_bytes=256)
+            copy = nc.vector.tensor_copy if on_vector else nc.scalar.copy
+            copy(out=egrp[(g, t)][:].bitcast(F32).rearrange("p (c r u) -> p c r u", c=CP, u=2), in_=xbank[(g, t)][:].rearrange("p (c u r) -> p c r u", c=CP, u=2))
 
         def quant_echo(g, t0, t1):
-            cols = slice(t0 * CP * P, t1 * CP * P)
-            nc.vector.quantize_mx(out=ecod[g][:, cols].bitcast(FP8X4), scales=escl[g][:, cols], in_=egrp[g][:, t0:t1, :].rearrange("p t k -> p (t k)"))
+            for t in range(t0, t1):
+                cols = slice(t * CP * P, (t + 1) * CP * P)
+                nc.vector.quantize_mx(out=ecod[g][:, cols].bitcast(FP8X4), scales=escl[g][:, cols], in_=egrp[(g, t)][:])
 
-        ybank = {}
-        dgrp = {}
+        def first_pass(dst, g, t, c, n0, n1):
+            ecols = slice((t * CP + c) * P, (t * CP + c + 1) * P)
+            nc.tensor.matmul_mx(
+                out=dst,
+                lhsT=ecod[g][:, ecols].bitcast(FP8X4),
+                lhsT_scale=escl[g][:, ecols],
+                rhs=scod[c][:, n0:n1].bitcast(FP8X4),
+                rhs_scale=sqsc[c][:, n0:n1],
+                start=(c == 0),
+                stop=(c == CP - 1),
+            )
 
-        def first_slot(g, b, t):
+        def first_slot(g, b, t, k):
             if t == 0:
-                ybank[(g, b)] = bank("b")
-            ncols = slice(b * P, (b + 1) * P)
+                ybank[(g, b)] = bank(k)
             for c in range(CP):
-                ecols = slice((t * CP + c) * P, (t * CP + c + 1) * P)
-                nc.tensor.matmul_mx(
-                    out=ybank[(g, b)][:, t * P : (t + 1) * P],
-                    lhsT=ecod[g][:, ecols].bitcast(FP8X4),
-                    lhsT_scale=escl[g][:, ecols],
-                    rhs=scod[c][:, ncols].bitcast(FP8X4),
-                    rhs_scale=sqsc[c][:, ncols],
-                    start=(c == 0),
-                    stop=(c == CP - 1),
-                )
+                first_pass(ybank[(g, b)][:, t * P : (t + 1) * P], g, t, c, b * P, (b + 1) * P)
 
-        def first(g, b):
+        def first(g, b, k):
             for t in range(4):
-                first_slot(g, b, t)
+                first_slot(g, b, t, k)
+
+        def first_pairs(g, b, k0, k1):
+            for t0 in (0, 2):
+                for e in range(2):
+                    for t in (t0, t0 + 1):
+                        first_slot(g, b + e, t, (k0, k1)[e])
+
+        def first_both(g, b, k0, k1):
+            for e, t in ((0, 0), (0, 1), (0, 2), (1, 0), (0, 3), (1, 1), (1, 2), (1, 3)):
+                first_slot(g, b + e, t, (k0, k1)[e])
+
+        def first_shared(g, b, t, k0, k1):
+            if t == 0:
+                ybank[(g, b)] = bank(k0)
+                ybank[(g, b + 1)] = bank(k1)
+            for c in range(CP):
+                for e in range(2):
+                    first_pass(ybank[(g, b + e)][:, t * P : (t + 1) * P], g, t, c, (b + e) * P, (b + e + 1) * P)
+
+        def d_tile(g, q):
+            if (g, q) not in dgrp:
+                dgrp[(g, q)] = ring.tile([P, QUART, 4], BF16, name="dgrp", tag="dgrp", align_bytes=256)
+            return dgrp[(g, q)]
 
         def gain(g, b):
-            if b % 4 == 0:
-                dgrp[(g, b // 4)] = ring.tile([P, HALF, 4], BF16, name="dgrp", tag="dgrp", align_bytes=256)
-            d = dgrp[(g, b // 4)][:, (b % 4) * P : (b % 4 + 1) * P, :]
+            d = d_tile(g, b // 2)[:, (b % 2) * P : (b % 2 + 1) * P, :]
             nc.vector.tensor_tensor(
                 out=d.rearrange("p (n i) t -> p n t i", i=4),
                 in0=ybank[(g, b)][:].rearrange("p (t n i) -> p n t i", t=4, i=4),
-                in1=cgain[b // 4][:, (b % 4) * P : (b % 4 + 1) * P].rearrange("p (n i) -> p n i", i=4).unsqueeze(2).to_broadcast([P, P // 4, 4, 4]),
+                in1=cgain[:, b * P : (b + 1) * P].rearrange("p (n i) -> p n i", i=4).unsqueeze(2).to_broadcast([P, P // 4, 4, 4]),
                 op=MULT,
             )
 
-        def quant_d(g, n0, n1):
-            h = n0 // HALF
-            src = dgrp[(g, h)][:, n0 - h * HALF : n1 - h * HALF, :]
-            nc.vector.quantize_mx(out=dcod[g][:, n0:n1].bitcast(FP8X4), scales=dscl[g][:, n0:n1], in_=src.rearrange("p n t -> p (n t)"))
-
-        lifted = {}
-
-        def first_wide(g):
-            lifted[g] = lift.tile([P, 4, HALF], F32, name="lifted", tag="lifted", align_bytes=256)
-            for t in range(4):
-                yb = bank("b")
+        def first_two(g, q, u, k):
+            ybank[(g, q, u)] = bank(k)
+            for e in range(2):
                 for c in range(CP):
-                    ecols = slice((t * CP + c) * P, (t * CP + c + 1) * P)
-                    nc.tensor.matmul_mx(
-                        out=yb[:],
-                        lhsT=ecod[g][:, ecols].bitcast(FP8X4),
-                        lhsT_scale=escl[g][:, ecols],
-                        rhs=scod[c][:, HALF:N].bitcast(FP8X4),
-                        rhs_scale=sqsc[c][:, HALF:N],
-                        start=(c == 0),
-                        stop=(c == CP - 1),
-                    )
-                nc.scalar.copy(out=lifted[g][:, t, :], in_=yb[:])
+                    first_pass(ybank[(g, q, u)][:, e * QUART : (e + 1) * QUART], g, 2 * u + e, c, q * QUART, (q + 1) * QUART)
 
-        def gain_wide(g, q):
-            if q == 0:
-                dgrp[(g, 1)] = ring.tile([P, HALF, 4], BF16, name="dgrp", tag="dgrp", align_bytes=256)
-            cols = slice(q * QUART, (q + 1) * QUART)
+        def gain_two(g, q, u):
+            if u == 0:
+                dtwo[(g, q)] = ring.tile([P, 2, QUART, 2], BF16, name="dtwo", tag="dtwo", align_bytes=256)
             nc.vector.tensor_tensor(
-                out=dgrp[(g, 1)][:, cols, :].rearrange("p (n i) t -> p n t i", i=4),
-                in0=lifted[g][:, :, cols].rearrange("p t (n i) -> p n t i", i=4),
-                in1=cgain[1][:, cols].rearrange("p (n i) -> p n i", i=4).unsqueeze(2).to_broadcast([P, QUART // 4, 4, 4]),
+                out=dtwo[(g, q)][:, u, :, :],
+                in0=ybank[(g, q, u)][:].rearrange("p (e n) -> p n e", e=2),
+                in1=cgain[:, q * QUART : (q + 1) * QUART].unsqueeze(2).to_broadcast([P, QUART, 2]),
                 op=MULT,
             )
 
-        acc = {}
-
-        def second(i, h, g):
-            if g == 0:
-                acc[(i, h)] = bank("b" if (h == 0 and i in (4, 5)) else "a")
-            ncols = slice(h * HALF, (h + 1) * HALF)
-            nc.tensor.matmul_mx(
-                out=acc[(i, h)][:],
-                lhsT=pcod[:, g, i * 2 * P : (i + 1) * 2 * P].bitcast(FP4X4),
-                lhsT_scale=pscl[:, g, i * P : (i + 1) * P],
-                rhs=dcod[g][:, ncols].bitcast(FP8X4),
-                rhs_scale=dscl[g][:, ncols],
-                start=(g == 0),
-                stop=(g == G - 1),
+        def join(g, q, on_vector):
+            copy = nc.vector.tensor_copy if on_vector else nc.scalar.copy
+            copy(
+                out=d_tile(g, q)[:].rearrange("p n t -> p (n t)").bitcast(F32).rearrange("p (n u) -> p n u", u=2),
+                in_=dtwo[(g, q)][:].rearrange("p u n e -> p (u n e)").bitcast(F32).rearrange("p (u n) -> p n u", u=2),
             )
 
-        def finish(i, h):
-            o = stage.tile([P, HALF], F32, name="o", tag="o")
-            nc.scalar.activation(out=o[:], in_=acc[(i, h)][:], func=SQUARE, scale=rgain[:, i : i + 1])
-            nc.sync.dma_start(out=out[i * P : (i + 1) * P, h * HALF : (h + 1) * HALF], in_=o[:])
+        def quant_d(g, b0, b1):
+            src = dgrp[(g, b0 // 2)][:, (b0 % 2) * P : (b0 % 2 + b1 - b0) * P, :]
+            cols = slice(b0 * P, b1 * P)
+            nc.vector.quantize_mx(out=dcod[g][:, cols].bitcast(FP8X4), scales=dscl[g][:, cols], in_=src.rearrange("p n t -> p (n t)"))
 
-        def last_tile():
-            i = R // P - 1
-            for j in range(4):
-                part = bank("b")
-                ncols = slice(HALF + j * P, HALF + (j + 1) * P)
-                for g in range(G):
-                    nc.tensor.matmul_mx(
-                        out=part[:, 0:P],
-                        lhsT=pcod[:, g, i * 2 * P : (i + 1) * 2 * P].bitcast(FP4X4),
-                        lhsT_scale=pscl[:, g, i * P : (i + 1) * P],
-                        rhs=dcod[g][:, ncols].bitcast(FP8X4),
-                        rhs_scale=dscl[g][:, ncols],
-                        start=(g == 0),
-                        stop=(g == G - 1),
-                    )
-                o = stage.tile([P, P], F32, name="olast", tag="olast")
-                nc.scalar.activation(out=o[:], in_=part[:, 0:P], func=SQUARE, scale=rgain[:, i : i + 1])
-                nc.sync.dma_start(out=out[i * P : (i + 1) * P, ncols], in_=o[:])
+        def second_pass(dst, i, g, n0, n1, start, stop):
+            nc.tensor.matmul_mx(
+                out=dst,
+                lhsT=pcod[g][:, i * 2 * P : (i + 1) * 2 * P].bitcast(FP4X4),
+                lhsT_scale=pscl[:, g, i * P : (i + 1) * P],
+                rhs=dcod[g][:, n0:n1].bitcast(FP8X4),
+                rhs_scale=dscl[g][:, n0:n1],
+                start=start,
+                stop=stop,
+            )
 
-        scratch = bank("a")
+        def second_quarter(g, q, banks):
+            for i in range(BANDS):
+                if g == 0 and i % 2 == 0:
+                    acc[(i // 2, q)] = bank(banks[i // 2])
+                dst = acc[(i // 2, q)][:, (i % 2) * QUART : (i % 2 + 1) * QUART]
+                second_pass(dst, i, g, q * QUART, (q + 1) * QUART, g == 0 and i % 2 == 0, g == G - 1 and i % 2 == 1)
 
-        def warm(n):
+        def finish_quarter(j, q):
+            o = stage.tile([P, 2, QUART], F32, name="o", tag="o", align_bytes=256)
+            for e in range(2):
+                i = 2 * j + e
+                nc.scalar.activation(out=o[:, e, :], in_=acc[(j, q)][:, e * QUART : (e + 1) * QUART], func=SQUARE, scale=rgain[:, i : i + 1])
+            nc.sync.dma_start(out=out[2 * j * P : (2 * j + 2) * P, q * QUART : (q + 1) * QUART].rearrange("(e p) n -> p e n", e=2), in_=o[:])
+
+        def second(i, g, n0, n1, k):
+            if g == 0:
+                acc[(i, n0, n1)] = bank(k)
+            second_pass(acc[(i, n0, n1)][:, 0 : n1 - n0], i, g, n0, n1, g == 0, g == G - 1)
+
+        def finish(i, n0, n1):
+            o = stage.tile([P, HALF], F32, name="o", tag="o", align_bytes=256)
+            nc.scalar.activation(out=o[:, 0 : n1 - n0], in_=acc[(i, n0, n1)][:, 0 : n1 - n0], func=SQUARE, scale=rgain[:, i : i + 1])
+            nc.sync.dma_start(out=out[i * P : (i + 1) * P, n0:n1], in_=o[:, 0 : n1 - n0])
+
+        def spread_gains(h, k):
+            gbank[h] = bank(k)
+            nc.tensor.matmul(out=gbank[h][:, 0:QUART].bitcast(BF16), lhsT=ones[:, 0:P], rhs=gains[:, h * HALF : (h + 1) * HALF], start=True, stop=True)
+
+        def keep_gains(h, on_vector):
+            copy = nc.vector.tensor_copy if on_vector else nc.scalar.copy
+            copy(out=cgain[:, h * HALF : (h + 1) * HALF], in_=gbank[h][:, 0:QUART].bitcast(BF16))
+
+        def row_gains(k):
+            rb = bank(k)
+            nc.tensor.matmul(out=rb[:, 0:BANDS], lhsT=gains[:, N : N + P], rhs=idb[:, 0:BANDS], start=True, stop=True)
+            return rb[:, 0:BANDS]
+
+        def constants():
+            nc.scalar.dma_start(out=sscl[:], in_=steer_scale.rearrange("(c p t) o -> p c (t o)", p=P, t=4))
+            nc.vector.memset(table_warm[:, 0:1], 1.0)
+            nc.scalar.activation(out=table_warm[:, 1:2], in_=table_warm[:, 0:1], func=SQUARE)
+            nc.vector.memset(ones[:].bitcast(I32), TWO_ONES)
+            nc.vector.memset(gains[:].bitcast(I32), 0)
+            make_identity(nc, idf[:])
+            nc.scalar.copy(out=idb[:], in_=idf[:])
+            nc.vector.memset(pscl[:].rearrange("p g n -> p (g n)").bitcast(I32), 0)
+
+        def load_col_gain():
+            nc.sync.dma_start(out=gains[0:1, 0:N], in_=col_gain.unsqueeze(0))
+
+        def load_row_gain():
+            nc.sync.dma_start(out=gains[0:BANDS, N : N + P], in_=row_gain.rearrange("(c m) -> c m", m=P))
+
+        def warm(n, k):
+            scratch = bank(k)
             for j in range(n):
-                nc.tensor.matmul(out=scratch[:], lhsT=idb[:], rhs=ones[:], start=True, stop=True)
-
-        def spread_gain():
-            pg = scratch[:, 0 : HALF // 2].bitcast(BF16)
-            nc.tensor.matmul(out=pg, lhsT=ones[:, 0:P], rhs=gains[:, 0:HALF], start=True, stop=True)
-            return pg
-
-        def row_gains():
-            pr = scratch[:, HALF // 2 : HALF // 2 + R // P]
-            nc.tensor.matmul(out=pr, lhsT=gains[:, HALF : HALF + P], rhs=idb[:, 0 : R // P], start=True, stop=True)
-            return pr
-
-        def partial(h, g, bands):
-            for i in bands:
-                second(i, h, g)
-
-        def whole(i, h):
-            for g in range(G):
-                second(i, h, g)
-            finish(i, h)
+                nc.tensor.matmul(out=scratch[:], lhsT=ones[:, 0:P], rhs=ones[:], start=True, stop=True)
 
 
-        warm(4)
-        widen(0, 0, QUART, True)
-        widen(1, 0, QUART, False)
-        widen(0, QUART, HALF, True)
+        V, S = True, False
+        constants()
+        load_steer(0, 0, QUART)
+        load_steer(1, 0, QUART)
+        load_col_gain()
         for t in range(4):
-            turn(0, t)
-            empty(0, t)
-        turn(1, 0)
-        interleave(0, 0, QUART, True)
-        interleave(1, 0, QUART, True)
+            load_echo(0, t, t + 1)
+        for t in range(4):
+            load_echo(1, t, t + 1)
+        load_words(0)
+        load_scales(0, 2)
+        load_echo(2, 0, 2)
+        load_echo(2, 2, 4)
+        load_words(1)
+        load_steer(0, QUART, HALF)
+        load_steer(1, QUART, HALF)
+        load_row_gain()
+        load_echo(3, 0, 2)
+        load_echo(3, 2, 4)
+        load_words(2)
+        load_scales(2, 4)
+        load_steer(0, HALF, N)
+        load_steer(1, HALF, N)
+        load_words(3)
+
+
+        warm(4, 7)
+        spread_gains(0, 6)
+        widen(0, 0, QUART, V)
+        widen(1, 0, QUART, V)
+        interleave(0, 0, QUART, S)
+        turn(0, 0, 0)
+        empty(0, 0)
+        spread_gains(1, 7)
+        interleave(1, 0, QUART, V)
+        turn(0, 1, 1)
+        empty(0, 1)
+        keep_gains(0, V)
         quant_steer(0, 0, QUART)
         quant_steer(1, 0, QUART)
-        quant_echo(0, 0, 2)
-        widen(1, QUART, HALF, True)
-        quant_echo(0, 2, 4)
-        interleave(0, QUART, HALF, True)
-        interleave(1, QUART, HALF, True)
-        quant_steer(0, QUART, HALF)
-        quant_steer(1, QUART, HALF)
-        pg = spread_gain()
-        pr = row_gains()
-        nc.scalar.copy(out=cgain[0][:], in_=pg)
-        nc.scalar.copy(out=rgain[:], in_=pr)
-        for t in range(1, 4):
-            sort_words(1, t, False)
+        quant_echo(0, 0, 1)
+        turn(0, 2, 2)
+        empty(0, 2)
+        turn(0, 3, 3)
+        empty(0, 3)
+        quant_echo(0, 1, 2)
+        quant_echo(0, 2, 3)
+        quant_echo(0, 3, 4)
         for t in range(4):
-            first_slot(0, 0, t)
-            first_slot(0, 1, t)
-        for t in range(4):
-            if t > 0:
-                turn(1, t)
-            empty(1, t)
-        first(0, 2)
-        first(0, 3)
-
+            first_slot(0, 0, t, 4)
+            first_slot(0, 1, t, 5)
+        sort_words(1, 0, S)
+        keep_gains(1, S)
+        sort_words(1, 1, V)
+        sort_words(1, 2, V)
         gain(0, 0)
-        for t in range(2):
-            sort_words(2, t, True)
         gain(0, 1)
-        quant_echo(1, 0, 2)
-        for t in range(1, 3):
-            sort_words(3, t, False)
         for t in range(4):
-            turn(2, t)
-            empty(2, t)
-        sort_words(3, 3, False)
-        gain(0, 2)
-        quant_echo(1, 2, 4)
-        first(1, 0)
-        first(1, 1)
-        gain(0, 3)
-        sort_words(3, 0, True)
-        first(1, 2)
-        first(1, 3)
-        for t in range(4):
-            turn(3, t)
-            empty(3, t)
-        for c in range(CP):
-            widen(c, HALF, N, False)
+            turn(1, t, (0, 1, 6, 7)[t])
+            empty(1, t)
+        quant_d(0, 0, 1)
+        quant_d(0, 1, 2)
+        quant_echo(1, 0, 4)
+        ACC = (2, 3, 0, 1)
+        work = [4, 5, 6, 7]
         for g in range(1, G):
-            nxt = g + 1
-            if g == 1:
-                quant_d(0, 0, HALF)
+            second_quarter(g - 1, 0, ACC)
+            if g < G - 1:
+                for t in range(4):
+                    sort_words(g + 1, t, t == 2 if g == 1 else t > 0)
+            if g == 2:
+                interleave(0, QUART, HALF, S)
+            first_both(g, 0, work[0], work[1])
             gain(g, 0)
             gain(g, 1)
-            if nxt < G:
-                quant_echo(nxt, 0, 4)
-            if g > 1:
-                quant_d(g - 1, 0, HALF)
-            if g == 2:
-                partial(0, 0, range(4))
-            if nxt < G:
-                first(nxt, 0)
-                first(nxt, 1)
-            gain(g, 2)
-            if g == 3:
-                quant_d(3, 0, QUART)
-            gain(g, 3)
-            if nxt < G:
-                first(nxt, 2)
-                first(nxt, 3)
-        partial(0, 1, range(4))
-        partial(0, 2, range(4))
+            quant_d(g, 0, 1)
+            quant_d(g, 1, 2)
+            if g < G - 1:
+                for t in range(4):
+                    turn(g + 1, t, work[(t + 2) % 4])
+                    empty(g + 1, t)
+                widen(g - 1, QUART, HALF, V)
+                quant_echo(g + 1, 0, 2)
+                quant_echo(g + 1, 2, 3)
+                quant_echo(g + 1, 3, 4)
+                if g == 2:
+                    interleave(1, QUART, HALF - P, V)
+                    quant_steer(0, QUART, HALF)
+                    quant_steer(1, QUART, HALF - P)
+                    interleave(1, HALF - P, HALF, S)
+                work = work[2:] + work[:2]
+        pr = row_gains(work[2])
+        nc.scalar.copy(out=rgain[:], in_=pr)
+        widen(0, HALF, N, S)
+        work = [work[3], work[2], work[0], work[1]]
         for g in range(G - 1):
-            partial(0, g, (4, 5))
-        quant_d(3, QUART, HALF)
-        for n0 in (HALF, HALF + QUART):
-            interleave(0, n0, n0 + QUART, False)
-            interleave(1, n0, n0 + QUART, True)
-            quant_steer(0, n0, n0 + QUART)
-            quant_steer(1, n0, n0 + QUART)
+            first(g, 2, work[g])
+        second_quarter(G - 1, 0, ACC)
+        quant_steer(1, HALF - P, HALF)
+        for g in range(G - 1):
+            gain(g, 2)
+        for j in range(4):
+            finish_quarter(j, 0)
+        widen(1, HALF, N, S)
+        interleave(0, HALF + QUART, N, S)
+        interleave(1, HALF + QUART, N, S)
+        for g in range(G - 1):
+            first(g, 3, work[(g + 3) % 4])
+        first(G - 1, 2, work[2])
+        interleave(0, HALF, HALF + QUART, V)
+        gain(0, 3)
+        gain(1, 3)
+        quant_d(0, 2, 4)
+        second_quarter(0, 1, ACC)
+        first(G - 1, 3, work[3])
+        gain(2, 3)
+        quant_d(1, 2, 4)
+        gain(3, 2)
+        quant_d(2, 2, 4)
+        second_quarter(1, 1, ACC)
+        second_quarter(2, 1, ACC)
+        gain(3, 3)
+        interleave(1, HALF, HALF + QUART, V)
+        quant_steer(0, HALF, HALF + QUART)
+        quant_steer(1, HALF, HALF + QUART)
+        quant_d(3, 2, 4)
+        quant_steer(0, HALF + QUART, N)
+        quant_steer(1, HALF + QUART, N)
 
-        partial(0, 3, (0, 4, 5, 1, 2, 3))
-        for i in (4, 5, 0, 1, 2, 3):
-            finish(i, 0)
-        for b in range(4, 8):
-            first(0, b)
-            gain(0, b)
-        quant_d(0, HALF, N)
-        for g in range(1, G):
-            first_wide(g)
-            if g > 1:
-                whole(4 + g, 0)
-            gain_wide(g, 0)
-            gain_wide(g, 1)
-            quant_d(g, HALF, HALF + QUART)
-            quant_d(g, HALF + QUART, N)
         for g in range(G):
-            partial(1, g, range(4))
+            narrow = g >= G - 2
+            first_two(g, 2, 0, work[0])
+            first_two(g, 2, 1, work[1])
+            gain_two(g, 2, 0)
+            if 0 < g < G - 1:
+                quant_d(g - 1, 6, 8)
+            gain_two(g, 2, 1)
+            join(g, 2, S)
+            if narrow:
+                first(g, 6, work[2])
+                first(g, 7, work[3])
+                gain(g, 6)
+                gain(g, 7)
+                quant_d(g, 4, 6)
+                quant_d(g, 6, 7)
+                quant_d(g, 7, 8)
+            else:
+                first_two(g, 3, 0, work[2])
+                first_two(g, 3, 1, work[3])
+                gain_two(g, 3, 0)
+                gain_two(g, 3, 1)
+                quant_d(g, 4, 6)
+                join(g, 3, S)
+            if g == 0:
+                second_quarter(G - 1, 1, ACC)
+                for j in range(4):
+                    finish_quarter(j, 1)
+            else:
+                for i in range(4):
+                    second(i, g - 1, HALF, N, ACC[i])
+        EARLY = 2
+        for g in range(EARLY):
+            second(4, g, HALF, N, work[0])
         for i in range(4):
-            finish(i, 1)
-        for i in range(4, 7):
-            whole(i, 1)
-        last_tile()
+            second(i, G - 1, HALF, N, i)
+            finish(i, HALF, N)
+        for i in (4, 5, 6):
+            for g in range(EARLY if i == 4 else 0, G):
+                second(i, g, HALF, N, work[i - 4])
+            finish(i, HALF, N)
+        for n0, n1, k in ((HALF, HALF + QUART, work[3]), (HALF + QUART, N - P, ACC[0]), (N - P, N, ACC[1])):
+            for g in range(G):
+                second(7, g, n0, n1, k)
+            finish(7, n0, n1)

@@ -227,8 +227,8 @@ def tile_sonar_ping_coherence_s13_kernel(tc, echo, steer_bytes, steer_scale, ref
                 stop=stop,
             )
 
-        def second_quarter(g, q, banks):
-            for i in range(BANDS):
+        def second_quarter(g, q, banks, bands=range(BANDS)):
+            for i in bands:
                 if g == 0 and i % 2 == 0:
                     acc[(i // 2, q)] = bank(banks[i // 2])
                 dst = acc[(i // 2, q)][:, (i % 2) * QUART : (i % 2 + 1) * QUART]
@@ -246,10 +246,12 @@ def tile_sonar_ping_coherence_s13_kernel(tc, echo, steer_bytes, steer_scale, ref
                 acc[(i, n0, n1)] = bank(k)
             second_pass(acc[(i, n0, n1)][:, 0 : n1 - n0], i, g, n0, n1, g == 0, g == G - 1)
 
-        def finish(i, n0, n1):
-            o = stage.tile([P, HALF], F32, name="o", tag="o", align_bytes=256)
-            nc.scalar.activation(out=o[:, 0 : n1 - n0], in_=acc[(i, n0, n1)][:, 0 : n1 - n0], func=SQUARE, scale=rgain[:, i : i + 1])
-            nc.sync.dma_start(out=out[i * P : (i + 1) * P, n0:n1], in_=o[:, 0 : n1 - n0])
+        def finish(i, n0, n1, piece=HALF):
+            for a in range(0, n1 - n0, piece):
+                w = min(piece, n1 - n0)
+                o = stage.tile([P, HALF], F32, name="o", tag="o", align_bytes=256)
+                nc.scalar.activation(out=o[:, 0:w], in_=acc[(i, n0, n1)][:, a : a + w], func=SQUARE, scale=rgain[:, i : i + 1])
+                nc.sync.dma_start(out=out[i * P : (i + 1) * P, n0 + a : n0 + a + w], in_=o[:, 0:w])
 
         def spread_gains(h, k):
             gbank[h] = bank(k)
@@ -296,21 +298,21 @@ def tile_sonar_ping_coherence_s13_kernel(tc, echo, steer_bytes, steer_scale, ref
         for t in range(4):
             load_echo(1, t, t + 1)
         load_words(0)
-        load_scales(0, 2)
+        load_scales(0, 1)
         load_echo(2, 0, 2)
         load_echo(2, 2, 4)
         load_words(1)
+        load_scales(1, 2)
         load_steer(0, QUART, HALF)
-        load_steer(1, QUART, HALF)
-        load_row_gain()
         load_echo(3, 0, 2)
         load_echo(3, 2, 4)
+        load_steer(1, QUART, HALF)
         load_words(2)
         load_scales(2, 4)
+        load_row_gain()
         load_steer(0, HALF, N)
-        load_steer(1, HALF, N)
         load_words(3)
-
+        load_steer(1, HALF, N)
 
         warm(4, 7)
         spread_gains(0, 6)
@@ -415,47 +417,47 @@ def tile_sonar_ping_coherence_s13_kernel(tc, echo, steer_bytes, steer_scale, ref
         quant_steer(0, HALF + QUART, N)
         quant_steer(1, HALF + QUART, N)
 
+        held = [(i, g) for g in range(G - 1) for i in range(4)]
         for g in range(G):
-            narrow = g >= G - 2
-            first_two(g, 2, 0, work[0])
-            first_two(g, 2, 1, work[1])
-            gain_two(g, 2, 0)
-            if 0 < g < G - 1:
-                quant_d(g - 1, 6, 8)
-            gain_two(g, 2, 1)
-            join(g, 2, S)
-            if narrow:
-                first(g, 6, work[2])
-                first(g, 7, work[3])
-                gain(g, 6)
-                gain(g, 7)
-                quant_d(g, 4, 6)
-                quant_d(g, 6, 7)
-                quant_d(g, 7, 8)
-            else:
-                first_two(g, 3, 0, work[2])
-                first_two(g, 3, 1, work[3])
-                gain_two(g, 3, 0)
-                gain_two(g, 3, 1)
-                quant_d(g, 4, 6)
-                join(g, 3, S)
-            if g == 0:
-                second_quarter(G - 1, 1, ACC)
-                for j in range(4):
-                    finish_quarter(j, 1)
-            else:
-                for i in range(4):
-                    second(i, g - 1, HALF, N, ACC[i])
-        EARLY = 2
-        for g in range(EARLY):
-            second(4, g, HALF, N, work[0])
+            for q in (2, 3):
+                step = 2 * g + q - 2
+                ka, kb = work[2 * (q - 2)], work[2 * (q - 2) + 1]
+                if step == 2 * G - 1:
+                    first(g, 6, ka)
+                    first(g, 7, kb)
+                    gain(g, 6)
+                    gain(g, 7)
+                    quant_d(g, 4, 6)
+                    quant_d(g, 6, 7)
+                    quant_d(g, 7, 8)
+                else:
+                    first_two(g, q, 0, ka)
+                    first_two(g, q, 1, kb)
+                    gain_two(g, q, 0)
+                    gain_two(g, q, 1)
+                    if step > 0:
+                        pg, pq = divmod(step - 1, 2)
+                        quant_d(pg, 4 + 2 * pq, 6 + 2 * pq)
+                    join(g, q, S)
+                if step in (2, 3):
+                    j0 = 2 * (step - 2)
+                    second_quarter(G - 1, 1, ACC, range(2 * j0, 2 * j0 + 4))
+                    finish_quarter(j0, 1)
+                    finish_quarter(j0 + 1, 1)
+                elif 3 < step < 2 * G - 1:
+                    i, gg = held.pop(0)
+                    second(i, gg, HALF, N, ACC[i])
+        for i, gg in held:
+            if gg < G - 2:
+                second(i, gg, HALF, N, ACC[i])
         for i in range(4):
-            second(i, G - 1, HALF, N, i)
+            second(i, G - 2, HALF, N, ACC[i])
+            second(i, G - 1, HALF, N, ACC[i])
             finish(i, HALF, N)
         for i in (4, 5, 6):
-            for g in range(EARLY if i == 4 else 0, G):
+            for g in range(G):
                 second(i, g, HALF, N, work[i - 4])
-            finish(i, HALF, N)
+            finish(i, HALF, N, QUART if i == 6 else HALF)
         for n0, n1, k in ((HALF, HALF + QUART, work[3]), (HALF + QUART, N - P, ACC[0]), (N - P, N, ACC[1])):
             for g in range(G):
                 second(7, g, n0, n1, k)

@@ -87,12 +87,13 @@ def tile_sonar_ping_coherence_s13_kernel(tc, echo, steer_bytes, steer_scale, ref
                     in_=ref_scales[g0:g1, 4 * q4 : 4 * q4 + 4, :].rearrange("g r n -> r g n").bitcast(I32),
                 )
 
-        def widen(c, n0, n1, on_vector):
+        def widen(c, n0, n1, on_vector, slots=range(4)):
             raw, base = sraw[(c, n0 // P)]
-            wide = kept([P, 4, n1 - n0], BF16, "swide%d_%d" % (c, n0))
-            for b in range(n0 // P, n1 // P):
-                swide[(c, b)] = (wide, n0)
-            for t in range(4):
+            if (c, n0 // P) not in swide:
+                for b in range(n0 // P, n1 // P):
+                    swide[(c, b)] = (kept([P, 4, n1 - n0], BF16, "swide%d_%d" % (c, n0)) if b == n0 // P else swide[(c, n0 // P)][0], n0)
+            wide = swide[(c, n0 // P)][0]
+            for t in slots:
                 src = raw[:, t, n0 - base : n1 - base].bitcast(FP8)
                 if on_vector:
                     nc.vector.tensor_scalar(out=wide[:, t, :], in0=src, scalar1=sscl[:, c, t : t + 1], scalar2=None, op0=MULT)
@@ -125,14 +126,17 @@ def tile_sonar_ping_coherence_s13_kernel(tc, echo, steer_bytes, steer_scale, ref
                     nc.tensor.transpose(xbank[(g, t)][:, j * P : (j + 1) * P], src, idf[:])
 
         def empty(g, t, on_vector=False):
-            egrp[(g, t)] = ring.tile([P, C], BF16, name="egrp", tag="egrp", align_bytes=256)
+            if g > 0 and t == 1:
+                egrp[(g, 1)] = egrp[(g, 0)]
+            else:
+                egrp[(g, t)] = ring.tile([P, 2, C], BF16, name="egrp", tag="egrp", align_bytes=256)
+            row = 1 if g > 0 and t == 1 else 0
             copy = nc.vector.tensor_copy if on_vector else nc.scalar.copy
-            copy(out=egrp[(g, t)][:].bitcast(F32).rearrange("p (c r u) -> p c r u", c=CP, u=2), in_=xbank[(g, t)][:].rearrange("p (c u r) -> p c r u", c=CP, u=2))
+            copy(out=egrp[(g, t)][:, row, :].bitcast(F32).rearrange("p (c r u) -> p c r u", c=CP, u=2), in_=xbank[(g, t)][:].rearrange("p (c u r) -> p c r u", c=CP, u=2))
 
         def quant_echo(g, t0, t1):
-            for t in range(t0, t1):
-                cols = slice(t * CP * P, (t + 1) * CP * P)
-                nc.vector.quantize_mx(out=ecod[g][:, cols].bitcast(FP8X4), scales=escl[g][:, cols], in_=egrp[(g, t)][:])
+            cols = slice(t0 * CP * P, t1 * CP * P)
+            nc.vector.quantize_mx(out=ecod[g][:, cols].bitcast(FP8X4), scales=escl[g][:, cols], in_=egrp[(g, t0)][:, 0 : t1 - t0, :].rearrange("p t k -> p (t k)"))
 
         def first_pass(dst, g, t, c, n0, n1):
             ecols = slice((t * CP + c) * P, (t * CP + c + 1) * P)
@@ -261,10 +265,11 @@ def tile_sonar_ping_coherence_s13_kernel(tc, echo, steer_bytes, steer_scale, ref
             copy = nc.vector.tensor_copy if on_vector else nc.scalar.copy
             copy(out=cgain[:, h * HALF : (h + 1) * HALF], in_=gbank[h][:, 0:QUART].bitcast(BF16))
 
-        def row_gains(k):
-            rb = bank(k)
-            nc.tensor.matmul(out=rb[:, 0:BANDS], lhsT=gains[:, N : N + P], rhs=idb[:, 0:BANDS], start=True, stop=True)
-            return rb[:, 0:BANDS]
+        def row_gains():
+            nc.tensor.matmul(out=gbank[1][:, QUART : QUART + BANDS], lhsT=gains[:, N : N + P], rhs=idb[:, 0:BANDS], start=True, stop=True)
+
+        def keep_row_gains():
+            nc.scalar.copy(out=rgain[:], in_=gbank[1][:, QUART : QUART + BANDS])
 
         def constants():
             nc.scalar.dma_start(out=sscl[:], in_=steer_scale.rearrange("(c p t) o -> p c (t o)", p=P, t=4))
@@ -295,37 +300,38 @@ def tile_sonar_ping_coherence_s13_kernel(tc, echo, steer_bytes, steer_scale, ref
         load_col_gain()
         for t in range(4):
             load_echo(0, t, t + 1)
+        load_row_gain()
         for t in range(4):
             load_echo(1, t, t + 1)
         load_words(0)
         load_scales(0, 1)
+        load_steer(0, QUART, HALF)
         load_echo(2, 0, 2)
         load_echo(2, 2, 4)
         load_words(1)
         load_scales(1, 2)
-        load_steer(0, QUART, HALF)
+        load_steer(1, QUART, HALF)
         load_echo(3, 0, 2)
         load_echo(3, 2, 4)
-        load_steer(1, QUART, HALF)
         load_words(2)
         load_scales(2, 4)
-        load_row_gain()
         load_steer(0, HALF, N)
-        load_words(3)
         load_steer(1, HALF, N)
+        load_words(3)
 
         warm(4, 7)
         spread_gains(0, 6)
         widen(0, 0, QUART, V)
-        widen(1, 0, QUART, V)
-        interleave(0, 0, QUART, S)
+        widen(1, 0, QUART, V, (0, 1))
+        widen(1, 0, QUART, S, (2, 3))
+        keep_gains(0, S)
+        interleave(0, 0, QUART, V)
         turn(0, 0, 0)
         empty(0, 0)
-        spread_gains(1, 7)
         interleave(1, 0, QUART, V)
         turn(0, 1, 1)
         empty(0, 1)
-        keep_gains(0, V)
+        spread_gains(1, 7)
         quant_steer(0, 0, QUART)
         quant_steer(1, 0, QUART)
         quant_echo(0, 0, 1)
@@ -339,119 +345,120 @@ def tile_sonar_ping_coherence_s13_kernel(tc, echo, steer_bytes, steer_scale, ref
         for t in range(4):
             first_slot(0, 0, t, 4)
             first_slot(0, 1, t, 5)
+            if t == 1:
+                row_gains()
         sort_words(1, 0, S)
         keep_gains(1, S)
+        keep_row_gains()
         sort_words(1, 1, V)
-        sort_words(1, 2, V)
-        gain(0, 0)
-        gain(0, 1)
-        for t in range(4):
-            turn(1, t, (0, 1, 6, 7)[t])
-            empty(1, t)
-        quant_d(0, 0, 1)
-        quant_d(0, 1, 2)
-        quant_echo(1, 0, 4)
+        sort_words(1, 2, S)
         ACC = (2, 3, 0, 1)
-        work = [4, 5, 6, 7]
-        for g in range(1, G):
-            second_quarter(g - 1, 0, ACC)
-            if g < G - 1:
-                for t in range(4):
-                    sort_words(g + 1, t, t == 2 if g == 1 else t > 0)
-            if g == 2:
-                interleave(0, QUART, HALF, S)
-            first_both(g, 0, work[0], work[1])
+        work = [4, 5, 0, 1]
+        MID = QUART + P
+        for g in range(G):
+            if g > 0:
+                second_quarter(g - 1, 0, ACC)
+                if g < G - 1:
+                    for t in range(3):
+                        sort_words(g + 1, t, S)
+                first_both(g, 0, work[0], work[1])
             gain(g, 0)
             gain(g, 1)
             quant_d(g, 0, 1)
             quant_d(g, 1, 2)
             if g < G - 1:
                 for t in range(4):
-                    turn(g + 1, t, work[(t + 2) % 4])
+                    turn(g + 1, t, (0, 1, 6, 7)[t] if g == 0 else work[(t + 2) % 4])
                     empty(g + 1, t)
-                widen(g - 1, QUART, HALF, V)
+                if g == 1:
+                    widen(1, QUART, HALF, V)
+                if g == 2:
+                    interleave(1, QUART, MID, V)
                 quant_echo(g + 1, 0, 2)
                 quant_echo(g + 1, 2, 3)
                 quant_echo(g + 1, 3, 4)
+                if g == 0:
+                    widen(0, QUART, HALF, V)
+                if g == 1:
+                    interleave(0, QUART, MID, V)
                 if g == 2:
-                    interleave(1, QUART, HALF - P, V)
-                    quant_steer(0, QUART, HALF)
-                    quant_steer(1, QUART, HALF - P)
-                    interleave(1, HALF - P, HALF, S)
-                work = work[2:] + work[:2]
-        pr = row_gains(work[2])
-        nc.scalar.copy(out=rgain[:], in_=pr)
+                    quant_steer(0, QUART, MID)
+                    quant_steer(1, QUART, MID)
+                    interleave(0, MID, HALF, S)
+                    interleave(1, MID, HALF, S)
+                work = [4, 5, 6, 7] if g == 0 else work[2:] + work[:2]
         widen(0, HALF, N, S)
-        work = [work[3], work[2], work[0], work[1]]
+        work = work[2:] + work[:2]
         for g in range(G - 1):
             first(g, 2, work[g])
         second_quarter(G - 1, 0, ACC)
-        quant_steer(1, HALF - P, HALF)
+        quant_steer(0, MID, HALF)
+        quant_steer(1, MID, HALF)
         for g in range(G - 1):
             gain(g, 2)
         for j in range(4):
             finish_quarter(j, 0)
-        widen(1, HALF, N, S)
-        interleave(0, HALF + QUART, N, S)
-        interleave(1, HALF + QUART, N, S)
+        widen(1, HALF, HALF + QUART, S)
+        widen(1, HALF + QUART, N, S)
+        for c in range(CP):
+            interleave(c, HALF + QUART, N, S)
         for g in range(G - 1):
             first(g, 3, work[(g + 3) % 4])
         first(G - 1, 2, work[2])
         interleave(0, HALF, HALF + QUART, V)
         gain(0, 3)
+        first(G - 1, 3, work[3])
         gain(1, 3)
         quant_d(0, 2, 4)
         second_quarter(0, 1, ACC)
-        first(G - 1, 3, work[3])
         gain(2, 3)
         quant_d(1, 2, 4)
-        gain(3, 2)
-        quant_d(2, 2, 4)
-        second_quarter(1, 1, ACC)
-        second_quarter(2, 1, ACC)
-        gain(3, 3)
         interleave(1, HALF, HALF + QUART, V)
         quant_steer(0, HALF, HALF + QUART)
         quant_steer(1, HALF, HALF + QUART)
-        quant_d(3, 2, 4)
-        quant_steer(0, HALF + QUART, N)
-        quant_steer(1, HALF + QUART, N)
+        gain(3, 2)
+        second_quarter(1, 1, ACC)
+        gain(3, 3)
+        quant_d(2, 2, 4)
 
         held = [(i, g) for g in range(G - 1) for i in range(4)]
-        for g in range(G):
-            for q in (2, 3):
-                step = 2 * g + q - 2
-                ka, kb = work[2 * (q - 2)], work[2 * (q - 2) + 1]
-                if step == 2 * G - 1:
-                    first(g, 6, ka)
-                    first(g, 7, kb)
-                    gain(g, 6)
-                    gain(g, 7)
-                    quant_d(g, 4, 6)
-                    quant_d(g, 6, 7)
-                    quant_d(g, 7, 8)
-                else:
-                    first_two(g, q, 0, ka)
-                    first_two(g, q, 1, kb)
-                    gain_two(g, q, 0)
-                    gain_two(g, q, 1)
-                    if step > 0:
-                        pg, pq = divmod(step - 1, 2)
-                        quant_d(pg, 4 + 2 * pq, 6 + 2 * pq)
-                    join(g, q, S)
-                if step in (2, 3):
-                    j0 = 2 * (step - 2)
-                    second_quarter(G - 1, 1, ACC, range(2 * j0, 2 * j0 + 4))
+        steps = [(0, 2), (1, 2), (0, 3), (1, 3), (2, 2), (2, 3), (3, 2), (3, 3)]
+        for step, (g, q) in enumerate(steps):
+            ka, kb = work[2 * (step % 2)], work[2 * (step % 2) + 1]
+            if step == 2 * G - 1:
+                first(g, 6, ka)
+                first(g, 7, kb)
+                gain(g, 6)
+                gain(g, 7)
+                quant_d(g, 4, 6)
+                quant_d(g, 6, 7)
+                quant_d(g, 7, 8)
+            else:
+                first_two(g, q, 0, ka)
+                first_two(g, q, 1, kb)
+                gain_two(g, q, 0)
+                if step == 0:
+                    quant_d(G - 1, 2, 4)
+                gain_two(g, q, 1)
+                if step == 0:
+                    quant_steer(0, HALF + QUART, N)
+                    quant_steer(1, HALF + QUART, N)
+                if step > 0:
+                    pg, pq = steps[step - 1]
+                    quant_d(pg, 2 * pq, 2 * pq + 2)
+                join(g, q, S)
+            if step < 4:
+                j0 = 2 * (step % 2)
+                second_quarter(G - 2 + step // 2, 1, ACC, range(2 * j0, 2 * j0 + 4))
+                if step >= 2:
                     finish_quarter(j0, 1)
                     finish_quarter(j0 + 1, 1)
-                elif 3 < step < 2 * G - 1:
-                    i, gg = held.pop(0)
-                    second(i, gg, HALF, N, ACC[i])
-        for i, gg in held:
-            if gg < G - 2:
+            elif 3 < step < 2 * G - 1:
+                i, gg = held.pop(0)
                 second(i, gg, HALF, N, ACC[i])
+        for i, gg in held:
+            second(i, gg, HALF, N, ACC[i])
         for i in range(4):
-            second(i, G - 2, HALF, N, ACC[i])
             second(i, G - 1, HALF, N, ACC[i])
             finish(i, HALF, N)
         for i in (4, 5, 6):

@@ -52,8 +52,8 @@ def tile_sonar_ping_coherence_s13_kernel(tc, echo, steer_bytes, steer_scale, ref
         dscl = [kept([P, N], U8, "dscl%d" % g) for g in range(G)]
         pcod = [kept([P, 2 * R], U8, "pcod%d" % g) for g in range(G)]
         pscl = kept([P, G, R], U8, "pscl")
-        gains = kept([P, N + P], BF16, "gains")
-        ones = kept([P, HALF], BF16, "ones")
+        gains = kept([P, N + P + 2], BF16, "gains")
+        ones = kept([P, HALF + 2], BF16, "ones")
         idf = kept([P, P], F32, "idf")
         idb = kept([P, P], BF16, "idb")
         cgain = kept([P, N], BF16, "cgain")
@@ -133,6 +133,25 @@ def tile_sonar_ping_coherence_s13_kernel(tc, echo, steer_bytes, steer_scale, ref
             row = 1 if g > 0 and t == 1 else 0
             copy = nc.vector.tensor_copy if on_vector else nc.scalar.copy
             copy(out=egrp[(g, t)][:, row, :].bitcast(F32).rearrange("p (c r u) -> p c r u", c=CP, u=2), in_=xbank[(g, t)][:].rearrange("p (c u r) -> p c r u", c=CP, u=2))
+
+        def load_echo_pass(g, t, c):
+            tile = kept([P, HALF], BF16, "eraw%d_%d_%d" % (g, t, c))
+            nc.sync.dma_start(out=tile[:], in_=echo_g[g][:, t, c * HALF : (c + 1) * HALF])
+            eraw[(g, t, c)] = tile
+
+        def turn_pass(g, t, c, k):
+            xbank[(g, t, c)] = bank(k)
+            words = eraw[(g, t, c)][:].bitcast(F32)
+            for u in range(2):
+                nc.tensor.transpose(xbank[(g, t, c)][:, u * P : (u + 1) * P], words[:, u:QUART:2], idf[:])
+
+        def empty_pass(g, t, c):
+            egrp[(g, t, c)] = kept([P, HALF], BF16, "epass%d_%d_%d" % (g, t, c))
+            nc.scalar.copy(out=egrp[(g, t, c)][:].bitcast(F32).rearrange("p (r u) -> p r u", u=2), in_=xbank[(g, t, c)][:, 0:QUART].rearrange("p (u r) -> p r u", u=2))
+
+        def quant_echo_pass(g, t, c):
+            cols = slice((t * CP + c) * P, (t * CP + c + 1) * P)
+            nc.vector.quantize_mx(out=ecod[g][:, cols].bitcast(FP8X4), scales=escl[g][:, cols], in_=egrp[(g, t, c)][:])
 
         def quant_echo(g, t0, t1):
             cols = slice(t0 * CP * P, t1 * CP * P)
@@ -250,12 +269,12 @@ def tile_sonar_ping_coherence_s13_kernel(tc, echo, steer_bytes, steer_scale, ref
                 acc[(i, n0, n1)] = bank(k)
             second_pass(acc[(i, n0, n1)][:, 0 : n1 - n0], i, g, n0, n1, g == 0, g == G - 1)
 
-        def finish(i, n0, n1, piece=HALF):
+        def finish(i, n0, n1, piece=HALF, queue=nc.sync):
             for a in range(0, n1 - n0, piece):
                 w = min(piece, n1 - n0)
                 o = stage.tile([P, HALF], F32, name="o", tag="o", align_bytes=256)
                 nc.scalar.activation(out=o[:, 0:w], in_=acc[(i, n0, n1)][:, a : a + w], func=SQUARE, scale=rgain[:, i : i + 1])
-                nc.sync.dma_start(out=out[i * P : (i + 1) * P, n0 + a : n0 + a + w], in_=o[:, 0:w])
+                queue.dma_start(out=out[i * P : (i + 1) * P, n0 + a : n0 + a + w], in_=o[:, 0:w])
 
         def spread_gains(h, k):
             gbank[h] = bank(k)
@@ -268,16 +287,17 @@ def tile_sonar_ping_coherence_s13_kernel(tc, echo, steer_bytes, steer_scale, ref
         def row_gains():
             nc.tensor.matmul(out=gbank[1][:, QUART : QUART + BANDS], lhsT=gains[:, N : N + P], rhs=idb[:, 0:BANDS], start=True, stop=True)
 
-        def keep_row_gains():
-            nc.scalar.copy(out=rgain[:], in_=gbank[1][:, QUART : QUART + BANDS])
+        def keep_row_gains(on_vector):
+            copy = nc.vector.tensor_copy if on_vector else nc.scalar.copy
+            copy(out=rgain[:], in_=gbank[1][:, QUART : QUART + BANDS])
 
         def constants():
             nc.scalar.dma_start(out=sscl[:], in_=steer_scale.rearrange("(c p t) o -> p c (t o)", p=P, t=4))
             nc.vector.memset(table_warm[:, 0:1], 1.0)
             nc.scalar.activation(out=table_warm[:, 1:2], in_=table_warm[:, 0:1], func=SQUARE)
             nc.vector.memset(ones[:].bitcast(I32), TWO_ONES)
-            nc.vector.memset(gains[:].bitcast(I32), 0)
             make_identity(nc, idf[:])
+            nc.vector.memset(gains[:].bitcast(I32), 0)
             nc.scalar.copy(out=idb[:], in_=idf[:])
             nc.vector.memset(pscl[:].rearrange("p g n -> p (g n)").bitcast(I32), 0)
 
@@ -287,19 +307,20 @@ def tile_sonar_ping_coherence_s13_kernel(tc, echo, steer_bytes, steer_scale, ref
         def load_row_gain():
             nc.sync.dma_start(out=gains[0:BANDS, N : N + P], in_=row_gain.rearrange("(c m) -> c m", m=P))
 
-        def warm(n, k):
+        def warm(n, k, moving):
             scratch = bank(k)
             for j in range(n):
-                nc.tensor.matmul(out=scratch[:], lhsT=ones[:, 0:P], rhs=ones[:], start=True, stop=True)
+                nc.tensor.matmul(out=scratch[:], lhsT=ones[:, 0:P], rhs=moving, start=True, stop=True)
 
 
         V, S = True, False
         constants()
         load_steer(0, 0, QUART)
         load_steer(1, 0, QUART)
-        load_col_gain()
         for t in range(4):
             load_echo(0, t, t + 1)
+            if t == 1:
+                load_col_gain()
         load_row_gain()
         for t in range(4):
             load_echo(1, t, t + 1)
@@ -319,19 +340,18 @@ def tile_sonar_ping_coherence_s13_kernel(tc, echo, steer_bytes, steer_scale, ref
         load_steer(1, HALF, N)
         load_words(3)
 
-        warm(4, 7)
-        spread_gains(0, 6)
+        warm(3, 7, ones[:, 0:HALF])
         widen(0, 0, QUART, V)
+        warm(2, 7, swide[(0, 0)][0][:, 0:2, :].rearrange("p t n -> p (t n)"))
         widen(1, 0, QUART, V, (0, 1))
         widen(1, 0, QUART, S, (2, 3))
-        keep_gains(0, S)
         interleave(0, 0, QUART, V)
         turn(0, 0, 0)
         empty(0, 0)
         interleave(1, 0, QUART, V)
         turn(0, 1, 1)
         empty(0, 1)
-        spread_gains(1, 7)
+        spread_gains(0, 6)
         quant_steer(0, 0, QUART)
         quant_steer(1, 0, QUART)
         quant_echo(0, 0, 1)
@@ -340,16 +360,18 @@ def tile_sonar_ping_coherence_s13_kernel(tc, echo, steer_bytes, steer_scale, ref
         turn(0, 3, 3)
         empty(0, 3)
         quant_echo(0, 1, 2)
+        keep_gains(0, V)
         quant_echo(0, 2, 3)
         quant_echo(0, 3, 4)
         for t in range(4):
             first_slot(0, 0, t, 4)
             first_slot(0, 1, t, 5)
             if t == 1:
+                spread_gains(1, 7)
                 row_gains()
         sort_words(1, 0, S)
         keep_gains(1, S)
-        keep_row_gains()
+        keep_row_gains(S)
         sort_words(1, 1, V)
         sort_words(1, 2, S)
         ACC = (2, 3, 0, 1)

@@ -52,10 +52,10 @@ def tile_sonar_ping_coherence_s13_kernel(tc, echo, steer_bytes, steer_scale, ref
         dscl = [kept([P, N], U8, "dscl%d" % g) for g in range(G)]
         pcod = [kept([P, 2 * R], U8, "pcod%d" % g) for g in range(G)]
         pscl = kept([P, G, R], U8, "pscl")
-        gains = kept([P, N + P + 2], BF16, "gains")
+        gains = kept([P, HALF + P + 2], BF16, "gains")
         ones = kept([P, HALF + 2], BF16, "ones")
         idf = kept([P, P], F32, "idf")
-        idb = kept([P, P], BF16, "idb")
+        idb = kept([P, BANDS], BF16, "idb")
         cgain = kept([P, N], BF16, "cgain")
         table_warm = kept([P, 2], F32, "table_warm")
         rgain = kept([P, BANDS], F32, "rgain")
@@ -280,16 +280,16 @@ def tile_sonar_ping_coherence_s13_kernel(tc, echo, steer_bytes, steer_scale, ref
             gbank[h] = bank(k)
             nc.tensor.matmul(out=gbank[h][:, 0:QUART].bitcast(BF16), lhsT=ones[:, 0:P], rhs=gains[:, h * HALF : (h + 1) * HALF], start=True, stop=True)
 
-        def keep_gains(h, on_vector):
+        def keep_gains(n0, n1, on_vector):
             copy = nc.vector.tensor_copy if on_vector else nc.scalar.copy
-            copy(out=cgain[:, h * HALF : (h + 1) * HALF], in_=gbank[h][:, 0:QUART].bitcast(BF16))
+            copy(out=cgain[:, n0:n1], in_=gbank[0][:, n0 // 2 : n1 // 2].bitcast(BF16))
 
         def row_gains():
-            nc.tensor.matmul(out=gbank[1][:, QUART : QUART + BANDS], lhsT=gains[:, N : N + P], rhs=idb[:, 0:BANDS], start=True, stop=True)
+            nc.tensor.matmul(out=gbank[0][:, QUART : QUART + BANDS], lhsT=gains[:, HALF : HALF + P], rhs=idb[:, 0:BANDS], start=True, stop=True)
 
         def keep_row_gains(on_vector):
             copy = nc.vector.tensor_copy if on_vector else nc.scalar.copy
-            copy(out=rgain[:], in_=gbank[1][:, QUART : QUART + BANDS])
+            copy(out=rgain[:], in_=gbank[0][:, QUART : QUART + BANDS])
 
         def constants():
             nc.scalar.dma_start(out=sscl[:], in_=steer_scale.rearrange("(c p t) o -> p c (t o)", p=P, t=4))
@@ -298,14 +298,19 @@ def tile_sonar_ping_coherence_s13_kernel(tc, echo, steer_bytes, steer_scale, ref
             nc.vector.memset(ones[:].bitcast(I32), TWO_ONES)
             make_identity(nc, idf[:])
             nc.vector.memset(gains[:].bitcast(I32), 0)
-            nc.scalar.copy(out=idb[:], in_=idf[:])
             nc.vector.memset(pscl[:].rearrange("p g n -> p (g n)").bitcast(I32), 0)
 
         def load_col_gain():
-            nc.sync.dma_start(out=gains[0:1, 0:N], in_=col_gain.unsqueeze(0))
+            nc.scalar.dma_start(out=gains[0:1, 0:HALF], in_=col_gain[0:HALF].unsqueeze(0))
+
+        def small_identity():
+            nc.scalar.copy(out=idb[:], in_=idf[:, 0:BANDS])
+
+        def load_spread_gain():
+            nc.sync.dma_start(out=cgain[:, HALF:N], in_=col_gain[HALF:N].partition_broadcast(P))
 
         def load_row_gain():
-            nc.sync.dma_start(out=gains[0:BANDS, N : N + P], in_=row_gain.rearrange("(c m) -> c m", m=P))
+            nc.scalar.dma_start(out=gains[0:BANDS, HALF : HALF + P], in_=row_gain.rearrange("(c m) -> c m", m=P))
 
         def warm(n, k, moving):
             scratch = bank(k)
@@ -319,26 +324,27 @@ def tile_sonar_ping_coherence_s13_kernel(tc, echo, steer_bytes, steer_scale, ref
         load_steer(1, 0, QUART)
         for t in range(4):
             load_echo(0, t, t + 1)
-            if t == 1:
-                load_col_gain()
+        load_col_gain()
         load_row_gain()
-        for t in range(4):
-            load_echo(1, t, t + 1)
+        small_identity()
+        load_echo(1, 0, 2)
+        load_scales(0, 2)
+        load_echo(1, 2, 3)
+        load_echo(1, 3, 4)
         load_words(0)
-        load_scales(0, 1)
-        load_steer(0, QUART, HALF)
         load_echo(2, 0, 2)
         load_echo(2, 2, 4)
+        load_steer(0, QUART, HALF)
         load_words(1)
-        load_scales(1, 2)
-        load_steer(1, QUART, HALF)
+        load_scales(2, 4)
         load_echo(3, 0, 2)
+        load_steer(1, QUART, HALF)
         load_echo(3, 2, 4)
         load_words(2)
-        load_scales(2, 4)
         load_steer(0, HALF, N)
         load_steer(1, HALF, N)
         load_words(3)
+        load_spread_gain()
 
         warm(3, 7, ones[:, 0:HALF])
         widen(0, 0, QUART, V)
@@ -351,7 +357,6 @@ def tile_sonar_ping_coherence_s13_kernel(tc, echo, steer_bytes, steer_scale, ref
         interleave(1, 0, QUART, V)
         turn(0, 1, 1)
         empty(0, 1)
-        spread_gains(0, 6)
         quant_steer(0, 0, QUART)
         quant_steer(1, 0, QUART)
         quant_echo(0, 0, 1)
@@ -359,21 +364,19 @@ def tile_sonar_ping_coherence_s13_kernel(tc, echo, steer_bytes, steer_scale, ref
         empty(0, 2)
         turn(0, 3, 3)
         empty(0, 3)
+        spread_gains(0, 6)
+        row_gains()
         quant_echo(0, 1, 2)
-        keep_gains(0, V)
         quant_echo(0, 2, 3)
+        keep_gains(0, QUART, V)
         quant_echo(0, 3, 4)
         for t in range(4):
             first_slot(0, 0, t, 4)
             first_slot(0, 1, t, 5)
-            if t == 1:
-                spread_gains(1, 7)
-                row_gains()
         sort_words(1, 0, S)
-        keep_gains(1, S)
+        keep_gains(QUART, HALF, S)
         keep_row_gains(S)
         sort_words(1, 1, V)
-        sort_words(1, 2, S)
         ACC = (2, 3, 0, 1)
         work = [4, 5, 0, 1]
         MID = QUART + P
@@ -393,16 +396,15 @@ def tile_sonar_ping_coherence_s13_kernel(tc, echo, steer_bytes, steer_scale, ref
                     turn(g + 1, t, (0, 1, 6, 7)[t] if g == 0 else work[(t + 2) % 4])
                     empty(g + 1, t)
                 if g == 1:
-                    widen(1, QUART, HALF, V)
+                    widen(0, QUART, HALF, V)
                 if g == 2:
+                    interleave(0, QUART, MID, V)
                     interleave(1, QUART, MID, V)
                 quant_echo(g + 1, 0, 2)
                 quant_echo(g + 1, 2, 3)
                 quant_echo(g + 1, 3, 4)
-                if g == 0:
-                    widen(0, QUART, HALF, V)
                 if g == 1:
-                    interleave(0, QUART, MID, V)
+                    widen(1, QUART, HALF, V)
                 if g == 2:
                     quant_steer(0, QUART, MID)
                     quant_steer(1, QUART, MID)

@@ -19,12 +19,16 @@ SQUARE = mybir.ActivationFunctionType.Square
 MULT = mybir.AluOpType.mult
 
 P = 128
+SLOTS = 4
 G = T // 512
 CP = C // 512
 HALF = 512
 QUART = 256
 BANDS = R // P
+OPEN = 4
+LAST_SLOT = SLOTS - 1
 TWO_ONES = 0x3F803F80
+VECTOR, SCALAR = True, False
 
 
 def tile_sonar_ping_coherence_s13_kernel(tc, echo, steer_bytes, steer_scale, ref_words, ref_scales, col_gain, row_gain, out):
@@ -42,10 +46,13 @@ def tile_sonar_ping_coherence_s13_kernel(tc, echo, steer_bytes, steer_scale, ref
         def bank(k):
             return psum.tile([P, 512], F32, name="bank%d" % k, tag="bank%d" % k)
 
-        ecod = [kept([P, 4 * CP * P], U32, "ecod%d" % g) for g in range(G)]
-        escl = [kept([P, 4 * CP * P], U8, "escl%d" % g) for g in range(G)]
-        sscl = kept([P, CP, 4], F32, "sscl")
-        sgrp = [kept([P, N, 4], BF16, "sgrp%d" % c) for c in range(CP)]
+        def copier(on_vector):
+            return nc.vector.tensor_copy if on_vector else nc.scalar.copy
+
+        ecod = [kept([P, SLOTS * CP * P], U32, "ecod%d" % g) for g in range(G)]
+        escl = [kept([P, SLOTS * CP * P], U8, "escl%d" % g) for g in range(G)]
+        sscl = kept([P, CP, SLOTS], F32, "sscl")
+        sgrp = [kept([P, N, SLOTS], BF16, "sgrp%d" % c) for c in range(CP)]
         scod = [kept([P, N], U32, "scod%d" % c) for c in range(CP)]
         sqsc = [kept([P, N], U8, "sqsc%d" % c) for c in range(CP)]
         dcod = [kept([P, N], U32, "dcod%d" % g) for g in range(G)]
@@ -60,10 +67,10 @@ def tile_sonar_ping_coherence_s13_kernel(tc, echo, steer_bytes, steer_scale, ref
         table_warm = kept([P, 2], F32, "table_warm")
         rgain = kept([P, BANDS], F32, "rgain")
 
-        echo_g = echo.rearrange("(g p t) k -> g p t k", p=P, t=4)
-        steer_c = steer_bytes.rearrange("(c p t) n -> c p t n", p=P, t=4)
-        eraw, esort, xbank, egrp, sraw, swide = {}, {}, {}, {}, {}, {}
-        ybank, dgrp, dtwo, acc, gbank = {}, {}, {}, {}, {}
+        echo_g = echo.rearrange("(g p t) k -> g p t k", p=P, t=SLOTS)
+        steer_c = steer_bytes.rearrange("(c p t) n -> c p t n", p=P, t=SLOTS)
+        eraw, esort, xbank, egrp, epass, sraw, swide = {}, {}, {}, {}, {}, {}, {}
+        ybank, ytwo, dgrp, dtwo, pair_sum, band_sum = {}, {}, {}, {}, {}, {}
 
         def load_echo(g, t0, t1):
             tile = kept([P, t1 - t0, C], BF16, "eraw%d_%d" % (g, t0))
@@ -72,7 +79,7 @@ def tile_sonar_ping_coherence_s13_kernel(tc, echo, steer_bytes, steer_scale, ref
                 eraw[(g, t)] = tile[:, t - t0, :]
 
         def load_steer(c, n0, n1):
-            tile = kept([P, 4, n1 - n0], U8, "sraw%d_%d" % (c, n0))
+            tile = kept([P, SLOTS, n1 - n0], U8, "sraw%d_%d" % (c, n0))
             nc.sync.dma_start(out=tile[:], in_=steer_c[c][:, :, n0:n1])
             for b in range(n0 // P, n1 // P):
                 sraw[(c, b)] = (tile, n0)
@@ -81,17 +88,18 @@ def tile_sonar_ping_coherence_s13_kernel(tc, echo, steer_bytes, steer_scale, ref
             nc.sync.dma_start(out=pcod[g][:].bitcast(I32), in_=ref_words[g].bitcast(I32))
 
         def load_scales(g0, g1):
-            for q4 in range(4):
+            for a in range(4):
                 nc.sync.dma_start(
-                    out=pscl[32 * q4 : 32 * q4 + 4, g0:g1, :].bitcast(I32),
-                    in_=ref_scales[g0:g1, 4 * q4 : 4 * q4 + 4, :].rearrange("g r n -> r g n").bitcast(I32),
+                    out=pscl[32 * a : 32 * a + 4, g0:g1, :].bitcast(I32),
+                    in_=ref_scales[g0:g1, 4 * a : 4 * a + 4, :].rearrange("g r n -> r g n").bitcast(I32),
                 )
 
-        def widen(c, n0, n1, on_vector, slots=range(4)):
+        def widen(c, n0, n1, on_vector, slots=range(SLOTS)):
             raw, base = sraw[(c, n0 // P)]
             if (c, n0 // P) not in swide:
+                tile = kept([P, SLOTS, n1 - n0], BF16, "swide%d_%d" % (c, n0))
                 for b in range(n0 // P, n1 // P):
-                    swide[(c, b)] = (kept([P, 4, n1 - n0], BF16, "swide%d_%d" % (c, n0)) if b == n0 // P else swide[(c, n0 // P)][0], n0)
+                    swide[(c, b)] = (tile, n0)
             wide = swide[(c, n0 // P)][0]
             for t in slots:
                 src = raw[:, t, n0 - base : n1 - base].bitcast(FP8)
@@ -102,8 +110,7 @@ def tile_sonar_ping_coherence_s13_kernel(tc, echo, steer_bytes, steer_scale, ref
 
         def interleave(c, n0, n1, on_vector):
             wide, base = swide[(c, n0 // P)]
-            copy = nc.vector.tensor_copy if on_vector else nc.scalar.copy
-            copy(
+            copier(on_vector)(
                 out=sgrp[c][:, n0:n1, :].rearrange("p (n i) t -> p n t i", i=4),
                 in_=wide[:, :, n0 - base : n1 - base].rearrange("p t (n i) -> p n t i", i=4),
             )
@@ -113,8 +120,10 @@ def tile_sonar_ping_coherence_s13_kernel(tc, echo, steer_bytes, steer_scale, ref
 
         def sort_words(g, t, on_vector):
             esort[(g, t)] = ring.tile([P, C // 2], F32, name="esort", tag="esort", align_bytes=256)
-            copy = nc.vector.tensor_copy if on_vector else nc.scalar.copy
-            copy(out=esort[(g, t)][:].rearrange("p (c u m) -> p c u m", c=CP, u=2), in_=eraw[(g, t)].bitcast(F32).rearrange("p (c m u) -> p c u m", c=CP, u=2))
+            copier(on_vector)(
+                out=esort[(g, t)][:].rearrange("p (c u m) -> p c u m", c=CP, u=2),
+                in_=eraw[(g, t)].bitcast(F32).rearrange("p (c m u) -> p c u m", c=CP, u=2),
+            )
 
         def turn(g, t, k):
             xbank[(g, t)] = bank(k)
@@ -122,114 +131,95 @@ def tile_sonar_ping_coherence_s13_kernel(tc, echo, steer_bytes, steer_scale, ref
             for c in range(CP):
                 for u in range(2):
                     j = 2 * c + u
-                    src = esort[(g, t)][:, j * P : (j + 1) * P] if (g, t) in esort else words[:, 256 * c + u : 256 * (c + 1) : 2]
+                    src = esort[(g, t)][:, j * P : (j + 1) * P] if (g, t) in esort else words[:, 2 * P * c + u : 2 * P * (c + 1) : 2]
                     nc.tensor.transpose(xbank[(g, t)][:, j * P : (j + 1) * P], src, idf[:])
 
-        def empty(g, t, on_vector=False):
-            if g > 0 and t == 1:
-                egrp[(g, 1)] = egrp[(g, 0)]
-            else:
-                egrp[(g, t)] = ring.tile([P, 2, C], BF16, name="egrp", tag="egrp", align_bytes=256)
-            row = 1 if g > 0 and t == 1 else 0
-            copy = nc.vector.tensor_copy if on_vector else nc.scalar.copy
-            copy(out=egrp[(g, t)][:, row, :].bitcast(F32).rearrange("p (c r u) -> p c r u", c=CP, u=2), in_=xbank[(g, t)][:].rearrange("p (c u r) -> p c r u", c=CP, u=2))
-
-        def load_echo_pass(g, t, c):
-            tile = kept([P, HALF], BF16, "eraw%d_%d_%d" % (g, t, c))
-            nc.sync.dma_start(out=tile[:], in_=echo_g[g][:, t, c * HALF : (c + 1) * HALF])
-            eraw[(g, t, c)] = tile
-
-        def turn_pass(g, t, c, k):
-            xbank[(g, t, c)] = bank(k)
-            words = eraw[(g, t, c)][:].bitcast(F32)
-            for u in range(2):
-                nc.tensor.transpose(xbank[(g, t, c)][:, u * P : (u + 1) * P], words[:, u:QUART:2], idf[:])
-
-        def empty_pass(g, t, c):
-            egrp[(g, t, c)] = kept([P, HALF], BF16, "epass%d_%d_%d" % (g, t, c))
-            nc.scalar.copy(out=egrp[(g, t, c)][:].bitcast(F32).rearrange("p (r u) -> p r u", u=2), in_=xbank[(g, t, c)][:, 0:QUART].rearrange("p (u r) -> p r u", u=2))
-
-        def quant_echo_pass(g, t, c):
-            cols = slice((t * CP + c) * P, (t * CP + c + 1) * P)
-            nc.vector.quantize_mx(out=ecod[g][:, cols].bitcast(FP8X4), scales=escl[g][:, cols], in_=egrp[(g, t, c)][:])
+        def empty(g, t):
+            shares = g > 0 and t == 1
+            egrp[(g, t)] = egrp[(g, 0)] if shares else ring.tile([P, 2, C], BF16, name="egrp", tag="egrp", align_bytes=256)
+            nc.scalar.copy(
+                out=egrp[(g, t)][:, 1 if shares else 0, :].bitcast(F32).rearrange("p (c r u) -> p c r u", c=CP, u=2),
+                in_=xbank[(g, t)][:].rearrange("p (c u r) -> p c r u", c=CP, u=2),
+            )
 
         def quant_echo(g, t0, t1):
             cols = slice(t0 * CP * P, t1 * CP * P)
             nc.vector.quantize_mx(out=ecod[g][:, cols].bitcast(FP8X4), scales=escl[g][:, cols], in_=egrp[(g, t0)][:, 0 : t1 - t0, :].rearrange("p t k -> p (t k)"))
 
-        def first_pass(dst, g, t, c, n0, n1):
-            ecols = slice((t * CP + c) * P, (t * CP + c + 1) * P)
-            nc.tensor.matmul_mx(
-                out=dst,
-                lhsT=ecod[g][:, ecols].bitcast(FP8X4),
-                lhsT_scale=escl[g][:, ecols],
-                rhs=scod[c][:, n0:n1].bitcast(FP8X4),
-                rhs_scale=sqsc[c][:, n0:n1],
-                start=(c == 0),
-                stop=(c == CP - 1),
-            )
+        def empty_last(g):
+            for c in range(CP):
+                epass[(g, c)] = ring.tile([P, HALF], BF16, name="epass", tag="epass", align_bytes=256)
+                nc.scalar.copy(
+                    out=epass[(g, c)][:].bitcast(F32).rearrange("p (r u) -> p r u", u=2),
+                    in_=xbank[(g, LAST_SLOT)][:, 2 * P * c : 2 * P * (c + 1)].rearrange("p (u r) -> p r u", u=2),
+                )
+
+        def quant_echo_last(g):
+            for c in range(CP):
+                cols = slice((LAST_SLOT * CP + c) * P, (LAST_SLOT * CP + c + 1) * P)
+                nc.vector.quantize_mx(out=ecod[g][:, cols].bitcast(FP8X4), scales=escl[g][:, cols], in_=epass[(g, c)][:])
+
+        def first_sum(dst, g, t, n0, n1):
+            for c in range(CP):
+                ecols = slice((t * CP + c) * P, (t * CP + c + 1) * P)
+                nc.tensor.matmul_mx(
+                    out=dst,
+                    lhsT=ecod[g][:, ecols].bitcast(FP8X4),
+                    lhsT_scale=escl[g][:, ecols],
+                    rhs=scod[c][:, n0:n1].bitcast(FP8X4),
+                    rhs_scale=sqsc[c][:, n0:n1],
+                    start=(c == 0),
+                    stop=(c == CP - 1),
+                )
 
         def first_slot(g, b, t, k):
             if t == 0:
                 ybank[(g, b)] = bank(k)
-            for c in range(CP):
-                first_pass(ybank[(g, b)][:, t * P : (t + 1) * P], g, t, c, b * P, (b + 1) * P)
+            first_sum(ybank[(g, b)][:, t * P : (t + 1) * P], g, t, b * P, (b + 1) * P)
 
         def first(g, b, k):
-            for t in range(4):
+            for t in range(SLOTS):
                 first_slot(g, b, t, k)
 
-        def first_pairs(g, b, k0, k1):
-            for t0 in (0, 2):
-                for e in range(2):
-                    for t in (t0, t0 + 1):
-                        first_slot(g, b + e, t, (k0, k1)[e])
-
-        def first_both(g, b, k0, k1):
-            for e, t in ((0, 0), (0, 1), (0, 2), (1, 0), (0, 3), (1, 1), (1, 2), (1, 3)):
-                first_slot(g, b + e, t, (k0, k1)[e])
-
-        def first_shared(g, b, t, k0, k1):
-            if t == 0:
-                ybank[(g, b)] = bank(k0)
-                ybank[(g, b + 1)] = bank(k1)
-            for c in range(CP):
-                for e in range(2):
-                    first_pass(ybank[(g, b + e)][:, t * P : (t + 1) * P], g, t, c, (b + e) * P, (b + e + 1) * P)
+        def first_both(g, k0, k1):
+            for t in range(LAST_SLOT):
+                first_slot(g, 0, t, k0)
+            first_slot(g, 1, 0, k1)
+            first_slot(g, 0, LAST_SLOT, k0)
+            for t in range(1, SLOTS):
+                first_slot(g, 1, t, k1)
 
         def d_tile(g, q):
             if (g, q) not in dgrp:
-                dgrp[(g, q)] = ring.tile([P, QUART, 4], BF16, name="dgrp", tag="dgrp", align_bytes=256)
+                dgrp[(g, q)] = ring.tile([P, QUART, SLOTS], BF16, name="dgrp", tag="dgrp", align_bytes=256)
             return dgrp[(g, q)]
 
         def gain(g, b):
             d = d_tile(g, b // 2)[:, (b % 2) * P : (b % 2 + 1) * P, :]
             nc.vector.tensor_tensor(
                 out=d.rearrange("p (n i) t -> p n t i", i=4),
-                in0=ybank[(g, b)][:].rearrange("p (t n i) -> p n t i", t=4, i=4),
-                in1=cgain[:, b * P : (b + 1) * P].rearrange("p (n i) -> p n i", i=4).unsqueeze(2).to_broadcast([P, P // 4, 4, 4]),
+                in0=ybank[(g, b)][:].rearrange("p (t n i) -> p n t i", t=SLOTS, i=4),
+                in1=cgain[:, b * P : (b + 1) * P].rearrange("p (n i) -> p n i", i=4).unsqueeze(2).to_broadcast([P, P // 4, SLOTS, 4]),
                 op=MULT,
             )
 
         def first_two(g, q, u, k):
-            ybank[(g, q, u)] = bank(k)
+            ytwo[(g, q, u)] = bank(k)
             for e in range(2):
-                for c in range(CP):
-                    first_pass(ybank[(g, q, u)][:, e * QUART : (e + 1) * QUART], g, 2 * u + e, c, q * QUART, (q + 1) * QUART)
+                first_sum(ytwo[(g, q, u)][:, e * QUART : (e + 1) * QUART], g, 2 * u + e, q * QUART, (q + 1) * QUART)
 
         def gain_two(g, q, u):
             if u == 0:
                 dtwo[(g, q)] = ring.tile([P, 2, QUART, 2], BF16, name="dtwo", tag="dtwo", align_bytes=256)
             nc.vector.tensor_tensor(
                 out=dtwo[(g, q)][:, u, :, :],
-                in0=ybank[(g, q, u)][:].rearrange("p (e n) -> p n e", e=2),
+                in0=ytwo[(g, q, u)][:].rearrange("p (e n) -> p n e", e=2),
                 in1=cgain[:, q * QUART : (q + 1) * QUART].unsqueeze(2).to_broadcast([P, QUART, 2]),
                 op=MULT,
             )
 
-        def join(g, q, on_vector):
-            copy = nc.vector.tensor_copy if on_vector else nc.scalar.copy
-            copy(
+        def join(g, q):
+            nc.scalar.copy(
                 out=d_tile(g, q)[:].rearrange("p n t -> p (n t)").bitcast(F32).rearrange("p (n u) -> p n u", u=2),
                 in_=dtwo[(g, q)][:].rearrange("p u n e -> p (u n e)").bitcast(F32).rearrange("p (u n) -> p n u", u=2),
             )
@@ -238,6 +228,9 @@ def tile_sonar_ping_coherence_s13_kernel(tc, echo, steer_bytes, steer_scale, ref
             src = dgrp[(g, b0 // 2)][:, (b0 % 2) * P : (b0 % 2 + b1 - b0) * P, :]
             cols = slice(b0 * P, b1 * P)
             nc.vector.quantize_mx(out=dcod[g][:, cols].bitcast(FP8X4), scales=dscl[g][:, cols], in_=src.rearrange("p n t -> p (n t)"))
+
+        def quant_d_quarter(g, q):
+            quant_d(g, 2 * q, 2 * q + 2)
 
         def second_pass(dst, i, g, n0, n1, start, stop):
             nc.tensor.matmul_mx(
@@ -250,246 +243,223 @@ def tile_sonar_ping_coherence_s13_kernel(tc, echo, steer_bytes, steer_scale, ref
                 stop=stop,
             )
 
-        def second_quarter(g, q, banks, bands=range(BANDS)):
-            for i in bands:
-                if g == 0 and i % 2 == 0:
-                    acc[(i // 2, q)] = bank(banks[i // 2])
-                dst = acc[(i // 2, q)][:, (i % 2) * QUART : (i % 2 + 1) * QUART]
-                second_pass(dst, i, g, q * QUART, (q + 1) * QUART, g == 0 and i % 2 == 0, g == G - 1 and i % 2 == 1)
+        def second_quarter(g, q, pairs=range(OPEN)):
+            for j in pairs:
+                if g == 0:
+                    pair_sum[(j, q)] = bank(sum_banks[j])
+                for e in range(2):
+                    dst = pair_sum[(j, q)][:, e * QUART : (e + 1) * QUART]
+                    second_pass(dst, 2 * j + e, g, q * QUART, (q + 1) * QUART, g == 0 and e == 0, g == G - 1 and e == 1)
 
         def finish_quarter(j, q):
             o = stage.tile([P, 2, QUART], F32, name="o", tag="o", align_bytes=256)
             for e in range(2):
                 i = 2 * j + e
-                nc.scalar.activation(out=o[:, e, :], in_=acc[(j, q)][:, e * QUART : (e + 1) * QUART], func=SQUARE, scale=rgain[:, i : i + 1])
+                nc.scalar.activation(out=o[:, e, :], in_=pair_sum[(j, q)][:, e * QUART : (e + 1) * QUART], func=SQUARE, scale=rgain[:, i : i + 1])
             nc.sync.dma_start(out=out[2 * j * P : (2 * j + 2) * P, q * QUART : (q + 1) * QUART].rearrange("(e p) n -> p e n", e=2), in_=o[:])
 
         def second(i, g, n0, n1, k):
             if g == 0:
-                acc[(i, n0, n1)] = bank(k)
-            second_pass(acc[(i, n0, n1)][:, 0 : n1 - n0], i, g, n0, n1, g == 0, g == G - 1)
+                band_sum[(i, n0)] = bank(k)
+            second_pass(band_sum[(i, n0)][:, 0 : n1 - n0], i, g, n0, n1, g == 0, g == G - 1)
 
-        def finish(i, n0, n1, piece=HALF, queue=nc.sync):
+        def finish(i, n0, n1, piece):
             for a in range(0, n1 - n0, piece):
-                w = min(piece, n1 - n0)
                 o = stage.tile([P, HALF], F32, name="o", tag="o", align_bytes=256)
-                nc.scalar.activation(out=o[:, 0:w], in_=acc[(i, n0, n1)][:, a : a + w], func=SQUARE, scale=rgain[:, i : i + 1])
-                queue.dma_start(out=out[i * P : (i + 1) * P, n0 + a : n0 + a + w], in_=o[:, 0:w])
-
-        def spread_gains(h, k):
-            gbank[h] = bank(k)
-            nc.tensor.matmul(out=gbank[h][:, 0:QUART].bitcast(BF16), lhsT=ones[:, 0:P], rhs=gains[:, h * HALF : (h + 1) * HALF], start=True, stop=True)
-
-        def keep_gains(n0, n1, on_vector):
-            copy = nc.vector.tensor_copy if on_vector else nc.scalar.copy
-            copy(out=cgain[:, n0:n1], in_=gbank[0][:, n0 // 2 : n1 // 2].bitcast(BF16))
-
-        def row_gains():
-            nc.tensor.matmul(out=gbank[0][:, QUART : QUART + BANDS], lhsT=gains[:, HALF : HALF + P], rhs=idb[:, 0:BANDS], start=True, stop=True)
-
-        def keep_row_gains(on_vector):
-            copy = nc.vector.tensor_copy if on_vector else nc.scalar.copy
-            copy(out=rgain[:], in_=gbank[0][:, QUART : QUART + BANDS])
-
-        def constants():
-            nc.scalar.dma_start(out=sscl[:], in_=steer_scale.rearrange("(c p t) o -> p c (t o)", p=P, t=4))
-            nc.vector.memset(table_warm[:, 0:1], 1.0)
-            nc.scalar.activation(out=table_warm[:, 1:2], in_=table_warm[:, 0:1], func=SQUARE)
-            nc.vector.memset(ones[:].bitcast(I32), TWO_ONES)
-            make_identity(nc, idf[:])
-            nc.vector.memset(gains[:].bitcast(I32), 0)
-            nc.vector.memset(pscl[:].rearrange("p g n -> p (g n)").bitcast(I32), 0)
-
-        def load_col_gain():
-            nc.scalar.dma_start(out=gains[0:1, 0:HALF], in_=col_gain[0:HALF].unsqueeze(0))
-
-        def small_identity():
-            nc.scalar.copy(out=idb[:], in_=idf[:, 0:BANDS])
-
-        def load_spread_gain():
-            nc.sync.dma_start(out=cgain[:, HALF:N], in_=col_gain[HALF:N].partition_broadcast(P))
-
-        def load_row_gain():
-            nc.scalar.dma_start(out=gains[0:BANDS, HALF : HALF + P], in_=row_gain.rearrange("(c m) -> c m", m=P))
+                nc.scalar.activation(out=o[:, 0:piece], in_=band_sum[(i, n0)][:, a : a + piece], func=SQUARE, scale=rgain[:, i : i + 1])
+                nc.sync.dma_start(out=out[i * P : (i + 1) * P, n0 + a : n0 + a + piece], in_=o[:, 0:piece])
 
         def warm(n, k, moving):
             scratch = bank(k)
             for j in range(n):
                 nc.tensor.matmul(out=scratch[:], lhsT=ones[:, 0:P], rhs=moving, start=True, stop=True)
 
+        nc.scalar.dma_start(out=sscl[:], in_=steer_scale.rearrange("(c p t) o -> p c (t o)", p=P, t=SLOTS))
+        nc.vector.memset(table_warm[:, 0:1], 1.0)
+        nc.scalar.activation(out=table_warm[:, 1:2], in_=table_warm[:, 0:1], func=SQUARE)
+        nc.vector.memset(ones[:].bitcast(I32), TWO_ONES)
+        make_identity(nc, idf[:])
+        nc.vector.memset(gains[:].bitcast(I32), 0)
+        nc.vector.memset(pscl[:].rearrange("p g n -> p (g n)").bitcast(I32), 0)
 
-        V, S = True, False
-        constants()
-        load_steer(0, 0, QUART)
-        load_steer(1, 0, QUART)
-        for t in range(4):
+        for c in range(CP):
+            load_steer(c, 0, QUART)
+        for t in range(SLOTS):
             load_echo(0, t, t + 1)
-        load_col_gain()
-        load_row_gain()
-        small_identity()
+        nc.scalar.dma_start(out=gains[0:1, 0:HALF], in_=col_gain[0:HALF].unsqueeze(0))
+        nc.scalar.dma_start(out=gains[0:BANDS, HALF : HALF + P], in_=row_gain.rearrange("(i m) -> i m", m=P))
+        nc.scalar.copy(out=idb[:], in_=idf[:, 0:BANDS])
         load_echo(1, 0, 2)
-        load_scales(0, 2)
         load_echo(1, 2, 3)
+        load_scales(0, 1)
         load_echo(1, 3, 4)
         load_words(0)
         load_echo(2, 0, 2)
         load_echo(2, 2, 4)
         load_steer(0, QUART, HALF)
         load_words(1)
-        load_scales(2, 4)
+        load_scales(1, 2)
         load_echo(3, 0, 2)
         load_steer(1, QUART, HALF)
         load_echo(3, 2, 4)
         load_words(2)
-        load_steer(0, HALF, N)
-        load_steer(1, HALF, N)
+        load_scales(2, G)
+        for c in range(CP):
+            load_steer(c, HALF, N)
         load_words(3)
-        load_spread_gain()
+        nc.sync.dma_start(out=cgain[:, HALF:N], in_=col_gain[HALF:N].partition_broadcast(P))
 
         warm(3, 7, ones[:, 0:HALF])
-        widen(0, 0, QUART, V)
+        widen(0, 0, QUART, VECTOR)
         warm(2, 7, swide[(0, 0)][0][:, 0:2, :].rearrange("p t n -> p (t n)"))
-        widen(1, 0, QUART, V, (0, 1))
-        widen(1, 0, QUART, S, (2, 3))
-        interleave(0, 0, QUART, V)
-        turn(0, 0, 0)
-        empty(0, 0)
-        interleave(1, 0, QUART, V)
-        turn(0, 1, 1)
-        empty(0, 1)
-        quant_steer(0, 0, QUART)
-        quant_steer(1, 0, QUART)
+        widen(1, 0, QUART, VECTOR, (0, 1))
+        widen(1, 0, QUART, SCALAR, (2, 3))
+        for t in range(2):
+            interleave(t, 0, QUART, VECTOR)
+            turn(0, t, t)
+            empty(0, t)
+        for c in range(CP):
+            quant_steer(c, 0, QUART)
         quant_echo(0, 0, 1)
         turn(0, 2, 2)
         empty(0, 2)
-        turn(0, 3, 3)
-        empty(0, 3)
-        spread_gains(0, 6)
-        row_gains()
+        turn(0, LAST_SLOT, 3)
+        empty_last(0)
+        gbank = bank(6)
+        nc.tensor.matmul(out=gbank[:, 0:QUART].bitcast(BF16), lhsT=ones[:, 0:P], rhs=gains[:, 0:HALF], start=True, stop=True)
+        nc.tensor.matmul(out=gbank[:, QUART : QUART + BANDS], lhsT=gains[:, HALF : HALF + P], rhs=idb[:], start=True, stop=True)
         quant_echo(0, 1, 2)
         quant_echo(0, 2, 3)
-        keep_gains(0, QUART, V)
-        quant_echo(0, 3, 4)
-        for t in range(4):
+        nc.vector.tensor_copy(out=cgain[:, 0:QUART], in_=gbank[:, 0:P].bitcast(BF16))
+        quant_echo_last(0)
+        for t in range(SLOTS):
             first_slot(0, 0, t, 4)
             first_slot(0, 1, t, 5)
-        sort_words(1, 0, S)
-        keep_gains(QUART, HALF, S)
-        keep_row_gains(S)
-        sort_words(1, 1, V)
-        ACC = (2, 3, 0, 1)
-        work = [4, 5, 0, 1]
+        sort_words(1, 0, SCALAR)
+        nc.scalar.copy(out=cgain[:, QUART:HALF], in_=gbank[:, P:QUART].bitcast(BF16))
+        nc.scalar.copy(out=rgain[:], in_=gbank[:, QUART : QUART + BANDS])
+        sort_words(1, 1, VECTOR)
+        sort_words(1, 2, SCALAR)
+
+        sum_banks = (2, 3, 0, 1)
+        work = [4, 5, 6, 7]
         MID = QUART + P
         for g in range(G):
             if g > 0:
-                second_quarter(g - 1, 0, ACC)
+                second_quarter(g - 1, 0)
                 if g < G - 1:
-                    for t in range(3):
-                        sort_words(g + 1, t, S)
-                first_both(g, 0, work[0], work[1])
+                    for t in range(SLOTS):
+                        sort_words(g + 1, t, VECTOR if t == LAST_SLOT else SCALAR)
+                first_both(g, work[0], work[1])
             gain(g, 0)
             gain(g, 1)
             quant_d(g, 0, 1)
             quant_d(g, 1, 2)
-            if g < G - 1:
-                for t in range(4):
-                    turn(g + 1, t, (0, 1, 6, 7)[t] if g == 0 else work[(t + 2) % 4])
+            if g == G - 1:
+                break
+            turn_banks = (0, 1, 6, 7) if g == 0 else work[2:] + work[:2]
+            for t in range(SLOTS):
+                turn(g + 1, t, turn_banks[t])
+                if t < LAST_SLOT:
                     empty(g + 1, t)
-                if g == 1:
-                    widen(0, QUART, HALF, V)
-                if g == 2:
-                    interleave(0, QUART, MID, V)
-                    interleave(1, QUART, MID, V)
-                quant_echo(g + 1, 0, 2)
-                quant_echo(g + 1, 2, 3)
-                quant_echo(g + 1, 3, 4)
-                if g == 1:
-                    widen(1, QUART, HALF, V)
-                if g == 2:
-                    quant_steer(0, QUART, MID)
-                    quant_steer(1, QUART, MID)
-                    interleave(0, MID, HALF, S)
-                    interleave(1, MID, HALF, S)
-                work = [4, 5, 6, 7] if g == 0 else work[2:] + work[:2]
-        widen(0, HALF, N, S)
+            empty_last(g + 1)
+            if g == 1:
+                widen(0, QUART, HALF, VECTOR)
+            if g == 2:
+                widen(1, QUART, HALF, VECTOR, (2, 3))
+                interleave(0, QUART, MID, VECTOR)
+            quant_echo(g + 1, 0, 2)
+            quant_echo(g + 1, 2, 3)
+            quant_echo_last(g + 1)
+            if g == 1:
+                widen(1, QUART, HALF, VECTOR, (0, 1))
+            if g == 2:
+                interleave(1, QUART, MID, VECTOR)
+                for c in range(CP):
+                    quant_steer(c, QUART, MID)
+                for c in range(CP):
+                    interleave(c, MID, HALF, SCALAR)
+            if g > 0:
+                work = work[2:] + work[:2]
+
+        widen(0, HALF, N, SCALAR)
         work = work[2:] + work[:2]
         for g in range(G - 1):
             first(g, 2, work[g])
-        second_quarter(G - 1, 0, ACC)
-        quant_steer(0, MID, HALF)
-        quant_steer(1, MID, HALF)
+        second_quarter(G - 1, 0)
+        for c in range(CP):
+            quant_steer(c, MID, HALF)
         for g in range(G - 1):
             gain(g, 2)
-        for j in range(4):
+        for j in range(OPEN):
             finish_quarter(j, 0)
-        widen(1, HALF, HALF + QUART, S)
-        widen(1, HALF + QUART, N, S)
+        widen(1, HALF, HALF + QUART, SCALAR)
+        widen(1, HALF + QUART, N, SCALAR)
         for c in range(CP):
-            interleave(c, HALF + QUART, N, S)
+            interleave(c, HALF + QUART, N, SCALAR)
         for g in range(G - 1):
             first(g, 3, work[(g + 3) % 4])
         first(G - 1, 2, work[2])
-        interleave(0, HALF, HALF + QUART, V)
+        interleave(0, HALF, HALF + QUART, VECTOR)
         gain(0, 3)
         first(G - 1, 3, work[3])
         gain(1, 3)
-        quant_d(0, 2, 4)
-        second_quarter(0, 1, ACC)
+        quant_d_quarter(0, 1)
+        second_quarter(0, 1)
         gain(2, 3)
-        quant_d(1, 2, 4)
-        interleave(1, HALF, HALF + QUART, V)
-        quant_steer(0, HALF, HALF + QUART)
-        quant_steer(1, HALF, HALF + QUART)
-        gain(3, 2)
-        second_quarter(1, 1, ACC)
-        gain(3, 3)
-        quant_d(2, 2, 4)
+        quant_d_quarter(1, 1)
+        interleave(1, HALF, HALF + QUART, VECTOR)
+        for c in range(CP):
+            quant_steer(c, HALF, HALF + QUART)
+        gain(G - 1, 2)
+        second_quarter(1, 1)
+        quant_d_quarter(2, 1)
+        gain(G - 1, 3)
 
-        held = [(i, g) for g in range(G - 1) for i in range(4)]
         steps = [(0, 2), (1, 2), (0, 3), (1, 3), (2, 2), (2, 3), (3, 2), (3, 3)]
+        held = [(i, g) for g in range(G - 1) for i in range(OPEN)]
         for step, (g, q) in enumerate(steps):
             ka, kb = work[2 * (step % 2)], work[2 * (step % 2) + 1]
-            if step == 2 * G - 1:
-                first(g, 6, ka)
-                first(g, 7, kb)
-                gain(g, 6)
-                gain(g, 7)
-                quant_d(g, 4, 6)
-                quant_d(g, 6, 7)
-                quant_d(g, 7, 8)
+            if step == len(steps) - 1:
+                first(g, 2 * q, ka)
+                first(g, 2 * q + 1, kb)
+                gain(g, 2 * q)
+                gain(g, 2 * q + 1)
+                quant_d_quarter(*steps[step - 1])
+                quant_d(g, 2 * q, 2 * q + 1)
+                quant_d(g, 2 * q + 1, 2 * q + 2)
             else:
                 first_two(g, q, 0, ka)
                 first_two(g, q, 1, kb)
                 gain_two(g, q, 0)
                 if step == 0:
-                    quant_d(G - 1, 2, 4)
+                    quant_d_quarter(G - 1, 1)
                 gain_two(g, q, 1)
                 if step == 0:
-                    quant_steer(0, HALF + QUART, N)
-                    quant_steer(1, HALF + QUART, N)
-                if step > 0:
-                    pg, pq = steps[step - 1]
-                    quant_d(pg, 2 * pq, 2 * pq + 2)
-                join(g, q, S)
+                    for c in range(CP):
+                        quant_steer(c, HALF + QUART, N)
+                else:
+                    quant_d_quarter(*steps[step - 1])
+                join(g, q)
             if step < 4:
-                j0 = 2 * (step % 2)
-                second_quarter(G - 2 + step // 2, 1, ACC, range(2 * j0, 2 * j0 + 4))
+                pairs = (2 * (step % 2), 2 * (step % 2) + 1)
+                second_quarter(G - 2 + step // 2, 1, pairs)
                 if step >= 2:
-                    finish_quarter(j0, 1)
-                    finish_quarter(j0 + 1, 1)
-            elif 3 < step < 2 * G - 1:
-                i, gg = held.pop(0)
-                second(i, gg, HALF, N, ACC[i])
-        for i, gg in held:
-            second(i, gg, HALF, N, ACC[i])
-        for i in range(4):
-            second(i, G - 1, HALF, N, ACC[i])
-            finish(i, HALF, N)
-        for i in (4, 5, 6):
+                    for j in pairs:
+                        finish_quarter(j, 1)
+            elif step < len(steps) - 1:
+                i, held_g = held.pop(0)
+                second(i, held_g, HALF, N, sum_banks[i])
+        for i, held_g in held:
+            second(i, held_g, HALF, N, sum_banks[i])
+        for i in range(OPEN):
+            second(i, G - 1, HALF, N, sum_banks[i])
+            finish(i, HALF, N, HALF)
+        for i in range(OPEN, BANDS - 1):
             for g in range(G):
-                second(i, g, HALF, N, work[i - 4])
-            finish(i, HALF, N, QUART if i == 6 else HALF)
-        for n0, n1, k in ((HALF, HALF + QUART, work[3]), (HALF + QUART, N - P, ACC[0]), (N - P, N, ACC[1])):
+                second(i, g, HALF, N, work[i - OPEN])
+            finish(i, HALF, N, QUART if i == BANDS - 2 else HALF)
+        for n0, n1, k in ((HALF, HALF + QUART, work[3]), (HALF + QUART, N - P, sum_banks[0]), (N - P, N, sum_banks[1])):
             for g in range(G):
-                second(7, g, n0, n1, k)
-            finish(7, n0, n1)
+                second(BANDS - 1, g, n0, n1, k)
+            finish(BANDS - 1, n0, n1, n1 - n0)

@@ -69,14 +69,14 @@ def tile_sonar_ping_coherence_s13_kernel(tc, echo, steer_bytes, steer_scale, ref
 
         echo_g = echo.rearrange("(g p t) k -> g p t k", p=P, t=SLOTS)
         steer_c = steer_bytes.rearrange("(c p t) n -> c p t n", p=P, t=SLOTS)
-        eraw, esort, xbank, egrp, epass, sraw, swide = {}, {}, {}, {}, {}, {}, {}
-        ybank, ytwo, dgrp, dtwo, pair_sum, band_sum = {}, {}, {}, {}, {}, {}
+        eraw, esort, xbank, egrp, sraw, swide = {}, {}, {}, {}, {}, {}
+        ybank, ytwo, dgrp, dtwo, dwide, pair_sum, band_sum = {}, {}, {}, {}, {}, {}, {}
 
-        def load_echo(g, t0, t1):
-            tile = kept([P, t1 - t0, C], BF16, "eraw%d_%d" % (g, t0))
-            nc.sync.dma_start(out=tile[:], in_=echo_g[g][:, t0:t1, :])
-            for t in range(t0, t1):
-                eraw[(g, t)] = tile[:, t - t0, :]
+        def load_echo(k0, k1):
+            tile = kept([P, k1 - k0, C], BF16, "eraw%d" % k0)
+            nc.sync.dma_start(out=tile[:], in_=echo_g[k0 // SLOTS][:, k0 % SLOTS : k0 % SLOTS + k1 - k0, :])
+            for k in range(k0, k1):
+                eraw[k] = tile[:, k - k0, :]
 
         def load_steer(c, n0, n1):
             tile = kept([P, SLOTS, n1 - n0], U8, "sraw%d_%d" % (c, n0))
@@ -118,46 +118,32 @@ def tile_sonar_ping_coherence_s13_kernel(tc, echo, steer_bytes, steer_scale, ref
         def quant_steer(c, n0, n1):
             nc.vector.quantize_mx(out=scod[c][:, n0:n1].bitcast(FP8X4), scales=sqsc[c][:, n0:n1], in_=sgrp[c][:, n0:n1, :].rearrange("p n t -> p (n t)"))
 
-        def sort_words(g, t, on_vector):
-            esort[(g, t)] = ring.tile([P, C // 2], F32, name="esort", tag="esort", align_bytes=256)
+        def sort_words(k, on_vector):
+            esort[k] = ring.tile([P, C // 2], F32, name="esort", tag="esort", align_bytes=256)
             copier(on_vector)(
-                out=esort[(g, t)][:].rearrange("p (c u m) -> p c u m", c=CP, u=2),
-                in_=eraw[(g, t)].bitcast(F32).rearrange("p (c m u) -> p c u m", c=CP, u=2),
+                out=esort[k][:].rearrange("p (c u m) -> p c u m", c=CP, u=2),
+                in_=eraw[k].bitcast(F32).rearrange("p (c m u) -> p c u m", c=CP, u=2),
             )
 
-        def turn(g, t, k):
-            xbank[(g, t)] = bank(k)
-            words = eraw[(g, t)].bitcast(F32)
+        def turn(k, kb):
+            xbank[k] = bank(kb)
+            words = eraw[k].bitcast(F32)
             for c in range(CP):
                 for u in range(2):
                     j = 2 * c + u
-                    src = esort[(g, t)][:, j * P : (j + 1) * P] if (g, t) in esort else words[:, 2 * P * c + u : 2 * P * (c + 1) : 2]
-                    nc.tensor.transpose(xbank[(g, t)][:, j * P : (j + 1) * P], src, idf[:])
+                    src = esort[k][:, j * P : (j + 1) * P] if k in esort else words[:, 2 * P * c + u : 2 * P * (c + 1) : 2]
+                    nc.tensor.transpose(xbank[k][:, j * P : (j + 1) * P], src, idf[:])
 
-        def empty(g, t):
-            shares = g > 0 and t == 1
-            egrp[(g, t)] = egrp[(g, 0)] if shares else ring.tile([P, 2, C], BF16, name="egrp", tag="egrp", align_bytes=256)
+        def empty(k):
+            egrp[k] = ring.tile([P, C], BF16, name="egrp", tag="egrp", align_bytes=256)
             nc.scalar.copy(
-                out=egrp[(g, t)][:, 1 if shares else 0, :].bitcast(F32).rearrange("p (c r u) -> p c r u", c=CP, u=2),
-                in_=xbank[(g, t)][:].rearrange("p (c u r) -> p c r u", c=CP, u=2),
+                out=egrp[k][:].bitcast(F32).rearrange("p (c r u) -> p c r u", c=CP, u=2),
+                in_=xbank[k][:].rearrange("p (c u r) -> p c r u", c=CP, u=2),
             )
 
-        def quant_echo(g, t0, t1):
-            cols = slice(t0 * CP * P, t1 * CP * P)
-            nc.vector.quantize_mx(out=ecod[g][:, cols].bitcast(FP8X4), scales=escl[g][:, cols], in_=egrp[(g, t0)][:, 0 : t1 - t0, :].rearrange("p t k -> p (t k)"))
-
-        def empty_last(g):
-            for c in range(CP):
-                epass[(g, c)] = ring.tile([P, HALF], BF16, name="epass", tag="epass", align_bytes=256)
-                nc.scalar.copy(
-                    out=epass[(g, c)][:].bitcast(F32).rearrange("p (r u) -> p r u", u=2),
-                    in_=xbank[(g, LAST_SLOT)][:, 2 * P * c : 2 * P * (c + 1)].rearrange("p (u r) -> p r u", u=2),
-                )
-
-        def quant_echo_last(g):
-            for c in range(CP):
-                cols = slice((LAST_SLOT * CP + c) * P, (LAST_SLOT * CP + c + 1) * P)
-                nc.vector.quantize_mx(out=ecod[g][:, cols].bitcast(FP8X4), scales=escl[g][:, cols], in_=epass[(g, c)][:])
+        def quant_echo(k):
+            cols = slice(k % SLOTS * CP * P, (k % SLOTS + 1) * CP * P)
+            nc.vector.quantize_mx(out=ecod[k // SLOTS][:, cols].bitcast(FP8X4), scales=escl[k // SLOTS][:, cols], in_=egrp[k][:])
 
         def first_sum(dst, g, t, n0, n1):
             for c in range(CP):
@@ -180,14 +166,6 @@ def tile_sonar_ping_coherence_s13_kernel(tc, echo, steer_bytes, steer_scale, ref
         def first(g, b, k):
             for t in range(SLOTS):
                 first_slot(g, b, t, k)
-
-        def first_both(g, k0, k1):
-            for t in range(LAST_SLOT):
-                first_slot(g, 0, t, k0)
-            first_slot(g, 1, 0, k1)
-            first_slot(g, 0, LAST_SLOT, k0)
-            for t in range(1, SLOTS):
-                first_slot(g, 1, t, k1)
 
         def d_tile(g, q):
             if (g, q) not in dgrp:
@@ -222,6 +200,21 @@ def tile_sonar_ping_coherence_s13_kernel(tc, echo, steer_bytes, steer_scale, ref
             nc.scalar.copy(
                 out=d_tile(g, q)[:].rearrange("p n t -> p (n t)").bitcast(F32).rearrange("p (n u) -> p n u", u=2),
                 in_=dtwo[(g, q)][:].rearrange("p u n e -> p (u n e)").bitcast(F32).rearrange("p (u n) -> p n u", u=2),
+            )
+
+        def first_wide(g, t, k):
+            ybank[(g, t, HALF)] = bank(k)
+            first_sum(ybank[(g, t, HALF)][:], g, t, HALF, N)
+
+        def gain_wide(g, t):
+            if t == 0:
+                dwide[g] = ring.tile([P, SLOTS, HALF], BF16, name="dwide", tag="dwide", align_bytes=256, bufs=2)
+            nc.vector.tensor_tensor(out=dwide[g][:, t, :], in0=ybank[(g, t, HALF)][:], in1=cgain[:, HALF:N], op=MULT)
+
+        def weave(g, q):
+            nc.scalar.copy(
+                out=d_tile(g, q)[:].rearrange("p (n i) t -> p n t i", i=4),
+                in_=dwide[g][:, :, q * QUART - HALF : (q + 1) * QUART - HALF].rearrange("p t (n i) -> p n t i", i=4),
             )
 
         def quant_d(g, b0, b1):
@@ -284,26 +277,22 @@ def tile_sonar_ping_coherence_s13_kernel(tc, echo, steer_bytes, steer_scale, ref
 
         for c in range(CP):
             load_steer(c, 0, QUART)
-        for t in range(SLOTS):
-            load_echo(0, t, t + 1)
+        for k in range(4):
+            load_echo(k, k + 1)
         nc.scalar.dma_start(out=gains[0:1, 0:HALF], in_=col_gain[0:HALF].unsqueeze(0))
         nc.scalar.dma_start(out=gains[0:BANDS, HALF : HALF + P], in_=row_gain.rearrange("(i m) -> i m", m=P))
         nc.scalar.copy(out=idb[:], in_=idf[:, 0:BANDS])
-        load_echo(1, 0, 2)
-        load_echo(1, 2, 3)
-        load_scales(0, 1)
-        load_echo(1, 3, 4)
-        load_words(0)
-        load_echo(2, 0, 2)
-        load_echo(2, 2, 4)
+        for k in range(4, 6):
+            load_echo(k, k + 1)
         load_steer(0, QUART, HALF)
-        load_words(1)
-        load_scales(1, 2)
-        load_echo(3, 0, 2)
+        for k in range(6, 16, 2):
+            load_echo(k, k + 2)
+        load_scales(0, 2)
+        load_words(0)
         load_steer(1, QUART, HALF)
-        load_echo(3, 2, 4)
-        load_words(2)
+        load_words(1)
         load_scales(2, G)
+        load_words(2)
         for c in range(CP):
             load_steer(c, HALF, N)
         load_words(3)
@@ -314,107 +303,127 @@ def tile_sonar_ping_coherence_s13_kernel(tc, echo, steer_bytes, steer_scale, ref
         warm(2, 7, swide[(0, 0)][0][:, 0:2, :].rearrange("p t n -> p (t n)"))
         widen(1, 0, QUART, VECTOR, (0, 1))
         widen(1, 0, QUART, SCALAR, (2, 3))
-        for t in range(2):
-            interleave(t, 0, QUART, VECTOR)
-            turn(0, t, t)
-            empty(0, t)
+        for c in range(CP):
+            interleave(c, 0, QUART, VECTOR)
         for c in range(CP):
             quant_steer(c, 0, QUART)
-        quant_echo(0, 0, 1)
-        turn(0, 2, 2)
-        empty(0, 2)
-        turn(0, LAST_SLOT, 3)
-        empty_last(0)
         gbank = bank(6)
-        nc.tensor.matmul(out=gbank[:, 0:QUART].bitcast(BF16), lhsT=ones[:, 0:P], rhs=gains[:, 0:HALF], start=True, stop=True)
-        nc.tensor.matmul(out=gbank[:, QUART : QUART + BANDS], lhsT=gains[:, HALF : HALF + P], rhs=idb[:], start=True, stop=True)
-        quant_echo(0, 1, 2)
-        quant_echo(0, 2, 3)
-        nc.vector.tensor_copy(out=cgain[:, 0:QUART], in_=gbank[:, 0:P].bitcast(BF16))
-        quant_echo_last(0)
-        for t in range(SLOTS):
-            first_slot(0, 0, t, 4)
-            first_slot(0, 1, t, 5)
-        sort_words(1, 0, SCALAR)
-        nc.scalar.copy(out=cgain[:, QUART:HALF], in_=gbank[:, P:QUART].bitcast(BF16))
+        for k in range(6):
+            turn(k, k)
+            empty(k)
+            if k < SLOTS:
+                quant_echo(k)
+            if k == 3:
+                nc.tensor.matmul(out=gbank[:, 0:QUART].bitcast(BF16), lhsT=ones[:, 0:P], rhs=gains[:, 0:HALF], start=True, stop=True)
+                nc.tensor.matmul(out=gbank[:, QUART : QUART + BANDS], lhsT=gains[:, HALF : HALF + P], rhs=idb[:], start=True, stop=True)
+                nc.vector.tensor_copy(out=cgain[:, 0:HALF], in_=gbank[:, 0:QUART].bitcast(BF16))
         nc.scalar.copy(out=rgain[:], in_=gbank[:, QUART : QUART + BANDS])
-        sort_words(1, 1, VECTOR)
-        sort_words(1, 2, SCALAR)
+        def first_pair(g, q, ka, kb):
+            for t in range(LAST_SLOT):
+                first_slot(g, 2 * q, t, ka)
+            first_slot(g, 2 * q + 1, 0, kb)
+            first_slot(g, 2 * q, LAST_SLOT, ka)
+            for t in range(1, SLOTS):
+                first_slot(g, 2 * q + 1, t, kb)
 
-        sum_banks = (2, 3, 0, 1)
-        work = [4, 5, 6, 7]
-        MID = QUART + P
-        for g in range(G):
-            if g > 0:
-                second_quarter(g - 1, 0)
-                if g < G - 1:
-                    for t in range(SLOTS):
-                        sort_words(g + 1, t, VECTOR if t == LAST_SLOT else SCALAR)
-                first_both(g, work[0], work[1])
-            gain(g, 0)
-            gain(g, 1)
-            quant_d(g, 0, 1)
-            quant_d(g, 1, 2)
-            if g == G - 1:
-                break
-            turn_banks = (0, 1, 6, 7) if g == 0 else work[2:] + work[:2]
+        def step(g, q, ka, kb):
+            first_two(g, q, 0, ka)
+            first_two(g, q, 1, kb)
+
+        def gains_two(g, q):
+            gain_two(g, q, 0)
+            gain_two(g, q, 1)
+
+        def first_by_slot(g, q, ka, kb):
             for t in range(SLOTS):
-                turn(g + 1, t, turn_banks[t])
-                if t < LAST_SLOT:
-                    empty(g + 1, t)
-            empty_last(g + 1)
-            if g == 1:
-                widen(0, QUART, HALF, VECTOR)
-            if g == 2:
-                widen(1, QUART, HALF, VECTOR, (2, 3))
-                interleave(0, QUART, MID, VECTOR)
-            quant_echo(g + 1, 0, 2)
-            quant_echo(g + 1, 2, 3)
-            quant_echo_last(g + 1)
-            if g == 1:
-                widen(1, QUART, HALF, VECTOR, (0, 1))
-            if g == 2:
-                interleave(1, QUART, MID, VECTOR)
-                for c in range(CP):
-                    quant_steer(c, QUART, MID)
-                for c in range(CP):
-                    interleave(c, MID, HALF, SCALAR)
-            if g > 0:
-                work = work[2:] + work[:2]
+                first_slot(g, 2 * q, t, ka)
+                first_slot(g, 2 * q + 1, t, kb)
 
+        first_pair(0, 0, 7, 0)
+        quant_echo(4)
+        gain(0, 0)
+        gain(0, 1)
+        widen(0, QUART, HALF, SCALAR)
+        for k in range(6, 10):
+            turn(k, k - 5)
+            empty(k)
+        quant_echo(5)
+        quant_d_quarter(0, 0)
+        sort_words(10, VECTOR)
+        quant_echo(6)
+        quant_echo(7)
+        first_by_slot(1, 0, 5, 6)
+        sort_words(11, VECTOR)
+        sort_words(12, VECTOR)
+        quant_echo(8)
+        sort_words(13, SCALAR)
+        sort_words(15, SCALAR)
+        quant_echo(9)
+        sort_words(14, VECTOR)
+        gain(1, 0)
+        gain(1, 1)
+        sum_banks = (5, 6, 7, 0)
+        work = (1, 2, 3, 4)
+        for k, kb in zip(range(10, 16), (7, 0) + work):
+            turn(k, kb)
+            empty(k)
+        second_quarter(0, 0)
+        quant_echo(10)
+        quant_d_quarter(1, 0)
+        quant_echo(11)
+        interleave(0, QUART, HALF, VECTOR)
+        first_pair(2, 0, work[0], work[1])
+        widen(1, QUART, HALF, VECTOR)
+        quant_echo(12)
+        gain(2, 0)
+        quant_echo(13)
+        gain(2, 1)
+        quant_echo(14)
+        quant_echo(15)
+        second_quarter(1, 0)
+        interleave(1, QUART, HALF, SCALAR)
         widen(0, HALF, N, SCALAR)
-        work = work[2:] + work[:2]
-        for g in range(G - 1):
-            first(g, 2, work[g])
-        second_quarter(G - 1, 0)
-        for c in range(CP):
-            quant_steer(c, MID, HALF)
-        for g in range(G - 1):
-            gain(g, 2)
-        for j in range(OPEN):
-            finish_quarter(j, 0)
-        widen(1, HALF, HALF + QUART, SCALAR)
-        widen(1, HALF + QUART, N, SCALAR)
-        for c in range(CP):
-            interleave(c, HALF + QUART, N, SCALAR)
-        for g in range(G - 1):
-            first(g, 3, work[(g + 3) % 4])
-        first(G - 1, 2, work[2])
-        interleave(0, HALF, HALF + QUART, VECTOR)
-        gain(0, 3)
-        first(G - 1, 3, work[3])
-        gain(1, 3)
-        quant_d_quarter(0, 1)
-        second_quarter(0, 1)
-        gain(2, 3)
-        quant_d_quarter(1, 1)
+        widen(1, HALF, N, SCALAR)
+        first_by_slot(3, 0, work[2], work[3])
+        quant_d_quarter(2, 0)
+        second_quarter(2, 0)
+        quant_steer(0, QUART, HALF)
+        quant_steer(1, QUART, HALF)
+        gain(3, 0)
+        gain(3, 1)
+
+        step(0, 1, work[0], work[1])
+        interleave(0, HALF, HALF + P, VECTOR)
+        quant_d_quarter(3, 0)
+        second_quarter(3, 0)
+        gains_two(0, 1)
+        step(1, 1, work[2], work[3])
+        interleave(0, HALF + P, HALF + QUART, VECTOR)
         interleave(1, HALF, HALF + QUART, VECTOR)
+        finish_quarter(0, 0)
+        finish_quarter(1, 0)
+        join(0, 1)
+        step(2, 1, work[0], work[1])
+        gains_two(1, 1)
+        finish_quarter(2, 0)
+        finish_quarter(3, 0)
+        join(1, 1)
+        step(3, 1, work[2], work[3])
+        gain_two(2, 1, 0)
+        quant_d_quarter(0, 1)
+        gain_two(2, 1, 1)
+        join(2, 1)
+        second_quarter(0, 1)
+        gain_two(3, 1, 0)
+        quant_d_quarter(1, 1)
+        second_quarter(1, 1)
+        gain_two(3, 1, 1)
         for c in range(CP):
             quant_steer(c, HALF, HALF + QUART)
-        gain(G - 1, 2)
-        second_quarter(1, 1)
+        interleave(0, HALF + QUART, N, SCALAR)
         quant_d_quarter(2, 1)
-        gain(G - 1, 3)
+        join(3, 1)
+        interleave(1, HALF + QUART, N, SCALAR)
 
         steps = [(0, 2), (1, 2), (0, 3), (1, 3), (2, 2), (2, 3), (3, 2), (3, 3)]
         held = [(i, g) for g in range(G - 1) for i in range(OPEN)]

@@ -59,12 +59,12 @@ def tile_sonar_ping_coherence_s13_kernel(tc, echo, steer_bytes, steer_scale, ref
         dscl = [kept([P, N], U8, "dscl%d" % g) for g in range(G)]
         pcod = [kept([P, 2 * R], U8, "pcod%d" % g) for g in range(G)]
         pscl = kept([P, G, R], U8, "pscl")
-        gains = kept([P, HALF + P + 2], BF16, "gains")
+        gains = kept([P, N + P + 2], BF16, "gains")
         ones = kept([P, HALF + 2], BF16, "ones")
         idf = kept([P, P], F32, "idf")
         idb = kept([P, BANDS], BF16, "idb")
         cgain = kept([P, N], BF16, "cgain")
-        table_warm = kept([P, 2], F32, "table_warm")
+        table_warm = kept([P, 1], F32, "table_warm")
         rgain = kept([P, BANDS], F32, "rgain")
 
         echo_g = echo.rearrange("(g p t) k -> g p t k", p=P, t=SLOTS)
@@ -265,42 +265,39 @@ def tile_sonar_ping_coherence_s13_kernel(tc, echo, steer_bytes, steer_scale, ref
         def warm(n, k, moving):
             scratch = bank(k)
             for j in range(n):
-                nc.tensor.matmul(out=scratch[:], lhsT=ones[:, 0:P], rhs=moving, start=True, stop=True)
+                nc.tensor.matmul(out=scratch[:, 0 : moving.shape[1]], lhsT=ones[:, 0:P], rhs=moving, start=True, stop=True)
 
         nc.scalar.dma_start(out=sscl[:], in_=steer_scale.rearrange("(c p t) o -> p c (t o)", p=P, t=SLOTS))
-        nc.vector.memset(table_warm[:, 0:1], 1.0)
-        nc.scalar.activation(out=table_warm[:, 1:2], in_=table_warm[:, 0:1], func=SQUARE)
         nc.vector.memset(ones[:].bitcast(I32), TWO_ONES)
+        nc.gpsimd.memset(gains[:].bitcast(I32), 0)
+        nc.scalar.activation(out=table_warm[:], in_=ones[:, 0:1], func=SQUARE)
         make_identity(nc, idf[:])
-        nc.vector.memset(gains[:].bitcast(I32), 0)
         nc.vector.memset(pscl[:].rearrange("p g n -> p (g n)").bitcast(I32), 0)
 
         for c in range(CP):
             load_steer(c, 0, QUART)
         for k in range(4):
             load_echo(k, k + 1)
-        nc.scalar.dma_start(out=gains[0:1, 0:HALF], in_=col_gain[0:HALF].unsqueeze(0))
-        nc.scalar.dma_start(out=gains[0:BANDS, HALF : HALF + P], in_=row_gain.rearrange("(i m) -> i m", m=P))
+            if k == 1:
+                nc.sync.dma_start(out=gains[0:1, 0:N], in_=col_gain.unsqueeze(0))
+        nc.scalar.dma_start(out=gains[0:BANDS, N : N + P], in_=row_gain.rearrange("(i m) -> i m", m=P))
         nc.scalar.copy(out=idb[:], in_=idf[:, 0:BANDS])
-        for k in range(4, 6):
+        for k in range(4, 16):
             load_echo(k, k + 1)
-        load_steer(0, QUART, HALF)
-        for k in range(6, 16, 2):
-            load_echo(k, k + 2)
         load_scales(0, 2)
         load_words(0)
-        load_steer(1, QUART, HALF)
+        for c in range(CP):
+            load_steer(c, QUART, HALF)
         load_words(1)
         load_scales(2, G)
         load_words(2)
         for c in range(CP):
             load_steer(c, HALF, N)
         load_words(3)
-        nc.sync.dma_start(out=cgain[:, HALF:N], in_=col_gain[HALF:N].partition_broadcast(P))
 
         warm(3, 7, ones[:, 0:HALF])
         widen(0, 0, QUART, VECTOR)
-        warm(2, 7, swide[(0, 0)][0][:, 0:2, :].rearrange("p t n -> p (t n)"))
+        warm(1, 7, swide[(0, 0)][0][:, 0:2, :].rearrange("p t n -> p (t n)"))
         widen(1, 0, QUART, VECTOR, (0, 1))
         widen(1, 0, QUART, SCALAR, (2, 3))
         for c in range(CP):
@@ -311,13 +308,18 @@ def tile_sonar_ping_coherence_s13_kernel(tc, echo, steer_bytes, steer_scale, ref
         for k in range(6):
             turn(k, k)
             empty(k)
+            if k == 0:
+                warm(1, 7, ones[:, 0:HALF])
+            elif k <= SLOTS:
+                q = k - 1
+                nc.tensor.matmul(out=gbank[:, q * P : (q + 1) * P].bitcast(BF16), lhsT=ones[:, 0:P], rhs=gains[:, q * QUART : (q + 1) * QUART], start=True, stop=True)
+            if k == SLOTS - 1:
+                sort_words(6, VECTOR)
             if k < SLOTS:
                 quant_echo(k)
-            if k == 3:
-                nc.tensor.matmul(out=gbank[:, 0:QUART].bitcast(BF16), lhsT=ones[:, 0:P], rhs=gains[:, 0:HALF], start=True, stop=True)
-                nc.tensor.matmul(out=gbank[:, QUART : QUART + BANDS], lhsT=gains[:, HALF : HALF + P], rhs=idb[:], start=True, stop=True)
-                nc.vector.tensor_copy(out=cgain[:, 0:HALF], in_=gbank[:, 0:QUART].bitcast(BF16))
-        nc.scalar.copy(out=rgain[:], in_=gbank[:, QUART : QUART + BANDS])
+        nc.vector.tensor_copy(out=cgain[:, 0:HALF], in_=gbank[:, 0:QUART].bitcast(BF16))
+        nc.scalar.copy(out=cgain[:, HALF:N], in_=gbank[:, QUART:HALF].bitcast(BF16))
+        sort_words(7, VECTOR)
         def first_pair(g, q, ka, kb):
             for t in range(LAST_SLOT):
                 first_slot(g, 2 * q, t, ka)
@@ -341,72 +343,74 @@ def tile_sonar_ping_coherence_s13_kernel(tc, echo, steer_bytes, steer_scale, ref
 
         first_pair(0, 0, 7, 0)
         quant_echo(4)
+        sort_words(8, SCALAR)
+        sort_words(9, SCALAR)
         gain(0, 0)
         gain(0, 1)
-        widen(0, QUART, HALF, SCALAR)
-        for k in range(6, 10):
+        sort_words(10, VECTOR)
+        for k in range(6, 11):
             turn(k, k - 5)
             empty(k)
+            if k == 8:
+                warm(1, 6, ones[:, 0:QUART])
+                rbank = bank(6)
+                nc.tensor.matmul(out=rbank[:, 0:BANDS], lhsT=gains[:, N : N + P], rhs=idb[:], start=True, stop=True)
         quant_echo(5)
         quant_d_quarter(0, 0)
-        sort_words(10, VECTOR)
         quant_echo(6)
+        nc.vector.tensor_copy(out=rgain[:], in_=rbank[:, 0:BANDS])
         quant_echo(7)
-        first_by_slot(1, 0, 5, 6)
-        sort_words(11, VECTOR)
-        sort_words(12, VECTOR)
-        quant_echo(8)
-        sort_words(13, SCALAR)
-        sort_words(15, SCALAR)
-        quant_echo(9)
-        sort_words(14, VECTOR)
+        first_by_slot(1, 0, 7, 0)
+        for k in range(11, 14):
+            sort_words(k, VECTOR)
+        sort_words(14, SCALAR)
         gain(1, 0)
-        gain(1, 1)
-        sum_banks = (5, 6, 7, 0)
-        work = (1, 2, 3, 4)
-        for k, kb in zip(range(10, 16), (7, 0) + work):
-            turn(k, kb)
+        sort_words(15, VECTOR)
+        sum_banks = (1, 2, 3, 0)
+        work = (6, 7, 4, 5)
+        for k in range(11, 16):
+            turn(k, k - 10)
             empty(k)
-        second_quarter(0, 0)
-        quant_echo(10)
-        quant_d_quarter(1, 0)
-        quant_echo(11)
-        interleave(0, QUART, HALF, VECTOR)
+            if k == 13:
+                warm(1, 6, ones[:, 0:QUART])
+        for k in range(8, 12):
+            quant_echo(k)
+        gain(1, 1)
         first_pair(2, 0, work[0], work[1])
-        widen(1, QUART, HALF, VECTOR)
+        second_quarter(0, 0)
         quant_echo(12)
-        gain(2, 0)
         quant_echo(13)
-        gain(2, 1)
+        quant_d_quarter(1, 0)
+        gain(2, 0)
         quant_echo(14)
         quant_echo(15)
-        second_quarter(1, 0)
-        interleave(1, QUART, HALF, SCALAR)
+        gain(2, 1)
+        first_pair(3, 0, work[2], work[3])
+        widen(0, QUART, HALF, SCALAR)
+        widen(1, QUART, HALF, SCALAR)
         widen(0, HALF, N, SCALAR)
-        widen(1, HALF, N, SCALAR)
-        first_by_slot(3, 0, work[2], work[3])
+        second_quarter(1, 0)
+        interleave(0, QUART, HALF, VECTOR)
         quant_d_quarter(2, 0)
         second_quarter(2, 0)
-        quant_steer(0, QUART, HALF)
-        quant_steer(1, QUART, HALF)
         gain(3, 0)
         gain(3, 1)
-
-        step(0, 1, work[0], work[1])
-        interleave(0, HALF, HALF + P, VECTOR)
+        quant_steer(0, QUART, HALF)
         quant_d_quarter(3, 0)
         second_quarter(3, 0)
-        gains_two(0, 1)
+        interleave(1, QUART, HALF, VECTOR)
+        for j in range(OPEN):
+            finish_quarter(j, 0)
+        quant_steer(1, QUART, HALF)
+
+        step(0, 1, work[0], work[1])
         step(1, 1, work[2], work[3])
-        interleave(0, HALF + P, HALF + QUART, VECTOR)
-        interleave(1, HALF, HALF + QUART, VECTOR)
-        finish_quarter(0, 0)
-        finish_quarter(1, 0)
+        interleave(0, HALF, N, VECTOR)
+        gains_two(0, 1)
         join(0, 1)
         step(2, 1, work[0], work[1])
         gains_two(1, 1)
-        finish_quarter(2, 0)
-        finish_quarter(3, 0)
+        widen(1, HALF, HALF + QUART, SCALAR)
         join(1, 1)
         step(3, 1, work[2], work[3])
         gain_two(2, 1, 0)
@@ -417,13 +421,14 @@ def tile_sonar_ping_coherence_s13_kernel(tc, echo, steer_bytes, steer_scale, ref
         gain_two(3, 1, 0)
         quant_d_quarter(1, 1)
         second_quarter(1, 1)
+        interleave(1, HALF, HALF + QUART, VECTOR)
+        quant_steer(0, HALF, HALF + QUART)
+        quant_steer(1, HALF, HALF + QUART)
         gain_two(3, 1, 1)
-        for c in range(CP):
-            quant_steer(c, HALF, HALF + QUART)
-        interleave(0, HALF + QUART, N, SCALAR)
+        widen(1, HALF + QUART, N, SCALAR)
         quant_d_quarter(2, 1)
-        join(3, 1)
         interleave(1, HALF + QUART, N, SCALAR)
+        join(3, 1)
 
         steps = [(0, 2), (1, 2), (0, 3), (1, 3), (2, 2), (2, 3), (3, 2), (3, 3)]
         held = [(i, g) for g in range(G - 1) for i in range(OPEN)]

@@ -59,7 +59,7 @@ def tile_sonar_ping_coherence_s13_kernel(tc, echo, steer_bytes, steer_scale, ref
         dscl = [kept([P, N], U8, "dscl%d" % g) for g in range(G)]
         pcod = [kept([P, 2 * R], U8, "pcod%d" % g) for g in range(G)]
         pscl = kept([P, G, R], U8, "pscl")
-        gains = kept([P, N + P + 2], BF16, "gains")
+        gains = kept([P, HALF + P + 2], BF16, "gains")
         ones = kept([P, HALF + 2], BF16, "ones")
         idf = kept([P, P], F32, "idf")
         idb = kept([P, BANDS], BF16, "idb")
@@ -279,25 +279,28 @@ def tile_sonar_ping_coherence_s13_kernel(tc, echo, steer_bytes, steer_scale, ref
         for k in range(4):
             load_echo(k, k + 1)
             if k == 1:
-                nc.sync.dma_start(out=gains[0:1, 0:N], in_=col_gain.unsqueeze(0))
-        nc.scalar.dma_start(out=gains[0:BANDS, N : N + P], in_=row_gain.rearrange("(i m) -> i m", m=P))
+                nc.sync.dma_start(out=gains[0:1, 0:HALF], in_=col_gain[0:HALF].unsqueeze(0))
+        nc.scalar.dma_start(out=gains[0:BANDS, HALF : HALF + P], in_=row_gain.rearrange("(i m) -> i m", m=P))
         nc.scalar.copy(out=idb[:], in_=idf[:, 0:BANDS])
-        for k in range(4, 16):
-            load_echo(k, k + 1)
-        load_scales(0, 2)
+        for k in range(4, 10, 2):
+            load_echo(k, k + 2)
         load_words(0)
+        load_scales(0, 1)
+        for k in range(10, 16, 2):
+            load_echo(k, k + 2)
         for c in range(CP):
             load_steer(c, QUART, HALF)
+        load_scales(1, G)
         load_words(1)
-        load_scales(2, G)
         load_words(2)
         for c in range(CP):
             load_steer(c, HALF, N)
         load_words(3)
+        nc.sync.dma_start(out=cgain[:, HALF:N], in_=col_gain[HALF:N].partition_broadcast(P))
 
         warm(3, 7, ones[:, 0:HALF])
         widen(0, 0, QUART, VECTOR)
-        warm(1, 7, swide[(0, 0)][0][:, 0:2, :].rearrange("p t n -> p (t n)"))
+        warm(2, 7, swide[(0, 0)][0][:, 0:2, :].rearrange("p t n -> p (t n)"))
         widen(1, 0, QUART, VECTOR, (0, 1))
         widen(1, 0, QUART, SCALAR, (2, 3))
         for c in range(CP):
@@ -305,21 +308,15 @@ def tile_sonar_ping_coherence_s13_kernel(tc, echo, steer_bytes, steer_scale, ref
         for c in range(CP):
             quant_steer(c, 0, QUART)
         gbank = bank(6)
-        for k in range(6):
+        for k in range(SLOTS):
             turn(k, k)
             empty(k)
-            if k == 0:
-                warm(1, 7, ones[:, 0:HALF])
-            elif k <= SLOTS:
+            if 0 < k < LAST_SLOT:
                 q = k - 1
                 nc.tensor.matmul(out=gbank[:, q * P : (q + 1) * P].bitcast(BF16), lhsT=ones[:, 0:P], rhs=gains[:, q * QUART : (q + 1) * QUART], start=True, stop=True)
-            if k == SLOTS - 1:
-                sort_words(6, VECTOR)
-            if k < SLOTS:
-                quant_echo(k)
-        nc.vector.tensor_copy(out=cgain[:, 0:HALF], in_=gbank[:, 0:QUART].bitcast(BF16))
-        nc.scalar.copy(out=cgain[:, HALF:N], in_=gbank[:, QUART:HALF].bitcast(BF16))
-        sort_words(7, VECTOR)
+            quant_echo(k)
+            if k == 2:
+                nc.vector.tensor_copy(out=cgain[:, 0:HALF], in_=gbank[:, 0:QUART].bitcast(BF16))
         def first_pair(g, q, ka, kb):
             for t in range(LAST_SLOT):
                 first_slot(g, 2 * q, t, ka)
@@ -336,99 +333,119 @@ def tile_sonar_ping_coherence_s13_kernel(tc, echo, steer_bytes, steer_scale, ref
             gain_two(g, q, 0)
             gain_two(g, q, 1)
 
+        def first_late(g, q, ka, kb):
+            for t in range(2):
+                first_slot(g, 2 * q, t, ka)
+                first_slot(g, 2 * q + 1, t, kb)
+            for b, k in ((2 * q, ka), (2 * q + 1, kb)):
+                for t in range(2, SLOTS):
+                    first_slot(g, b, t, k)
+
         def first_by_slot(g, q, ka, kb):
             for t in range(SLOTS):
                 first_slot(g, 2 * q, t, ka)
                 first_slot(g, 2 * q + 1, t, kb)
 
-        first_pair(0, 0, 7, 0)
-        quant_echo(4)
-        sort_words(8, SCALAR)
-        sort_words(9, SCALAR)
-        gain(0, 0)
-        gain(0, 1)
-        sort_words(10, VECTOR)
-        for k in range(6, 11):
-            turn(k, k - 5)
+        for t in range(2):
+            first_slot(0, 0, t, 4)
+            first_slot(0, 1, t, 5)
+        for k in range(4, 6):
+            turn(k, k - 4)
             empty(k)
-            if k == 8:
-                warm(1, 6, ones[:, 0:QUART])
-                rbank = bank(6)
-                nc.tensor.matmul(out=rbank[:, 0:BANDS], lhsT=gains[:, N : N + P], rhs=idb[:], start=True, stop=True)
-        quant_echo(5)
-        quant_d_quarter(0, 0)
-        quant_echo(6)
+        rbank = bank(7)
+        nc.tensor.matmul(out=rbank[:, 0:BANDS], lhsT=gains[:, HALF : HALF + P], rhs=idb[:], start=True, stop=True)
+        for b in range(2):
+            for t in range(2, SLOTS):
+                first_slot(0, b, t, 4 + b)
+        sort_words(6, VECTOR)
+        sort_words(7, VECTOR)
         nc.vector.tensor_copy(out=rgain[:], in_=rbank[:, 0:BANDS])
-        quant_echo(7)
-        first_by_slot(1, 0, 7, 0)
-        for k in range(11, 14):
-            sort_words(k, VECTOR)
-        sort_words(14, SCALAR)
-        gain(1, 0)
-        sort_words(15, VECTOR)
-        sum_banks = (1, 2, 3, 0)
-        work = (6, 7, 4, 5)
-        for k in range(11, 16):
-            turn(k, k - 10)
+        quant_echo(4)
+        gain(0, 0)
+        quant_echo(5)
+        gain(0, 1)
+        for k, kb in zip(range(6, 10), (2, 3, 7, 0)):
+            turn(k, kb)
             empty(k)
-            if k == 13:
-                warm(1, 6, ones[:, 0:QUART])
-        for k in range(8, 12):
-            quant_echo(k)
+        quant_echo(6)
+        quant_d_quarter(0, 0)
+        quant_echo(7)
+        first_by_slot(1, 0, 6, 1)
+        sort_words(10, VECTOR)
+        sort_words(11, SCALAR)
+        quant_echo(8)
+        gain(1, 0)
+        quant_echo(9)
         gain(1, 1)
-        first_pair(2, 0, work[0], work[1])
+        for k in range(10, 12):
+            turn(k, k - 8)
+            empty(k)
+        sum_banks = (4, 5, 7, 0)
+        work = (6, 1, 2, 3)
         second_quarter(0, 0)
-        quant_echo(12)
-        quant_echo(13)
-        quant_d_quarter(1, 0)
+        sort_words(12, SCALAR)
+        quant_echo(10)
+        quant_echo(11)
+        first_late(2, 0, work[0], work[1])
+        for k in range(13, 16):
+            sort_words(k, VECTOR)
         gain(2, 0)
+        gain(2, 1)
+        quant_d_quarter(1, 0)
+        widen(0, QUART, HALF, SCALAR)
+        for k in range(12, 16):
+            turn(k, work[(k + 2) % 4])
+            empty(k)
+        second_quarter(1, 0)
+        widen(1, QUART, HALF, VECTOR)
+        quant_echo(12)
+        quant_d_quarter(2, 0)
+        quant_echo(13)
+        interleave(0, QUART, QUART + P, VECTOR)
         quant_echo(14)
         quant_echo(15)
-        gain(2, 1)
-        first_pair(3, 0, work[2], work[3])
-        widen(0, QUART, HALF, SCALAR)
-        widen(1, QUART, HALF, SCALAR)
+        interleave(0, QUART + P, HALF, VECTOR)
+        first_by_slot(3, 0, work[2], work[3])
         widen(0, HALF, N, SCALAR)
-        second_quarter(1, 0)
-        interleave(0, QUART, HALF, VECTOR)
-        quant_d_quarter(2, 0)
+        widen(1, HALF, N, SCALAR)
         second_quarter(2, 0)
+        interleave(1, QUART, HALF, VECTOR)
+        quant_steer(0, QUART, HALF)
+        quant_steer(1, QUART, HALF)
         gain(3, 0)
         gain(3, 1)
-        quant_steer(0, QUART, HALF)
-        quant_d_quarter(3, 0)
-        second_quarter(3, 0)
-        interleave(1, QUART, HALF, VECTOR)
-        for j in range(OPEN):
-            finish_quarter(j, 0)
-        quant_steer(1, QUART, HALF)
 
         step(0, 1, work[0], work[1])
+        gain_two(0, 1, 0)
+        quant_d_quarter(3, 0)
         step(1, 1, work[2], work[3])
-        interleave(0, HALF, N, VECTOR)
-        gains_two(0, 1)
+        second_quarter(3, 0)
+        gain_two(0, 1, 1)
         join(0, 1)
+        for j in range(2):
+            finish_quarter(j, 0)
         step(2, 1, work[0], work[1])
         gains_two(1, 1)
-        widen(1, HALF, HALF + QUART, SCALAR)
         join(1, 1)
-        step(3, 1, work[2], work[3])
-        gain_two(2, 1, 0)
+        for j in range(2, OPEN):
+            finish_quarter(j, 0)
+        interleave(0, HALF, HALF + QUART, VECTOR)
         quant_d_quarter(0, 1)
-        gain_two(2, 1, 1)
+        step(3, 1, work[2], work[3])
+        gains_two(2, 1)
         join(2, 1)
-        second_quarter(0, 1)
-        gain_two(3, 1, 0)
+        interleave(0, HALF + QUART, N, SCALAR)
         quant_d_quarter(1, 1)
+        second_quarter(0, 1)
         second_quarter(1, 1)
+        gain_two(3, 1, 0)
         interleave(1, HALF, HALF + QUART, VECTOR)
         quant_steer(0, HALF, HALF + QUART)
         quant_steer(1, HALF, HALF + QUART)
         gain_two(3, 1, 1)
-        widen(1, HALF + QUART, N, SCALAR)
         quant_d_quarter(2, 1)
-        interleave(1, HALF + QUART, N, SCALAR)
         join(3, 1)
+        interleave(1, HALF + QUART, N, SCALAR)
 
         steps = [(0, 2), (1, 2), (0, 3), (1, 3), (2, 2), (2, 3), (3, 2), (3, 3)]
         held = [(i, g) for g in range(G - 1) for i in range(OPEN)]
@@ -464,16 +481,16 @@ def tile_sonar_ping_coherence_s13_kernel(tc, echo, steer_bytes, steer_scale, ref
             elif step < len(steps) - 1:
                 i, held_g = held.pop(0)
                 second(i, held_g, HALF, N, sum_banks[i])
-        for i, held_g in held:
+        for i, held_g in held[:-2]:
             second(i, held_g, HALF, N, sum_banks[i])
         for i in range(OPEN):
+            if (i, G - 2) in held[-2:]:
+                second(i, G - 2, HALF, N, sum_banks[i])
             second(i, G - 1, HALF, N, sum_banks[i])
             finish(i, HALF, N, HALF)
-        for i in range(OPEN, BANDS - 1):
+        pieces = [(i, HALF, N) for i in range(OPEN, BANDS - 2)]
+        pieces += [(BANDS - 2, HALF, HALF + QUART), (BANDS - 2, HALF + QUART, N), (BANDS - 1, HALF, HALF + QUART), (BANDS - 1, HALF + QUART, N - P), (BANDS - 1, N - P, N)]
+        for (i, n0, n1), k in zip(pieces, work + sum_banks):
             for g in range(G):
-                second(i, g, HALF, N, work[i - OPEN])
-            finish(i, HALF, N, QUART if i == BANDS - 2 else HALF)
-        for n0, n1, k in ((HALF, HALF + QUART, work[3]), (HALF + QUART, N - P, sum_banks[0]), (N - P, N, sum_banks[1])):
-            for g in range(G):
-                second(BANDS - 1, g, n0, n1, k)
-            finish(BANDS - 1, n0, n1, n1 - n0)
+                second(i, g, n0, n1, k)
+            finish(i, n0, n1, n1 - n0)

@@ -69,7 +69,7 @@ def tile_sonar_ping_coherence_s13_kernel(tc, echo, steer_bytes, steer_scale, ref
 
         echo_g = echo.rearrange("(g p t) k -> g p t k", p=P, t=SLOTS)
         steer_c = steer_bytes.rearrange("(c p t) n -> c p t n", p=P, t=SLOTS)
-        eraw, esort, xbank, egrp, sraw, swide = {}, {}, {}, {}, {}, {}
+        eraw, esort, xbank, egrp, epass, sraw, swide = {}, {}, {}, {}, {}, {}, {}
         ybank, ytwo, dgrp, dtwo, dwide, pair_sum, band_sum = {}, {}, {}, {}, {}, {}, {}
 
         def load_echo(k0, k1):
@@ -140,6 +140,18 @@ def tile_sonar_ping_coherence_s13_kernel(tc, echo, steer_bytes, steer_scale, ref
                 out=egrp[k][:].bitcast(F32).rearrange("p (c r u) -> p c r u", c=CP, u=2),
                 in_=xbank[k][:].rearrange("p (c u r) -> p c r u", c=CP, u=2),
             )
+
+        def empty_by_pass(k):
+            for c in range(CP):
+                epass[(k, c)] = ring.tile([P, HALF], BF16, name="epass", tag="epass", align_bytes=256)
+                nc.scalar.copy(
+                    out=epass[(k, c)][:].bitcast(F32).rearrange("p (r u) -> p r u", u=2),
+                    in_=xbank[k][:, 2 * P * c : 2 * P * (c + 1)].rearrange("p (u r) -> p r u", u=2),
+                )
+
+        def quant_echo_pass(k, c):
+            cols = slice((k % SLOTS * CP + c) * P, (k % SLOTS * CP + c + 1) * P)
+            nc.vector.quantize_mx(out=ecod[k // SLOTS][:, cols].bitcast(FP8X4), scales=escl[k // SLOTS][:, cols], in_=epass[(k, c)][:])
 
         def quant_echo(k):
             cols = slice(k % SLOTS * CP * P, (k % SLOTS + 1) * CP * P)
@@ -286,10 +298,11 @@ def tile_sonar_ping_coherence_s13_kernel(tc, echo, steer_bytes, steer_scale, ref
             load_echo(k, k + 2)
         load_words(0)
         load_scales(0, 1)
-        for k in range(10, 16, 2):
+        load_echo(10, 12)
+        load_steer(0, QUART, HALF)
+        for k in range(12, 16, 2):
             load_echo(k, k + 2)
-        for c in range(CP):
-            load_steer(c, QUART, HALF)
+        load_steer(1, QUART, HALF)
         load_scales(1, G)
         load_words(1)
         load_words(2)
@@ -368,15 +381,16 @@ def tile_sonar_ping_coherence_s13_kernel(tc, echo, steer_bytes, steer_scale, ref
             turn(k, kb)
             empty(k)
         quant_echo(6)
-        quant_d_quarter(0, 0)
         quant_echo(7)
         first_by_slot(1, 0, 6, 1)
         sort_words(10, VECTOR)
-        sort_words(11, SCALAR)
-        quant_echo(8)
+        sort_words(11, VECTOR)
+        quant_d_quarter(0, 0)
+        widen(0, QUART, HALF, SCALAR, (0, 1))
         gain(1, 0)
-        quant_echo(9)
         gain(1, 1)
+        quant_echo(8)
+        quant_echo(9)
         for k in range(10, 12):
             turn(k, k - 8)
             empty(k)
@@ -384,32 +398,34 @@ def tile_sonar_ping_coherence_s13_kernel(tc, echo, steer_bytes, steer_scale, ref
         work = (6, 1, 2, 3)
         second_quarter(0, 0)
         sort_words(12, SCALAR)
+        sort_words(15, SCALAR)
+        widen(0, QUART, HALF, SCALAR, (2, 3))
         quant_echo(10)
         quant_echo(11)
         first_late(2, 0, work[0], work[1])
-        for k in range(13, 16):
+        for k in range(13, 15):
             sort_words(k, VECTOR)
         gain(2, 0)
         gain(2, 1)
         quant_d_quarter(1, 0)
-        widen(0, QUART, HALF, SCALAR)
+        widen(1, QUART, HALF, SCALAR, (0,))
         for k in range(12, 16):
             turn(k, work[(k + 2) % 4])
             empty(k)
         second_quarter(1, 0)
-        widen(1, QUART, HALF, VECTOR)
-        quant_echo(12)
+        widen(1, QUART, HALF, VECTOR, (1, 2, 3))
+        for k in range(12, 16):
+            quant_echo(k)
+            if k == 13:
+                interleave(1, QUART, QUART + P, VECTOR)
         quant_d_quarter(2, 0)
-        quant_echo(13)
-        interleave(0, QUART, QUART + P, VECTOR)
-        quant_echo(14)
-        quant_echo(15)
-        interleave(0, QUART + P, HALF, VECTOR)
         first_by_slot(3, 0, work[2], work[3])
-        widen(0, HALF, N, SCALAR)
-        widen(1, HALF, N, SCALAR)
+        interleave(0, QUART, HALF, SCALAR)
+        for c in range(CP):
+            widen(c, HALF, HALF + QUART, SCALAR)
+        widen(0, HALF + QUART, N, SCALAR)
         second_quarter(2, 0)
-        interleave(1, QUART, HALF, VECTOR)
+        interleave(1, QUART + P, HALF, VECTOR)
         quant_steer(0, QUART, HALF)
         quant_steer(1, QUART, HALF)
         gain(3, 0)
@@ -434,10 +450,11 @@ def tile_sonar_ping_coherence_s13_kernel(tc, echo, steer_bytes, steer_scale, ref
         step(3, 1, work[2], work[3])
         gains_two(2, 1)
         join(2, 1)
-        interleave(0, HALF + QUART, N, SCALAR)
+        widen(1, HALF + QUART, N, SCALAR)
         quant_d_quarter(1, 1)
-        second_quarter(0, 1)
-        second_quarter(1, 1)
+        for pairs in ((0, 1), (2, 3)):
+            second_quarter(0, 1, pairs)
+            second_quarter(1, 1, pairs)
         gain_two(3, 1, 0)
         interleave(1, HALF, HALF + QUART, VECTOR)
         quant_steer(0, HALF, HALF + QUART)
@@ -445,9 +462,10 @@ def tile_sonar_ping_coherence_s13_kernel(tc, echo, steer_bytes, steer_scale, ref
         gain_two(3, 1, 1)
         quant_d_quarter(2, 1)
         join(3, 1)
-        interleave(1, HALF + QUART, N, SCALAR)
+        for c in range(CP):
+            interleave(c, HALF + QUART, N, SCALAR)
 
-        steps = [(0, 2), (1, 2), (0, 3), (1, 3), (2, 2), (2, 3), (3, 2), (3, 3)]
+        steps = [(0, 2), (1, 2), (2, 2), (0, 3), (1, 3), (2, 3), (3, 2), (3, 3)]
         held = [(i, g) for g in range(G - 1) for i in range(OPEN)]
         for step, (g, q) in enumerate(steps):
             ka, kb = work[2 * (step % 2)], work[2 * (step % 2) + 1]
@@ -466,10 +484,12 @@ def tile_sonar_ping_coherence_s13_kernel(tc, echo, steer_bytes, steer_scale, ref
                 if step == 0:
                     quant_d_quarter(G - 1, 1)
                 gain_two(g, q, 1)
-                if step == 0:
+                if step == 1:
                     for c in range(CP):
                         quant_steer(c, HALF + QUART, N)
-                else:
+                if step == 2:
+                    quant_d_quarter(*steps[0])
+                if step > 1:
                     quant_d_quarter(*steps[step - 1])
                 join(g, q)
             if step < 4:
@@ -478,9 +498,10 @@ def tile_sonar_ping_coherence_s13_kernel(tc, echo, steer_bytes, steer_scale, ref
                 if step >= 2:
                     for j in pairs:
                         finish_quarter(j, 1)
-            elif step < len(steps) - 1:
-                i, held_g = held.pop(0)
-                second(i, held_g, HALF, N, sum_banks[i])
+            elif step == len(steps) - 2:
+                for j in range(3):
+                    i, held_g = held.pop(0)
+                    second(i, held_g, HALF, N, sum_banks[i])
         for i, held_g in held[:-2]:
             second(i, held_g, HALF, N, sum_banks[i])
         for i in range(OPEN):

@@ -208,8 +208,8 @@ def tile_sonar_ping_coherence_s13_kernel(tc, echo, steer_bytes, steer_scale, ref
                 op=MULT,
             )
 
-        def join(g, q):
-            nc.scalar.copy(
+        def join(g, q, on_vector=False):
+            copier(on_vector)(
                 out=d_tile(g, q)[:].rearrange("p n t -> p (n t)").bitcast(F32).rearrange("p (n u) -> p n u", u=2),
                 in_=dtwo[(g, q)][:].rearrange("p u n e -> p (u n e)").bitcast(F32).rearrange("p (u n) -> p n u", u=2),
             )
@@ -277,7 +277,7 @@ def tile_sonar_ping_coherence_s13_kernel(tc, echo, steer_bytes, steer_scale, ref
         def warm(n, k, moving):
             scratch = bank(k)
             for j in range(n):
-                nc.tensor.matmul(out=scratch[:, 0 : moving.shape[1]], lhsT=ones[:, 0:P], rhs=moving, start=True, stop=True)
+                nc.tensor.matmul(out=scratch[:], lhsT=ones[:, 0:P], rhs=moving, start=True, stop=True)
 
         nc.scalar.dma_start(out=sscl[:], in_=steer_scale.rearrange("(c p t) o -> p c (t o)", p=P, t=SLOTS))
         nc.vector.memset(ones[:].bitcast(I32), TWO_ONES)
@@ -294,14 +294,13 @@ def tile_sonar_ping_coherence_s13_kernel(tc, echo, steer_bytes, steer_scale, ref
                 nc.sync.dma_start(out=gains[0:1, 0:HALF], in_=col_gain[0:HALF].unsqueeze(0))
         nc.scalar.dma_start(out=gains[0:BANDS, HALF : HALF + P], in_=row_gain.rearrange("(i m) -> i m", m=P))
         nc.scalar.copy(out=idb[:], in_=idf[:, 0:BANDS])
-        for k in range(4, 10, 2):
+        for k in range(4, 12, 2):
             load_echo(k, k + 2)
-        load_words(0)
         load_scales(0, 1)
-        load_echo(10, 12)
+        load_echo(12, 14)
+        load_words(0)
         load_steer(0, QUART, HALF)
-        for k in range(12, 16, 2):
-            load_echo(k, k + 2)
+        load_echo(14, 16)
         load_steer(1, QUART, HALF)
         load_scales(1, G)
         load_words(1)
@@ -327,9 +326,10 @@ def tile_sonar_ping_coherence_s13_kernel(tc, echo, steer_bytes, steer_scale, ref
             if 0 < k < LAST_SLOT:
                 q = k - 1
                 nc.tensor.matmul(out=gbank[:, q * P : (q + 1) * P].bitcast(BF16), lhsT=ones[:, 0:P], rhs=gains[:, q * QUART : (q + 1) * QUART], start=True, stop=True)
-            quant_echo(k)
             if k == 2:
                 nc.vector.tensor_copy(out=cgain[:, 0:HALF], in_=gbank[:, 0:QUART].bitcast(BF16))
+            if k < LAST_SLOT:
+                quant_echo(k)
         def first_pair(g, q, ka, kb):
             for t in range(LAST_SLOT):
                 first_slot(g, 2 * q, t, ka)
@@ -359,24 +359,22 @@ def tile_sonar_ping_coherence_s13_kernel(tc, echo, steer_bytes, steer_scale, ref
                 first_slot(g, 2 * q, t, ka)
                 first_slot(g, 2 * q + 1, t, kb)
 
-        for t in range(2):
-            first_slot(0, 0, t, 4)
-            first_slot(0, 1, t, 5)
+        first_two(0, 0, 0, 4)
+        gain_two(0, 0, 0)
+        quant_echo(LAST_SLOT)
         for k in range(4, 6):
             turn(k, k - 4)
             empty(k)
         rbank = bank(7)
         nc.tensor.matmul(out=rbank[:, 0:BANDS], lhsT=gains[:, HALF : HALF + P], rhs=idb[:], start=True, stop=True)
-        for b in range(2):
-            for t in range(2, SLOTS):
-                first_slot(0, b, t, 4 + b)
+        first_two(0, 0, 1, 5)
         sort_words(6, VECTOR)
         sort_words(7, VECTOR)
         nc.vector.tensor_copy(out=rgain[:], in_=rbank[:, 0:BANDS])
         quant_echo(4)
-        gain(0, 0)
+        gain_two(0, 0, 1)
         quant_echo(5)
-        gain(0, 1)
+        join(0, 0, VECTOR)
         for k, kb in zip(range(6, 10), (2, 3, 7, 0)):
             turn(k, kb)
             empty(k)
@@ -386,7 +384,7 @@ def tile_sonar_ping_coherence_s13_kernel(tc, echo, steer_bytes, steer_scale, ref
         sort_words(10, VECTOR)
         sort_words(11, VECTOR)
         quant_d_quarter(0, 0)
-        widen(0, QUART, HALF, SCALAR, (0, 1))
+        sort_words(12, SCALAR)
         gain(1, 0)
         gain(1, 1)
         quant_echo(8)
@@ -397,35 +395,33 @@ def tile_sonar_ping_coherence_s13_kernel(tc, echo, steer_bytes, steer_scale, ref
         sum_banks = (4, 5, 7, 0)
         work = (6, 1, 2, 3)
         second_quarter(0, 0)
-        sort_words(12, SCALAR)
+        sort_words(13, SCALAR)
+        sort_words(14, SCALAR)
         sort_words(15, SCALAR)
-        widen(0, QUART, HALF, SCALAR, (2, 3))
+        widen(0, QUART, HALF, SCALAR, (0,))
         quant_echo(10)
         quant_echo(11)
-        first_late(2, 0, work[0], work[1])
-        for k in range(13, 15):
-            sort_words(k, VECTOR)
-        gain(2, 0)
-        gain(2, 1)
+        step(2, 0, work[0], work[1])
+        widen(0, QUART, HALF, VECTOR, (1, 2))
+        gains_two(2, 0)
         quant_d_quarter(1, 0)
-        widen(1, QUART, HALF, SCALAR, (0,))
+        widen(0, QUART, HALF, VECTOR, (3,))
+        join(2, 0, VECTOR)
         for k in range(12, 16):
             turn(k, work[(k + 2) % 4])
             empty(k)
         second_quarter(1, 0)
-        widen(1, QUART, HALF, VECTOR, (1, 2, 3))
         for k in range(12, 16):
             quant_echo(k)
-            if k == 13:
-                interleave(1, QUART, QUART + P, VECTOR)
+            if k < 14:
+                widen(1, QUART, HALF, VECTOR, (2 * k - 24, 2 * k - 23))
         quant_d_quarter(2, 0)
         first_by_slot(3, 0, work[2], work[3])
         interleave(0, QUART, HALF, SCALAR)
-        for c in range(CP):
-            widen(c, HALF, HALF + QUART, SCALAR)
-        widen(0, HALF + QUART, N, SCALAR)
+        widen(0, HALF, N, SCALAR)
+        widen(1, HALF, HALF + QUART, SCALAR)
         second_quarter(2, 0)
-        interleave(1, QUART + P, HALF, VECTOR)
+        interleave(1, QUART, HALF, VECTOR)
         quant_steer(0, QUART, HALF)
         quant_steer(1, QUART, HALF)
         gain(3, 0)

@@ -299,9 +299,9 @@ def tile_sonar_ping_coherence_s13_kernel(tc, echo, steer_bytes, steer_scale, ref
         load_scales(0, 1)
         load_echo(12, 14)
         load_words(0)
-        load_steer(0, QUART, HALF)
         load_echo(14, 16)
-        load_steer(1, QUART, HALF)
+        for c in range(CP):
+            load_steer(c, QUART, HALF)
         load_scales(1, G)
         load_words(1)
         load_words(2)
@@ -379,9 +379,9 @@ def tile_sonar_ping_coherence_s13_kernel(tc, echo, steer_bytes, steer_scale, ref
             turn(k, kb)
             empty(k)
         quant_echo(6)
+        sort_words(10, VECTOR)
         quant_echo(7)
         first_by_slot(1, 0, 6, 1)
-        sort_words(10, VECTOR)
         sort_words(11, VECTOR)
         quant_d_quarter(0, 0)
         sort_words(12, SCALAR)
@@ -402,19 +402,22 @@ def tile_sonar_ping_coherence_s13_kernel(tc, echo, steer_bytes, steer_scale, ref
         quant_echo(10)
         quant_echo(11)
         step(2, 0, work[0], work[1])
-        widen(0, QUART, HALF, VECTOR, (1, 2))
-        gains_two(2, 0)
         quant_d_quarter(1, 0)
-        widen(0, QUART, HALF, VECTOR, (3,))
+        gains_two(2, 0)
+        widen(0, QUART, HALF, VECTOR, (1, 2, 3))
         join(2, 0, VECTOR)
         for k in range(12, 16):
             turn(k, work[(k + 2) % 4])
-            empty(k)
+            if k < 15:
+                empty(k)
+        empty_by_pass(15)
         second_quarter(1, 0)
-        for k in range(12, 16):
+        for k in range(12, 15):
             quant_echo(k)
             if k < 14:
                 widen(1, QUART, HALF, VECTOR, (2 * k - 24, 2 * k - 23))
+        for c in range(CP):
+            quant_echo_pass(15, c)
         quant_d_quarter(2, 0)
         first_by_slot(3, 0, work[2], work[3])
         interleave(0, QUART, HALF, SCALAR)

@@ -27,6 +27,7 @@ QUART = 256
 BANDS = R // P
 OPEN = 4
 LAST_SLOT = SLOTS - 1
+GAINS = HALF + QUART
 TWO_ONES = 0x3F803F80
 VECTOR, SCALAR = True, False
 
@@ -59,7 +60,7 @@ def tile_sonar_ping_coherence_s13_kernel(tc, echo, steer_bytes, steer_scale, ref
         dscl = [kept([P, N], U8, "dscl%d" % g) for g in range(G)]
         pcod = [kept([P, 2 * R], U8, "pcod%d" % g) for g in range(G)]
         pscl = kept([P, G, R], U8, "pscl")
-        gains = kept([P, HALF + P + 2], BF16, "gains")
+        gains = kept([P, GAINS + P + 2], BF16, "gains")
         ones = kept([P, HALF + 2], BF16, "ones")
         idf = kept([P, P], F32, "idf")
         idb = kept([P, BANDS], BF16, "idb")
@@ -290,25 +291,26 @@ def tile_sonar_ping_coherence_s13_kernel(tc, echo, steer_bytes, steer_scale, ref
             load_steer(c, 0, QUART)
         for k in range(4):
             load_echo(k, k + 1)
-            if k == 1:
-                nc.sync.dma_start(out=gains[0:1, 0:HALF], in_=col_gain[0:HALF].unsqueeze(0))
-        nc.scalar.dma_start(out=gains[0:BANDS, HALF : HALF + P], in_=row_gain.rearrange("(i m) -> i m", m=P))
+            if k == 0:
+                nc.sync.dma_start(out=gains[0:1, 0:GAINS], in_=col_gain[0:GAINS].unsqueeze(0))
+        nc.scalar.dma_start(out=gains[0:BANDS, GAINS : GAINS + P], in_=row_gain.rearrange("(i m) -> i m", m=P))
         nc.scalar.copy(out=idb[:], in_=idf[:, 0:BANDS])
-        for k in range(4, 12, 2):
-            load_echo(k, k + 2)
+        for k0, k1 in ((4, 6), (6, 8), (8, 9), (9, 10), (10, 12)):
+            load_echo(k0, k1)
         load_scales(0, 1)
-        load_echo(12, 14)
+        load_echo(12, 13)
         load_words(0)
+        load_echo(13, 14)
         load_echo(14, 16)
-        for c in range(CP):
-            load_steer(c, QUART, HALF)
+        load_steer(0, QUART, HALF)
         load_scales(1, G)
         load_words(1)
+        load_steer(1, QUART, HALF)
         load_words(2)
         for c in range(CP):
             load_steer(c, HALF, N)
         load_words(3)
-        nc.sync.dma_start(out=cgain[:, HALF:N], in_=col_gain[HALF:N].partition_broadcast(P))
+        nc.sync.dma_start(out=cgain[:, GAINS:N], in_=col_gain[GAINS:N].partition_broadcast(P))
 
         warm(3, 7, ones[:, 0:HALF])
         widen(0, 0, QUART, VECTOR)
@@ -323,11 +325,11 @@ def tile_sonar_ping_coherence_s13_kernel(tc, echo, steer_bytes, steer_scale, ref
         for k in range(SLOTS):
             turn(k, k)
             empty(k)
-            if 0 < k < LAST_SLOT:
-                q = k - 1
+            if k < LAST_SLOT:
+                q = k
                 nc.tensor.matmul(out=gbank[:, q * P : (q + 1) * P].bitcast(BF16), lhsT=ones[:, 0:P], rhs=gains[:, q * QUART : (q + 1) * QUART], start=True, stop=True)
             if k == 2:
-                nc.vector.tensor_copy(out=cgain[:, 0:HALF], in_=gbank[:, 0:QUART].bitcast(BF16))
+                nc.vector.tensor_copy(out=cgain[:, 0:GAINS], in_=gbank[:, 0 : GAINS // 2].bitcast(BF16))
             if k < LAST_SLOT:
                 quant_echo(k)
         def first_pair(g, q, ka, kb):
@@ -366,7 +368,7 @@ def tile_sonar_ping_coherence_s13_kernel(tc, echo, steer_bytes, steer_scale, ref
             turn(k, k - 4)
             empty(k)
         rbank = bank(7)
-        nc.tensor.matmul(out=rbank[:, 0:BANDS], lhsT=gains[:, HALF : HALF + P], rhs=idb[:], start=True, stop=True)
+        nc.tensor.matmul(out=rbank[:, 0:BANDS], lhsT=gains[:, GAINS : GAINS + P], rhs=idb[:], start=True, stop=True)
         first_two(0, 0, 1, 5)
         sort_words(6, VECTOR)
         sort_words(7, VECTOR)
@@ -375,13 +377,15 @@ def tile_sonar_ping_coherence_s13_kernel(tc, echo, steer_bytes, steer_scale, ref
         gain_two(0, 0, 1)
         quant_echo(5)
         join(0, 0, VECTOR)
-        for k, kb in zip(range(6, 10), (2, 3, 7, 0)):
+        sort_words(8, SCALAR)
+        for k, kb in zip((6, 7, 9, 8), (2, 3, 7, 0)):
             turn(k, kb)
-            empty(k)
+            (empty_by_pass if k == 7 else empty)(k)
         quant_echo(6)
-        sort_words(10, VECTOR)
-        quant_echo(7)
+        for c in range(CP):
+            quant_echo_pass(7, c)
         first_by_slot(1, 0, 6, 1)
+        sort_words(10, VECTOR)
         sort_words(11, VECTOR)
         quant_d_quarter(0, 0)
         sort_words(12, SCALAR)

@@ -27,7 +27,6 @@ QUART = 256
 BANDS = R // P
 OPEN = 4
 LAST_SLOT = SLOTS - 1
-GAINS = HALF + QUART
 TWO_ONES = 0x3F803F80
 VECTOR, SCALAR = True, False
 
@@ -60,7 +59,7 @@ def tile_sonar_ping_coherence_s13_kernel(tc, echo, steer_bytes, steer_scale, ref
         dscl = [kept([P, N], U8, "dscl%d" % g) for g in range(G)]
         pcod = [kept([P, 2 * R], U8, "pcod%d" % g) for g in range(G)]
         pscl = kept([P, G, R], U8, "pscl")
-        gains = kept([P, GAINS + P + 2], BF16, "gains")
+        gains = kept([P, HALF + P + 2], BF16, "gains")
         ones = kept([P, HALF + 2], BF16, "ones")
         idf = kept([P, P], F32, "idf")
         idb = kept([P, BANDS], BF16, "idb")
@@ -291,9 +290,9 @@ def tile_sonar_ping_coherence_s13_kernel(tc, echo, steer_bytes, steer_scale, ref
             load_steer(c, 0, QUART)
         for k in range(4):
             load_echo(k, k + 1)
-            if k == 0:
-                nc.sync.dma_start(out=gains[0:1, 0:GAINS], in_=col_gain[0:GAINS].unsqueeze(0))
-        nc.scalar.dma_start(out=gains[0:BANDS, GAINS : GAINS + P], in_=row_gain.rearrange("(i m) -> i m", m=P))
+            if k == 1:
+                nc.sync.dma_start(out=gains[0:1, 0:HALF], in_=col_gain[0:HALF].unsqueeze(0))
+        nc.scalar.dma_start(out=gains[0:BANDS, HALF : HALF + P], in_=row_gain.rearrange("(i m) -> i m", m=P))
         nc.scalar.copy(out=idb[:], in_=idf[:, 0:BANDS])
         for k0, k1 in ((4, 6), (6, 8), (8, 9), (9, 10), (10, 12)):
             load_echo(k0, k1)
@@ -310,7 +309,7 @@ def tile_sonar_ping_coherence_s13_kernel(tc, echo, steer_bytes, steer_scale, ref
         for c in range(CP):
             load_steer(c, HALF, N)
         load_words(3)
-        nc.sync.dma_start(out=cgain[:, GAINS:N], in_=col_gain[GAINS:N].partition_broadcast(P))
+        nc.sync.dma_start(out=cgain[:, HALF:N], in_=col_gain[HALF:N].partition_broadcast(P))
 
         warm(3, 7, ones[:, 0:HALF])
         widen(0, 0, QUART, VECTOR)
@@ -325,11 +324,11 @@ def tile_sonar_ping_coherence_s13_kernel(tc, echo, steer_bytes, steer_scale, ref
         for k in range(SLOTS):
             turn(k, k)
             empty(k)
-            if k < LAST_SLOT:
-                q = k
+            if 0 < k < LAST_SLOT:
+                q = k - 1
                 nc.tensor.matmul(out=gbank[:, q * P : (q + 1) * P].bitcast(BF16), lhsT=ones[:, 0:P], rhs=gains[:, q * QUART : (q + 1) * QUART], start=True, stop=True)
             if k == 2:
-                nc.vector.tensor_copy(out=cgain[:, 0:GAINS], in_=gbank[:, 0 : GAINS // 2].bitcast(BF16))
+                nc.vector.tensor_copy(out=cgain[:, 0:HALF], in_=gbank[:, 0:QUART].bitcast(BF16))
             if k < LAST_SLOT:
                 quant_echo(k)
         def first_pair(g, q, ka, kb):
@@ -368,7 +367,7 @@ def tile_sonar_ping_coherence_s13_kernel(tc, echo, steer_bytes, steer_scale, ref
             turn(k, k - 4)
             empty(k)
         rbank = bank(7)
-        nc.tensor.matmul(out=rbank[:, 0:BANDS], lhsT=gains[:, GAINS : GAINS + P], rhs=idb[:], start=True, stop=True)
+        nc.tensor.matmul(out=rbank[:, 0:BANDS], lhsT=gains[:, HALF : HALF + P], rhs=idb[:], start=True, stop=True)
         first_two(0, 0, 1, 5)
         sort_words(6, VECTOR)
         sort_words(7, VECTOR)

@@ -35,7 +35,7 @@ def tile_sonar_ping_coherence_s13_kernel(tc, echo, steer_bytes, steer_scale, ref
     nc = tc.nc
     with ExitStack() as ctx:
         keep = ctx.enter_context(tc.tile_pool(name="keep", bufs=1))
-        ring = ctx.enter_context(tc.tile_pool(name="ring", bufs=4))
+        ring = ctx.enter_context(tc.tile_pool(name="ring", bufs=6))
         stage = ctx.enter_context(tc.tile_pool(name="stage", bufs=8))
         psum = ctx.enter_context(tc.psum_pool(name="psum", bufs=1))
         ctx.enter_context(tc.manual_schedule())
@@ -70,7 +70,7 @@ def tile_sonar_ping_coherence_s13_kernel(tc, echo, steer_bytes, steer_scale, ref
         echo_g = echo.rearrange("(g p t) k -> g p t k", p=P, t=SLOTS)
         steer_c = steer_bytes.rearrange("(c p t) n -> c p t n", p=P, t=SLOTS)
         eraw, esort, xbank, egrp, epass, sraw, swide = {}, {}, {}, {}, {}, {}, {}
-        ybank, ytwo, dgrp, dtwo, dwide, pair_sum, band_sum = {}, {}, {}, {}, {}, {}, {}
+        ybank, ytwo, dgrp, dtwo, band_sum = {}, {}, {}, {}, {}
 
         def load_echo(k0, k1):
             tile = kept([P, k1 - k0, C], BF16, "eraw%d" % k0)
@@ -88,10 +88,10 @@ def tile_sonar_ping_coherence_s13_kernel(tc, echo, steer_bytes, steer_scale, ref
             nc.sync.dma_start(out=pcod[g][:].bitcast(I32), in_=ref_words[g].bitcast(I32))
 
         def load_scales(g0, g1):
-            for a in range(4):
+            for r in range(4):
                 nc.sync.dma_start(
-                    out=pscl[32 * a : 32 * a + 4, g0:g1, :].bitcast(I32),
-                    in_=ref_scales[g0:g1, 4 * a : 4 * a + 4, :].rearrange("g r n -> r g n").bitcast(I32),
+                    out=pscl[r:P:32, g0:g1, :].bitcast(I32),
+                    in_=ref_scales[g0:g1, r:16:4, :].rearrange("g a n -> a g n").bitcast(I32),
                 )
 
         def widen(c, n0, n1, on_vector, slots=range(SLOTS)):
@@ -214,21 +214,6 @@ def tile_sonar_ping_coherence_s13_kernel(tc, echo, steer_bytes, steer_scale, ref
                 in_=dtwo[(g, q)][:].rearrange("p u n e -> p (u n e)").bitcast(F32).rearrange("p (u n) -> p n u", u=2),
             )
 
-        def first_wide(g, t, k):
-            ybank[(g, t, HALF)] = bank(k)
-            first_sum(ybank[(g, t, HALF)][:], g, t, HALF, N)
-
-        def gain_wide(g, t):
-            if t == 0:
-                dwide[g] = ring.tile([P, SLOTS, HALF], BF16, name="dwide", tag="dwide", align_bytes=256, bufs=2)
-            nc.vector.tensor_tensor(out=dwide[g][:, t, :], in0=ybank[(g, t, HALF)][:], in1=cgain[:, HALF:N], op=MULT)
-
-        def weave(g, q):
-            nc.scalar.copy(
-                out=d_tile(g, q)[:].rearrange("p (n i) t -> p n t i", i=4),
-                in_=dwide[g][:, :, q * QUART - HALF : (q + 1) * QUART - HALF].rearrange("p t (n i) -> p n t i", i=4),
-            )
-
         def quant_d(g, b0, b1):
             src = dgrp[(g, b0 // 2)][:, (b0 % 2) * P : (b0 % 2 + b1 - b0) * P, :]
             cols = slice(b0 * P, b1 * P)
@@ -247,21 +232,6 @@ def tile_sonar_ping_coherence_s13_kernel(tc, echo, steer_bytes, steer_scale, ref
                 start=start,
                 stop=stop,
             )
-
-        def second_quarter(g, q, pairs=range(OPEN)):
-            for j in pairs:
-                if g == 0:
-                    pair_sum[(j, q)] = bank(sum_banks[j])
-                for e in range(2):
-                    dst = pair_sum[(j, q)][:, e * QUART : (e + 1) * QUART]
-                    second_pass(dst, 2 * j + e, g, q * QUART, (q + 1) * QUART, g == 0 and e == 0, g == G - 1 and e == 1)
-
-        def finish_quarter(j, q):
-            o = stage.tile([P, 2, QUART], F32, name="o", tag="o", align_bytes=256)
-            for e in range(2):
-                i = 2 * j + e
-                nc.scalar.activation(out=o[:, e, :], in_=pair_sum[(j, q)][:, e * QUART : (e + 1) * QUART], func=SQUARE, scale=rgain[:, i : i + 1])
-            nc.sync.dma_start(out=out[2 * j * P : (2 * j + 2) * P, q * QUART : (q + 1) * QUART].rearrange("(e p) n -> p e n", e=2), in_=o[:])
 
         def second(i, g, n0, n1, k):
             if g == 0:
@@ -286,234 +256,218 @@ def tile_sonar_ping_coherence_s13_kernel(tc, echo, steer_bytes, steer_scale, ref
         make_identity(nc, idf[:])
         nc.vector.memset(pscl[:].rearrange("p g n -> p (g n)").bitcast(I32), 0)
 
+
         for c in range(CP):
-            load_steer(c, 0, QUART)
+            load_steer(c, 0, HALF)
         for k in range(4):
             load_echo(k, k + 1)
             if k == 1:
                 nc.sync.dma_start(out=gains[0:1, 0:HALF], in_=col_gain[0:HALF].unsqueeze(0))
         nc.scalar.dma_start(out=gains[0:BANDS, HALF : HALF + P], in_=row_gain.rearrange("(i m) -> i m", m=P))
-        nc.scalar.copy(out=idb[:], in_=idf[:, 0:BANDS])
-        for k0, k1 in ((4, 6), (6, 8), (8, 9), (9, 10), (10, 12)):
-            load_echo(k0, k1)
-        load_scales(0, 1)
-        load_echo(12, 13)
+        for k in range(4, 16, 2):
+            load_echo(k, k + 2)
+        load_scales(0, G)
         load_words(0)
-        load_echo(13, 14)
-        load_echo(14, 16)
-        load_steer(0, QUART, HALF)
-        load_scales(1, G)
         load_words(1)
-        load_steer(1, QUART, HALF)
-        load_words(2)
         for c in range(CP):
             load_steer(c, HALF, N)
-        load_words(3)
+        load_words(2)
         nc.sync.dma_start(out=cgain[:, HALF:N], in_=col_gain[HALF:N].partition_broadcast(P))
+        load_words(3)
 
-        warm(3, 7, ones[:, 0:HALF])
-        widen(0, 0, QUART, VECTOR)
-        warm(2, 7, swide[(0, 0)][0][:, 0:2, :].rearrange("p t n -> p (t n)"))
-        widen(1, 0, QUART, VECTOR, (0, 1))
-        widen(1, 0, QUART, SCALAR, (2, 3))
-        for c in range(CP):
-            interleave(c, 0, QUART, VECTOR)
-        for c in range(CP):
-            quant_steer(c, 0, QUART)
-        gbank = bank(6)
-        for k in range(SLOTS):
-            turn(k, k)
-            empty(k)
-            if 0 < k < LAST_SLOT:
-                q = k - 1
-                nc.tensor.matmul(out=gbank[:, q * P : (q + 1) * P].bitcast(BF16), lhsT=ones[:, 0:P], rhs=gains[:, q * QUART : (q + 1) * QUART], start=True, stop=True)
-            if k == 2:
-                nc.vector.tensor_copy(out=cgain[:, 0:HALF], in_=gbank[:, 0:QUART].bitcast(BF16))
-            if k < LAST_SLOT:
-                quant_echo(k)
-        def first_pair(g, q, ka, kb):
-            for t in range(LAST_SLOT):
-                first_slot(g, 2 * q, t, ka)
-            first_slot(g, 2 * q + 1, 0, kb)
-            first_slot(g, 2 * q, LAST_SLOT, ka)
-            for t in range(1, SLOTS):
-                first_slot(g, 2 * q + 1, t, kb)
+        sums = (2, 3, 6, 7)
 
-        def step(g, q, ka, kb):
-            first_two(g, q, 0, ka)
-            first_two(g, q, 1, kb)
+        def second_open(g, n0):
+            for i in range(OPEN):
+                second(i, g, n0, n0 + HALF, sums[i])
+
+        def whole_band(i, n0, n1, k):
+            for g in range(G):
+                second(i, g, n0, n1, k)
+            finish(i, n0, n1, n1 - n0)
 
         def gains_two(g, q):
             gain_two(g, q, 0)
             gain_two(g, q, 1)
 
-        def first_late(g, q, ka, kb):
-            for t in range(2):
-                first_slot(g, 2 * q, t, ka)
-                first_slot(g, 2 * q + 1, t, kb)
-            for b, k in ((2 * q, ka), (2 * q + 1, kb)):
-                for t in range(2, SLOTS):
-                    first_slot(g, b, t, k)
-
-        def first_by_slot(g, q, ka, kb):
-            for t in range(SLOTS):
-                first_slot(g, 2 * q, t, ka)
-                first_slot(g, 2 * q + 1, t, kb)
-
+        warm(3, 7, ones[:, 0:HALF])
+        widen(0, 0, QUART, VECTOR)
+        warm(2, 7, swide[(0, 0)][0][:, 0:2, :].rearrange("p t n -> p (t n)"))
+        widen(0, QUART, HALF, SCALAR)
+        interleave(0, 0, QUART, VECTOR)
+        widen(1, 0, QUART, VECTOR, (0, 1))
+        widen(1, 0, QUART, SCALAR, (2, 3))
+        widen(1, QUART, HALF, SCALAR, (0, 1))
+        quant_steer(0, 0, QUART)
+        interleave(1, 0, QUART, VECTOR)
+        interleave(0, QUART, HALF, VECTOR)
+        quant_steer(1, 0, QUART)
+        gbank = bank(6)
+        for k in range(SLOTS):
+            turn(k, k)
+            if k == LAST_SLOT:
+                widen(1, QUART, HALF, SCALAR, (2, 3))
+                nc.scalar.copy(out=idb[:], in_=idf[:, 0:BANDS])
+            empty(k)
+            if 0 < k < LAST_SLOT:
+                q = k - 1
+                nc.tensor.matmul(out=gbank[:, q * P : (q + 1) * P].bitcast(BF16), lhsT=ones[:, 0:P], rhs=gains[:, q * QUART : (q + 1) * QUART], start=True, stop=True)
+        quant_echo(0)
+        quant_echo(1)
+        nc.vector.tensor_copy(out=cgain[:, 0:HALF], in_=gbank[:, 0:QUART].bitcast(BF16))
+        quant_steer(0, QUART, HALF)
+        quant_echo(2)
+        interleave(1, QUART, HALF, VECTOR)
+        quant_echo(3)
         first_two(0, 0, 0, 4)
-        gain_two(0, 0, 0)
-        quant_echo(LAST_SLOT)
-        for k in range(4, 6):
+        for k in (4, 5):
             turn(k, k - 4)
             empty(k)
         rbank = bank(7)
         nc.tensor.matmul(out=rbank[:, 0:BANDS], lhsT=gains[:, HALF : HALF + P], rhs=idb[:], start=True, stop=True)
-        first_two(0, 0, 1, 5)
-        sort_words(6, VECTOR)
-        sort_words(7, VECTOR)
+        quant_steer(1, QUART, HALF)
+        gain_two(0, 0, 0)
         nc.vector.tensor_copy(out=rgain[:], in_=rbank[:, 0:BANDS])
+        first_two(0, 0, 1, 5)
+        first_two(0, 1, 0, 6)
+        first_two(0, 1, 1, 7)
         quant_echo(4)
-        gain_two(0, 0, 1)
+        sort_words(6, VECTOR)
+        for k in range(7, 10):
+            sort_words(k, SCALAR)
         quant_echo(5)
-        join(0, 0, VECTOR)
-        sort_words(8, SCALAR)
-        for k, kb in zip((6, 7, 9, 8), (2, 3, 7, 0)):
+        gain_two(0, 0, 1)
+        gain_two(0, 1, 0)
+        gain_two(0, 1, 1)
+        for k, kb in zip(range(6, 10), (2, 3, 0, 1)):
             turn(k, kb)
-            (empty_by_pass if k == 7 else empty)(k)
-        quant_echo(6)
-        for c in range(CP):
-            quant_echo_pass(7, c)
-        first_by_slot(1, 0, 6, 1)
-        sort_words(10, VECTOR)
-        sort_words(11, VECTOR)
-        quant_d_quarter(0, 0)
-        sort_words(12, SCALAR)
-        gain(1, 0)
-        gain(1, 1)
-        quant_echo(8)
-        quant_echo(9)
-        for k in range(10, 12):
-            turn(k, k - 8)
             empty(k)
-        sum_banks = (4, 5, 7, 0)
-        work = (6, 1, 2, 3)
-        second_quarter(0, 0)
+        quant_echo(6)
+        sort_words(10, VECTOR)
+        quant_echo(7)
+        sort_words(11, VECTOR)
+        for u in range(2):
+            for q in range(2):
+                first_two(1, q, u, 4 + 2 * u + q)
+        sort_words(12, SCALAR)
         sort_words(13, SCALAR)
-        sort_words(14, SCALAR)
-        sort_words(15, SCALAR)
-        widen(0, QUART, HALF, SCALAR, (0,))
+        join(0, 0)
+        gain_two(1, 0, 0)
+        quant_echo(8)
+        gain_two(1, 1, 0)
+        quant_echo(9)
+        for k, kb in zip(range(10, 14), (2, 3, 0, 1)):
+            turn(k, kb)
+            empty(k)
+        join(0, 1, VECTOR)
+        gain_two(1, 0, 1)
+        quant_d_quarter(0, 0)
+        quant_d_quarter(0, 1)
+        gain_two(1, 1, 1)
+        first_two(2, 0, 0, 4)
+        first_two(2, 1, 0, 5)
         quant_echo(10)
         quant_echo(11)
-        step(2, 0, work[0], work[1])
+        second_open(0, 0)
+        join(1, 0)
+        sort_words(14, SCALAR)
+        sort_words(15, SCALAR)
+        widen(0, HALF, HALF + QUART, SCALAR, (0, 1))
+        join(1, 1, VECTOR)
+        gain_two(2, 0, 0)
+        gain_two(2, 1, 0)
+        first_two(2, 0, 1, 0)
+        first_two(2, 1, 1, 1)
         quant_d_quarter(1, 0)
-        gains_two(2, 0)
-        widen(0, QUART, HALF, VECTOR, (1, 2, 3))
-        join(2, 0, VECTOR)
-        for k in range(12, 16):
-            turn(k, work[(k + 2) % 4])
-            if k < 15:
-                empty(k)
-        empty_by_pass(15)
-        second_quarter(1, 0)
-        for k in range(12, 15):
-            quant_echo(k)
-            if k < 14:
-                widen(1, QUART, HALF, VECTOR, (2 * k - 24, 2 * k - 23))
-        for c in range(CP):
-            quant_echo_pass(15, c)
-        quant_d_quarter(2, 0)
-        first_by_slot(3, 0, work[2], work[3])
-        interleave(0, QUART, HALF, SCALAR)
-        widen(0, HALF, N, SCALAR)
-        widen(1, HALF, HALF + QUART, SCALAR)
-        second_quarter(2, 0)
-        interleave(1, QUART, HALF, VECTOR)
-        quant_steer(0, QUART, HALF)
-        quant_steer(1, QUART, HALF)
-        gain(3, 0)
-        gain(3, 1)
-
-        step(0, 1, work[0], work[1])
-        gain_two(0, 1, 0)
-        quant_d_quarter(3, 0)
-        step(1, 1, work[2], work[3])
-        second_quarter(3, 0)
-        gain_two(0, 1, 1)
-        join(0, 1)
-        for j in range(2):
-            finish_quarter(j, 0)
-        step(2, 1, work[0], work[1])
-        gains_two(1, 1)
-        join(1, 1)
-        for j in range(2, OPEN):
-            finish_quarter(j, 0)
-        interleave(0, HALF, HALF + QUART, VECTOR)
-        quant_d_quarter(0, 1)
-        step(3, 1, work[2], work[3])
-        gains_two(2, 1)
-        join(2, 1)
-        widen(1, HALF + QUART, N, SCALAR)
         quant_d_quarter(1, 1)
-        for pairs in ((0, 1), (2, 3)):
-            second_quarter(0, 1, pairs)
-            second_quarter(1, 1, pairs)
-        gain_two(3, 1, 0)
-        interleave(1, HALF, HALF + QUART, VECTOR)
-        quant_steer(0, HALF, HALF + QUART)
-        quant_steer(1, HALF, HALF + QUART)
-        gain_two(3, 1, 1)
+        quant_echo(12)
+        quant_echo(13)
+        for k in (14, 15):
+            turn(k, k - 10)
+            empty(k)
+        gain_two(2, 0, 1)
+        gain_two(2, 1, 1)
+        second_open(1, 0)
+        join(2, 0)
+        join(2, 1)
+        quant_echo(14)
+        quant_echo(15)
+        widen(0, HALF, HALF + QUART, VECTOR, (2, 3))
+        first_two(3, 0, 0, 0)
+        first_two(3, 1, 0, 1)
+        first_two(3, 0, 1, 4)
+        first_two(3, 1, 1, 5)
+        widen(1, HALF, HALF + QUART, SCALAR)
+        interleave(0, HALF, HALF + QUART, SCALAR)
+        quant_d_quarter(2, 0)
         quant_d_quarter(2, 1)
-        join(3, 1)
-        for c in range(CP):
-            interleave(c, HALF + QUART, N, SCALAR)
+        second_open(2, 0)
+        gain_two(3, 0, 0)
+        gain_two(3, 1, 0)
+        gain_two(3, 0, 1)
+        join(3, 0)
+        gain_two(3, 1, 1)
+        quant_steer(0, HALF, HALF + QUART)
+        join(3, 1, VECTOR)
+        quant_d_quarter(3, 0)
+        quant_d_quarter(3, 1)
+        widen(0, HALF + QUART, N, SCALAR)
+        interleave(1, HALF, HALF + QUART, VECTOR)
+        widen(1, HALF + QUART, N, VECTOR, (0, 1))
+        quant_steer(1, HALF, HALF + QUART)
+        widen(1, HALF + QUART, N, VECTOR, (2, 3))
 
+        for i, k in ((4, 0), (5, 1), (6, 4)):
+            for g in range(G - 1):
+                second(i, g, 0, HALF, k)
+        interleave(0, HALF + QUART, N, VECTOR)
+        interleave(1, HALF + QUART, N, VECTOR)
+
+        def close(bands):
+            for i in bands:
+                second(i, G - 1, 0, HALF, None)
+                finish(i, 0, HALF, HALF)
+
+        close((4, 5, 6))
         steps = [(0, 2), (1, 2), (2, 2), (0, 3), (1, 3), (2, 3), (3, 2), (3, 3)]
         held = [(i, g) for g in range(G - 1) for i in range(OPEN)]
-        for step, (g, q) in enumerate(steps):
-            ka, kb = work[2 * (step % 2)], work[2 * (step % 2) + 1]
-            if step == len(steps) - 1:
+        work = (5, 0, 1, 4)
+        for n, (g, q) in enumerate(steps):
+            ka, kb = work[2 * (n % 2)], work[2 * (n % 2) + 1]
+            if n == len(steps) - 1:
                 first(g, 2 * q, ka)
                 first(g, 2 * q + 1, kb)
                 gain(g, 2 * q)
                 gain(g, 2 * q + 1)
-                quant_d_quarter(*steps[step - 1])
+                quant_d_quarter(*steps[n - 1])
                 quant_d(g, 2 * q, 2 * q + 1)
                 quant_d(g, 2 * q + 1, 2 * q + 2)
             else:
                 first_two(g, q, 0, ka)
                 first_two(g, q, 1, kb)
-                gain_two(g, q, 0)
-                if step == 0:
-                    quant_d_quarter(G - 1, 1)
-                gain_two(g, q, 1)
-                if step == 1:
+                gains_two(g, q)
+                if n == 0:
                     for c in range(CP):
                         quant_steer(c, HALF + QUART, N)
-                if step == 2:
-                    quant_d_quarter(*steps[0])
-                if step > 1:
-                    quant_d_quarter(*steps[step - 1])
+                if n > 0:
+                    quant_d_quarter(*steps[n - 1])
                 join(g, q)
-            if step < 4:
-                pairs = (2 * (step % 2), 2 * (step % 2) + 1)
-                second_quarter(G - 2 + step // 2, 1, pairs)
-                if step >= 2:
-                    for j in pairs:
-                        finish_quarter(j, 1)
-            elif step == len(steps) - 2:
+            if n < 2:
+                close((2 * n, 2 * n + 1))
+            elif n == 3:
+                whole_band(BANDS - 1, 0, HALF, sums[0])
+            elif n == len(steps) - 2:
                 for j in range(3):
                     i, held_g = held.pop(0)
-                    second(i, held_g, HALF, N, sum_banks[i])
+                    second(i, held_g, HALF, N, sums[(i + 1) % OPEN])
         for i, held_g in held[:-2]:
-            second(i, held_g, HALF, N, sum_banks[i])
+            second(i, held_g, HALF, N, sums[(i + 1) % OPEN])
         for i in range(OPEN):
             if (i, G - 2) in held[-2:]:
-                second(i, G - 2, HALF, N, sum_banks[i])
-            second(i, G - 1, HALF, N, sum_banks[i])
+                second(i, G - 2, HALF, N, None)
+            second(i, G - 1, HALF, N, None)
             finish(i, HALF, N, HALF)
         pieces = [(i, HALF, N) for i in range(OPEN, BANDS - 2)]
         pieces += [(BANDS - 2, HALF, HALF + QUART), (BANDS - 2, HALF + QUART, N), (BANDS - 1, HALF, HALF + QUART), (BANDS - 1, HALF + QUART, N - P), (BANDS - 1, N - P, N)]
-        for (i, n0, n1), k in zip(pieces, work + sum_banks):
-            for g in range(G):
-                second(i, g, n0, n1, k)
-            finish(i, n0, n1, n1 - n0)
+        for (i, n0, n1), k in zip(pieces, work + sums[1:]):
+            whole_band(i, n0, n1, k)

@@ -29,6 +29,7 @@ OPEN = 4
 LAST_SLOT = SLOTS - 1
 TWO_ONES = 0x3F803F80
 VECTOR, SCALAR = True, False
+ALONE = (0, 1, 2, 3, 6, 7)
 
 
 def tile_sonar_ping_coherence_s13_kernel(tc, echo, steer_bytes, steer_scale, ref_words, ref_scales, col_gain, row_gain, out):
@@ -52,9 +53,10 @@ def tile_sonar_ping_coherence_s13_kernel(tc, echo, steer_bytes, steer_scale, ref
         ecod = [kept([P, SLOTS * CP * P], U32, "ecod%d" % g) for g in range(G)]
         escl = [kept([P, SLOTS * CP * P], U8, "escl%d" % g) for g in range(G)]
         sscl = kept([P, CP, SLOTS], F32, "sscl")
-        sgrp = [kept([P, N, SLOTS], BF16, "sgrp%d" % c) for c in range(CP)]
-        scod = [kept([P, N], U32, "scod%d" % c) for c in range(CP)]
-        sqsc = [kept([P, N], U8, "sqsc%d" % c) for c in range(CP)]
+        swide = [kept([P, CP * SLOTS * QUART], BF16, "swide%d" % q) for q in range(N // QUART)]
+        sgrp = [kept([P, CP * QUART * SLOTS], BF16, "sgrp%d" % q) for q in range(N // QUART)]
+        scod = [kept([P, CP * QUART], U32, "scod%d" % q) for q in range(N // QUART)]
+        sqsc = [kept([P, CP * QUART], U8, "sqsc%d" % q) for q in range(N // QUART)]
         dcod = [kept([P, N], U32, "dcod%d" % g) for g in range(G)]
         dscl = [kept([P, N], U8, "dscl%d" % g) for g in range(G)]
         pcod = [kept([P, 2 * R], U8, "pcod%d" % g) for g in range(G)]
@@ -69,14 +71,14 @@ def tile_sonar_ping_coherence_s13_kernel(tc, echo, steer_bytes, steer_scale, ref
 
         echo_g = echo.rearrange("(g p t) k -> g p t k", p=P, t=SLOTS)
         steer_c = steer_bytes.rearrange("(c p t) n -> c p t n", p=P, t=SLOTS)
-        eraw, esort, xbank, egrp, epass, sraw, swide = {}, {}, {}, {}, {}, {}, {}
+        eraw, epiece, esort, xbank, egrp, epair, sraw = {}, {}, {}, {}, {}, {}, {}
         ybank, ytwo, dgrp, dtwo, band_sum = {}, {}, {}, {}, {}
 
         def load_echo(k0, k1):
-            tile = kept([P, k1 - k0, C], BF16, "eraw%d" % k0)
-            nc.sync.dma_start(out=tile[:], in_=echo_g[k0 // SLOTS][:, k0 % SLOTS : k0 % SLOTS + k1 - k0, :])
+            epiece[k0] = kept([P, (k1 - k0) * C], BF16, "eraw%d" % k0)
+            nc.sync.dma_start(out=epiece[k0][:], in_=echo_g[k0 // SLOTS][:, k0 % SLOTS : k0 % SLOTS + k1 - k0, :].rearrange("p t k -> p (t k)"))
             for k in range(k0, k1):
-                eraw[k] = tile[:, k - k0, :]
+                eraw[k] = epiece[k0][:, (k - k0) * C : (k - k0 + 1) * C]
 
         def load_steer(c, n0, n1):
             tile = kept([P, SLOTS, n1 - n0], U8, "sraw%d_%d" % (c, n0))
@@ -94,36 +96,36 @@ def tile_sonar_ping_coherence_s13_kernel(tc, echo, steer_bytes, steer_scale, ref
                     in_=ref_scales[g0:g1, r:16:4, :].rearrange("g a n -> a g n").bitcast(I32),
                 )
 
-        def widen(c, n0, n1, on_vector, slots=range(SLOTS)):
-            raw, base = sraw[(c, n0 // P)]
-            if (c, n0 // P) not in swide:
-                tile = kept([P, SLOTS, n1 - n0], BF16, "swide%d_%d" % (c, n0))
-                for b in range(n0 // P, n1 // P):
-                    swide[(c, b)] = (tile, n0)
-            wide = swide[(c, n0 // P)][0]
+        def widen(c, q, on_vector, slots=range(SLOTS)):
+            raw, base = sraw[(c, 2 * q)]
             for t in slots:
-                src = raw[:, t, n0 - base : n1 - base].bitcast(FP8)
+                src = raw[:, t, q * QUART - base : (q + 1) * QUART - base].bitcast(FP8)
+                dst = swide[q][:, (c * SLOTS + t) * QUART : (c * SLOTS + t + 1) * QUART]
                 if on_vector:
-                    nc.vector.tensor_scalar(out=wide[:, t, :], in0=src, scalar1=sscl[:, c, t : t + 1], scalar2=None, op0=MULT)
+                    nc.vector.tensor_scalar(out=dst, in0=src, scalar1=sscl[:, c, t : t + 1], scalar2=None, op0=MULT)
                 else:
-                    nc.scalar.activation(out=wide[:, t, :], in_=src, func=COPY, scale=sscl[:, c, t : t + 1])
+                    nc.scalar.activation(out=dst, in_=src, func=COPY, scale=sscl[:, c, t : t + 1])
 
-        def interleave(c, n0, n1, on_vector):
-            wide, base = swide[(c, n0 // P)]
+        def interleave(q, c0, c1, on_vector):
+            part = slice(c0 * SLOTS * QUART, c1 * SLOTS * QUART)
             copier(on_vector)(
-                out=sgrp[c][:, n0:n1, :].rearrange("p (n i) t -> p n t i", i=4),
-                in_=wide[:, :, n0 - base : n1 - base].rearrange("p t (n i) -> p n t i", i=4),
+                out=sgrp[q][:, part].rearrange("p (c n i t) -> p c n t i", c=c1 - c0, i=4, t=SLOTS),
+                in_=swide[q][:, part].rearrange("p (c t n i) -> p c n t i", c=c1 - c0, i=4, t=SLOTS),
             )
 
-        def quant_steer(c, n0, n1):
-            nc.vector.quantize_mx(out=scod[c][:, n0:n1].bitcast(FP8X4), scales=sqsc[c][:, n0:n1], in_=sgrp[c][:, n0:n1, :].rearrange("p n t -> p (n t)"))
+        def quant_steer(q, c0, c1):
+            cols = slice(c0 * QUART, c1 * QUART)
+            nc.vector.quantize_mx(out=scod[q][:, cols].bitcast(FP8X4), scales=sqsc[q][:, cols], in_=sgrp[q][:, c0 * SLOTS * QUART : c1 * SLOTS * QUART])
 
-        def sort_words(k, on_vector):
-            esort[k] = ring.tile([P, C // 2], F32, name="esort", tag="esort", align_bytes=256)
+        def sort_words(k, on_vector, count=1):
+            tile = ring.tile([P, count * C // 2], F32, name="esort%d" % count, tag="esort%d" % count, align_bytes=256, bufs=4 // count)
+            src = eraw[k] if count == 1 else epiece[k][:]
             copier(on_vector)(
-                out=esort[k][:].rearrange("p (c u m) -> p c u m", c=CP, u=2),
-                in_=eraw[k].bitcast(F32).rearrange("p (c m u) -> p c u m", c=CP, u=2),
+                out=tile[:].rearrange("p (c u m) -> p c u m", c=count * CP, u=2),
+                in_=src.bitcast(F32).rearrange("p (c m u) -> p c u m", c=count * CP, u=2),
             )
+            for j in range(count):
+                esort[k + j] = tile[:, j * C // 2 : (j + 1) * C // 2]
 
         def turn(k, kb):
             xbank[k] = bank(kb)
@@ -135,37 +137,33 @@ def tile_sonar_ping_coherence_s13_kernel(tc, echo, steer_bytes, steer_scale, ref
                     nc.tensor.transpose(xbank[k][:, j * P : (j + 1) * P], src, idf[:])
 
         def empty(k):
-            egrp[k] = ring.tile([P, C], BF16, name="egrp", tag="egrp", align_bytes=256)
+            if k in ALONE:
+                egrp[k] = ring.tile([P, C], BF16, name="egrp", tag="egrp", align_bytes=256, bufs=4)[:]
+            else:
+                if k % 2 == 0:
+                    epair[k] = ring.tile([P, 2 * C], BF16, name="epair", tag="epair", align_bytes=256, bufs=3)
+                egrp[k] = epair[k - k % 2][:, k % 2 * C : (k % 2 + 1) * C]
             nc.scalar.copy(
-                out=egrp[k][:].bitcast(F32).rearrange("p (c r u) -> p c r u", c=CP, u=2),
+                out=egrp[k].bitcast(F32).rearrange("p (c r u) -> p c r u", c=CP, u=2),
                 in_=xbank[k][:].rearrange("p (c u r) -> p c r u", c=CP, u=2),
             )
 
-        def empty_by_pass(k):
-            for c in range(CP):
-                epass[(k, c)] = ring.tile([P, HALF], BF16, name="epass", tag="epass", align_bytes=256)
-                nc.scalar.copy(
-                    out=epass[(k, c)][:].bitcast(F32).rearrange("p (r u) -> p r u", u=2),
-                    in_=xbank[k][:, 2 * P * c : 2 * P * (c + 1)].rearrange("p (u r) -> p r u", u=2),
-                )
-
-        def quant_echo_pass(k, c):
-            cols = slice((k % SLOTS * CP + c) * P, (k % SLOTS * CP + c + 1) * P)
-            nc.vector.quantize_mx(out=ecod[k // SLOTS][:, cols].bitcast(FP8X4), scales=escl[k // SLOTS][:, cols], in_=epass[(k, c)][:])
-
         def quant_echo(k):
-            cols = slice(k % SLOTS * CP * P, (k % SLOTS + 1) * CP * P)
-            nc.vector.quantize_mx(out=ecod[k // SLOTS][:, cols].bitcast(FP8X4), scales=escl[k // SLOTS][:, cols], in_=egrp[k][:])
+            src, count = (egrp[k], 1) if k in ALONE else (epair[k][:], 2)
+            cols = slice(k % SLOTS * CP * P, (k % SLOTS + count) * CP * P)
+            nc.vector.quantize_mx(out=ecod[k // SLOTS][:, cols].bitcast(FP8X4), scales=escl[k // SLOTS][:, cols], in_=src)
 
         def first_sum(dst, g, t, n0, n1):
             for c in range(CP):
                 ecols = slice((t * CP + c) * P, (t * CP + c + 1) * P)
+                q = n0 // QUART
+                scols = slice((c - q) * QUART + n0, (c - q) * QUART + n1)
                 nc.tensor.matmul_mx(
                     out=dst,
                     lhsT=ecod[g][:, ecols].bitcast(FP8X4),
                     lhsT_scale=escl[g][:, ecols],
-                    rhs=scod[c][:, n0:n1].bitcast(FP8X4),
-                    rhs_scale=sqsc[c][:, n0:n1],
+                    rhs=scod[q][:, scols].bitcast(FP8X4),
+                    rhs_scale=sqsc[q][:, scols],
                     start=(c == 0),
                     stop=(c == CP - 1),
                 )
@@ -179,15 +177,15 @@ def tile_sonar_ping_coherence_s13_kernel(tc, echo, steer_bytes, steer_scale, ref
             for t in range(SLOTS):
                 first_slot(g, b, t, k)
 
-        def d_tile(g, q):
-            if (g, q) not in dgrp:
-                dgrp[(g, q)] = ring.tile([P, QUART, SLOTS], BF16, name="dgrp", tag="dgrp", align_bytes=256)
-            return dgrp[(g, q)]
+        def d_cols(g, n0, n1):
+            h = n0 // HALF
+            if (g, h) not in dgrp:
+                dgrp[(g, h)] = ring.tile([P, HALF * SLOTS], BF16, name="dgrp", tag="dgrp", align_bytes=256, bufs=4)
+            return dgrp[(g, h)][:, (n0 - h * HALF) * SLOTS : (n1 - h * HALF) * SLOTS]
 
         def gain(g, b):
-            d = d_tile(g, b // 2)[:, (b % 2) * P : (b % 2 + 1) * P, :]
             nc.vector.tensor_tensor(
-                out=d.rearrange("p (n i) t -> p n t i", i=4),
+                out=d_cols(g, b * P, (b + 1) * P).rearrange("p (n i t) -> p n t i", i=4, t=SLOTS),
                 in0=ybank[(g, b)][:].rearrange("p (t n i) -> p n t i", t=SLOTS, i=4),
                 in1=cgain[:, b * P : (b + 1) * P].rearrange("p (n i) -> p n i", i=4).unsqueeze(2).to_broadcast([P, P // 4, SLOTS, 4]),
                 op=MULT,
@@ -210,17 +208,12 @@ def tile_sonar_ping_coherence_s13_kernel(tc, echo, steer_bytes, steer_scale, ref
 
         def join(g, q, on_vector=False):
             copier(on_vector)(
-                out=d_tile(g, q)[:].rearrange("p n t -> p (n t)").bitcast(F32).rearrange("p (n u) -> p n u", u=2),
+                out=d_cols(g, q * QUART, (q + 1) * QUART).bitcast(F32).rearrange("p (n u) -> p n u", u=2),
                 in_=dtwo[(g, q)][:].rearrange("p u n e -> p (u n e)").bitcast(F32).rearrange("p (u n) -> p n u", u=2),
             )
 
-        def quant_d(g, b0, b1):
-            src = dgrp[(g, b0 // 2)][:, (b0 % 2) * P : (b0 % 2 + b1 - b0) * P, :]
-            cols = slice(b0 * P, b1 * P)
-            nc.vector.quantize_mx(out=dcod[g][:, cols].bitcast(FP8X4), scales=dscl[g][:, cols], in_=src.rearrange("p n t -> p (n t)"))
-
-        def quant_d_quarter(g, q):
-            quant_d(g, 2 * q, 2 * q + 2)
+        def quant_d(g, n0, n1):
+            nc.vector.quantize_mx(out=dcod[g][:, n0:n1].bitcast(FP8X4), scales=dscl[g][:, n0:n1], in_=d_cols(g, n0, n1))
 
         def second_pass(dst, i, g, n0, n1, start, stop):
             nc.tensor.matmul_mx(
@@ -291,33 +284,31 @@ def tile_sonar_ping_coherence_s13_kernel(tc, echo, steer_bytes, steer_scale, ref
             gain_two(g, q, 1)
 
         warm(3, 7, ones[:, 0:HALF])
-        widen(0, 0, QUART, VECTOR)
-        warm(2, 7, swide[(0, 0)][0][:, 0:2, :].rearrange("p t n -> p (t n)"))
-        widen(0, QUART, HALF, SCALAR)
-        interleave(0, 0, QUART, VECTOR)
-        widen(1, 0, QUART, VECTOR, (0, 1))
-        widen(1, 0, QUART, SCALAR, (2, 3))
-        widen(1, QUART, HALF, SCALAR, (0, 1))
-        quant_steer(0, 0, QUART)
-        interleave(1, 0, QUART, VECTOR)
-        interleave(0, QUART, HALF, VECTOR)
-        quant_steer(1, 0, QUART)
+        widen(0, 0, VECTOR)
+        warm(2, 7, swide[0][:, 0:HALF])
+        widen(0, 1, SCALAR)
+        interleave(0, 0, 1, VECTOR)
+        widen(1, 0, VECTOR, (0, 1))
+        widen(1, 0, SCALAR, (2, 3))
+        widen(1, 1, SCALAR, (0, 1))
+        quant_steer(0, 0, 1)
+        interleave(0, 1, 2, VECTOR)
         gbank = bank(6)
         for k in range(SLOTS):
             turn(k, k)
-            if k == LAST_SLOT:
-                widen(1, QUART, HALF, SCALAR, (2, 3))
+            if k == LAST_SLOT - 1:
+                widen(1, 1, SCALAR, (2, 3))
                 nc.scalar.copy(out=idb[:], in_=idf[:, 0:BANDS])
             empty(k)
             if 0 < k < LAST_SLOT:
                 q = k - 1
                 nc.tensor.matmul(out=gbank[:, q * P : (q + 1) * P].bitcast(BF16), lhsT=ones[:, 0:P], rhs=gains[:, q * QUART : (q + 1) * QUART], start=True, stop=True)
+        nc.scalar.copy(out=cgain[:, 0:HALF], in_=gbank[:, 0:QUART].bitcast(BF16))
         quant_echo(0)
+        quant_steer(0, 1, 2)
         quant_echo(1)
-        nc.vector.tensor_copy(out=cgain[:, 0:HALF], in_=gbank[:, 0:QUART].bitcast(BF16))
-        quant_steer(0, QUART, HALF)
+        interleave(1, 0, CP, VECTOR)
         quant_echo(2)
-        interleave(1, QUART, HALF, VECTOR)
         quant_echo(3)
         first_two(0, 0, 0, 4)
         for k in (4, 5):
@@ -325,63 +316,54 @@ def tile_sonar_ping_coherence_s13_kernel(tc, echo, steer_bytes, steer_scale, ref
             empty(k)
         rbank = bank(7)
         nc.tensor.matmul(out=rbank[:, 0:BANDS], lhsT=gains[:, HALF : HALF + P], rhs=idb[:], start=True, stop=True)
-        quant_steer(1, QUART, HALF)
+        quant_steer(1, 0, CP)
         gain_two(0, 0, 0)
         nc.vector.tensor_copy(out=rgain[:], in_=rbank[:, 0:BANDS])
         first_two(0, 0, 1, 5)
         first_two(0, 1, 0, 6)
         first_two(0, 1, 1, 7)
-        quant_echo(4)
-        sort_words(6, VECTOR)
         for k in range(7, 10):
             sort_words(k, SCALAR)
-        quant_echo(5)
         gain_two(0, 0, 1)
+        join(0, 0)
+        quant_echo(4)
         gain_two(0, 1, 0)
         gain_two(0, 1, 1)
         for k, kb in zip(range(6, 10), (2, 3, 0, 1)):
             turn(k, kb)
             empty(k)
         quant_echo(6)
-        sort_words(10, VECTOR)
         quant_echo(7)
-        sort_words(11, VECTOR)
+        sort_words(10, VECTOR, 2)
         for u in range(2):
             for q in range(2):
                 first_two(1, q, u, 4 + 2 * u + q)
         sort_words(12, SCALAR)
         sort_words(13, SCALAR)
-        join(0, 0)
+        join(0, 1)
         gain_two(1, 0, 0)
         quant_echo(8)
         gain_two(1, 1, 0)
-        quant_echo(9)
         for k, kb in zip(range(10, 14), (2, 3, 0, 1)):
             turn(k, kb)
             empty(k)
-        join(0, 1, VECTOR)
         gain_two(1, 0, 1)
-        quant_d_quarter(0, 0)
-        quant_d_quarter(0, 1)
+        quant_d(0, 0, HALF)
         gain_two(1, 1, 1)
+        quant_echo(10)
         first_two(2, 0, 0, 4)
         first_two(2, 1, 0, 5)
-        quant_echo(10)
-        quant_echo(11)
         second_open(0, 0)
         join(1, 0)
         sort_words(14, SCALAR)
-        sort_words(15, SCALAR)
-        widen(0, HALF, HALF + QUART, SCALAR, (0, 1))
-        join(1, 1, VECTOR)
+        join(1, 1)
+        widen(0, 2, SCALAR)
         gain_two(2, 0, 0)
         gain_two(2, 1, 0)
         first_two(2, 0, 1, 0)
         first_two(2, 1, 1, 1)
-        quant_d_quarter(1, 0)
-        quant_d_quarter(1, 1)
+        quant_d(1, 0, HALF)
         quant_echo(12)
-        quant_echo(13)
         for k in (14, 15):
             turn(k, k - 10)
             empty(k)
@@ -391,37 +373,29 @@ def tile_sonar_ping_coherence_s13_kernel(tc, echo, steer_bytes, steer_scale, ref
         join(2, 0)
         join(2, 1)
         quant_echo(14)
-        quant_echo(15)
-        widen(0, HALF, HALF + QUART, VECTOR, (2, 3))
-        first_two(3, 0, 0, 0)
-        first_two(3, 1, 0, 1)
-        first_two(3, 0, 1, 4)
-        first_two(3, 1, 1, 5)
-        widen(1, HALF, HALF + QUART, SCALAR)
-        interleave(0, HALF, HALF + QUART, SCALAR)
-        quant_d_quarter(2, 0)
-        quant_d_quarter(2, 1)
-        second_open(2, 0)
+        for u in range(2):
+            first_two(3, 0, u, 4 * u)
+            for b in (2, 3):
+                for t in (2 * u, 2 * u + 1):
+                    first_slot(3, b, t, (1, 5)[b - 2])
+        widen(1, 2, SCALAR)
+        interleave(2, 0, 1, SCALAR)
         gain_two(3, 0, 0)
-        gain_two(3, 1, 0)
+        quant_d(2, 0, HALF)
+        second_open(2, 0)
         gain_two(3, 0, 1)
         join(3, 0)
-        gain_two(3, 1, 1)
-        quant_steer(0, HALF, HALF + QUART)
-        join(3, 1, VECTOR)
-        quant_d_quarter(3, 0)
-        quant_d_quarter(3, 1)
-        widen(0, HALF + QUART, N, SCALAR)
-        interleave(1, HALF, HALF + QUART, VECTOR)
-        widen(1, HALF + QUART, N, VECTOR, (0, 1))
-        quant_steer(1, HALF, HALF + QUART)
-        widen(1, HALF + QUART, N, VECTOR, (2, 3))
+        gain(3, 2)
+        gain(3, 3)
+        interleave(2, 1, 2, VECTOR)
+        quant_d(3, 0, HALF)
+        quant_steer(2, 0, CP)
+        widen(0, 3, SCALAR)
+        widen(1, 3, SCALAR)
 
-        for i, k in ((4, 0), (5, 1), (6, 4)):
+        for i, k in ((4, 0), (5, 4), (6, 1)):
             for g in range(G - 1):
                 second(i, g, 0, HALF, k)
-        interleave(0, HALF + QUART, N, VECTOR)
-        interleave(1, HALF + QUART, N, VECTOR)
 
         def close(bands):
             for i in bands:
@@ -429,9 +403,10 @@ def tile_sonar_ping_coherence_s13_kernel(tc, echo, steer_bytes, steer_scale, ref
                 finish(i, 0, HALF, HALF)
 
         close((4, 5, 6))
+        interleave(3, 0, CP, VECTOR)
         steps = [(0, 2), (1, 2), (2, 2), (0, 3), (1, 3), (2, 3), (3, 2), (3, 3)]
         held = [(i, g) for g in range(G - 1) for i in range(OPEN)]
-        work = (5, 0, 1, 4)
+        work = (5, 0, 4, 1)
         for n, (g, q) in enumerate(steps):
             ka, kb = work[2 * (n % 2)], work[2 * (n % 2) + 1]
             if n == len(steps) - 1:
@@ -439,25 +414,27 @@ def tile_sonar_ping_coherence_s13_kernel(tc, echo, steer_bytes, steer_scale, ref
                 first(g, 2 * q + 1, kb)
                 gain(g, 2 * q)
                 gain(g, 2 * q + 1)
-                quant_d_quarter(*steps[n - 1])
-                quant_d(g, 2 * q, 2 * q + 1)
-                quant_d(g, 2 * q + 1, 2 * q + 2)
+                quant_d(g, HALF, HALF + QUART)
+                quant_d(g, HALF + QUART, N)
             else:
                 first_two(g, q, 0, ka)
-                first_two(g, q, 1, kb)
-                gains_two(g, q)
                 if n == 0:
-                    for c in range(CP):
-                        quant_steer(c, HALF + QUART, N)
+                    close((0,))
+                first_two(g, q, 1, kb)
+                gain_two(g, q, 0)
+                if n == 0:
+                    quant_steer(3, 0, CP)
+                gain_two(g, q, 1)
                 if n > 0:
-                    quant_d_quarter(*steps[n - 1])
+                    last_g, last_q = steps[n - 1]
+                    quant_d(last_g, last_q * QUART, (last_q + 1) * QUART)
                 join(g, q)
-            if n < 2:
-                close((2 * n, 2 * n + 1))
+            if n < 3:
+                close((n + 1,))
             elif n == 3:
                 whole_band(BANDS - 1, 0, HALF, sums[0])
             elif n == len(steps) - 2:
-                for j in range(3):
+                for j in range(2):
                     i, held_g = held.pop(0)
                     second(i, held_g, HALF, N, sums[(i + 1) % OPEN])
         for i, held_g in held[:-2]:

@@ -29,7 +29,7 @@ OPEN = 4
 LAST_SLOT = SLOTS - 1
 TWO_ONES = 0x3F803F80
 VECTOR, SCALAR = True, False
-ALONE = (0, 1, 2, 3, 6, 7)
+ALONE = (0, 1, 2, 3, 6, 7, 10, 11)
 
 
 def tile_sonar_ping_coherence_s13_kernel(tc, echo, steer_bytes, steer_scale, ref_words, ref_scales, col_gain, row_gain, out):
@@ -268,7 +268,7 @@ def tile_sonar_ping_coherence_s13_kernel(tc, echo, steer_bytes, steer_scale, ref
         nc.sync.dma_start(out=cgain[:, HALF:N], in_=col_gain[HALF:N].partition_broadcast(P))
         load_words(3)
 
-        sums = (2, 3, 6, 7)
+        sums = (2, 0, 6, 7)
 
         def second_open(g, n0):
             for i in range(OPEN):
@@ -286,29 +286,31 @@ def tile_sonar_ping_coherence_s13_kernel(tc, echo, steer_bytes, steer_scale, ref
         warm(3, 7, ones[:, 0:HALF])
         widen(0, 0, VECTOR)
         warm(2, 7, swide[0][:, 0:HALF])
-        widen(0, 1, SCALAR)
-        interleave(0, 0, 1, VECTOR)
+        widen(0, 1, SCALAR, (0, 1))
         widen(1, 0, VECTOR, (0, 1))
         widen(1, 0, SCALAR, (2, 3))
+        widen(0, 1, SCALAR, (2, 3))
         widen(1, 1, SCALAR, (0, 1))
-        quant_steer(0, 0, 1)
+        interleave(0, 0, 1, VECTOR)
         interleave(0, 1, 2, VECTOR)
+        interleave(1, 0, 1, VECTOR)
+        quant_steer(0, 0, CP)
         gbank = bank(6)
         for k in range(SLOTS):
             turn(k, k)
-            if k == LAST_SLOT - 1:
+            if k == LAST_SLOT:
                 widen(1, 1, SCALAR, (2, 3))
-                nc.scalar.copy(out=idb[:], in_=idf[:, 0:BANDS])
             empty(k)
             if 0 < k < LAST_SLOT:
                 q = k - 1
                 nc.tensor.matmul(out=gbank[:, q * P : (q + 1) * P].bitcast(BF16), lhsT=ones[:, 0:P], rhs=gains[:, q * QUART : (q + 1) * QUART], start=True, stop=True)
         nc.scalar.copy(out=cgain[:, 0:HALF], in_=gbank[:, 0:QUART].bitcast(BF16))
+        nc.scalar.copy(out=idb[:], in_=idf[:, 0:BANDS])
         quant_echo(0)
-        quant_steer(0, 1, 2)
         quant_echo(1)
-        interleave(1, 0, CP, VECTOR)
         quant_echo(2)
+        quant_steer(1, 0, 1)
+        interleave(1, 1, 2, VECTOR)
         quant_echo(3)
         first_two(0, 0, 0, 4)
         for k in (4, 5):
@@ -316,51 +318,55 @@ def tile_sonar_ping_coherence_s13_kernel(tc, echo, steer_bytes, steer_scale, ref
             empty(k)
         rbank = bank(7)
         nc.tensor.matmul(out=rbank[:, 0:BANDS], lhsT=gains[:, HALF : HALF + P], rhs=idb[:], start=True, stop=True)
-        quant_steer(1, 0, CP)
-        gain_two(0, 0, 0)
+        quant_steer(1, 1, 2)
         nc.vector.tensor_copy(out=rgain[:], in_=rbank[:, 0:BANDS])
+        gain_two(0, 0, 0)
         first_two(0, 0, 1, 5)
         first_two(0, 1, 0, 6)
         first_two(0, 1, 1, 7)
-        for k in range(7, 10):
-            sort_words(k, SCALAR)
-        gain_two(0, 0, 1)
-        join(0, 0)
+        sort_words(6, SCALAR)
+        sort_words(7, SCALAR)
+        sort_words(8, VECTOR, 2)
+        sort_words(10, SCALAR)
         quant_echo(4)
+        gain_two(0, 0, 1)
         gain_two(0, 1, 0)
         gain_two(0, 1, 1)
-        for k, kb in zip(range(6, 10), (2, 3, 0, 1)):
+        for k, kb in zip((6, 8, 7, 9), (2, 3, 0, 1)):
             turn(k, kb)
+        for k in range(6, 10):
             empty(k)
         quant_echo(6)
         quant_echo(7)
-        sort_words(10, VECTOR, 2)
+        sort_words(11, VECTOR)
         for u in range(2):
             for q in range(2):
                 first_two(1, q, u, 4 + 2 * u + q)
         sort_words(12, SCALAR)
         sort_words(13, SCALAR)
         join(0, 1)
+        join(0, 0, VECTOR)
         gain_two(1, 0, 0)
         quant_echo(8)
         gain_two(1, 1, 0)
-        for k, kb in zip(range(10, 14), (2, 3, 0, 1)):
+        for k, kb in zip(range(10, 14), (2, 0, 3, 1)):
             turn(k, kb)
             empty(k)
         gain_two(1, 0, 1)
         quant_d(0, 0, HALF)
         gain_two(1, 1, 1)
         quant_echo(10)
+        quant_echo(11)
         first_two(2, 0, 0, 4)
         first_two(2, 1, 0, 5)
         second_open(0, 0)
         join(1, 0)
-        sort_words(14, SCALAR)
         join(1, 1)
+        sort_words(15, SCALAR)
         widen(0, 2, SCALAR)
         gain_two(2, 0, 0)
         gain_two(2, 1, 0)
-        first_two(2, 0, 1, 0)
+        first_two(2, 0, 1, 3)
         first_two(2, 1, 1, 1)
         quant_d(1, 0, HALF)
         quant_echo(12)
@@ -374,7 +380,7 @@ def tile_sonar_ping_coherence_s13_kernel(tc, echo, steer_bytes, steer_scale, ref
         join(2, 1)
         quant_echo(14)
         for u in range(2):
-            first_two(3, 0, u, 4 * u)
+            first_two(3, 0, u, 3 + u)
             for b in (2, 3):
                 for t in (2 * u, 2 * u + 1):
                     first_slot(3, b, t, (1, 5)[b - 2])
@@ -393,7 +399,7 @@ def tile_sonar_ping_coherence_s13_kernel(tc, echo, steer_bytes, steer_scale, ref
         widen(0, 3, SCALAR)
         widen(1, 3, SCALAR)
 
-        for i, k in ((4, 0), (5, 4), (6, 1)):
+        for i, k in ((4, 3), (5, 4), (6, 1)):
             for g in range(G - 1):
                 second(i, g, 0, HALF, k)
 
@@ -406,7 +412,7 @@ def tile_sonar_ping_coherence_s13_kernel(tc, echo, steer_bytes, steer_scale, ref
         interleave(3, 0, CP, VECTOR)
         steps = [(0, 2), (1, 2), (2, 2), (0, 3), (1, 3), (2, 3), (3, 2), (3, 3)]
         held = [(i, g) for g in range(G - 1) for i in range(OPEN)]
-        work = (5, 0, 4, 1)
+        work = (5, 3, 4, 1)
         for n, (g, q) in enumerate(steps):
             ka, kb = work[2 * (n % 2)], work[2 * (n % 2) + 1]
             if n == len(steps) - 1:

@@ -244,7 +244,7 @@ def tile_sonar_ping_coherence_s13_kernel(tc, echo, steer_bytes, steer_scale, ref
 
         nc.scalar.dma_start(out=sscl[:], in_=steer_scale.rearrange("(c p t) o -> p c (t o)", p=P, t=SLOTS))
         nc.vector.memset(ones[:].bitcast(I32), TWO_ONES)
-        nc.gpsimd.memset(gains[:].bitcast(I32), 0)
+        nc.vector.memset(gains[:].bitcast(I32), 0)
         nc.scalar.activation(out=table_warm[:], in_=ones[:, 0:1], func=SQUARE)
         make_identity(nc, idf[:])
         nc.vector.memset(pscl[:].rearrange("p g n -> p (g n)").bitcast(I32), 0)
@@ -285,9 +285,11 @@ def tile_sonar_ping_coherence_s13_kernel(tc, echo, steer_bytes, steer_scale, ref
 
         warm(3, 7, ones[:, 0:HALF])
         widen(0, 0, VECTOR)
-        warm(2, 7, swide[0][:, 0:HALF])
+        warm(1, 7, swide[0][:, 0:HALF])
+        nc.scalar.copy(out=idb[:], in_=idf[:, 0:BANDS])
         widen(0, 1, SCALAR, (0, 1))
         widen(1, 0, VECTOR, (0, 1))
+        warm(1, 7, swide[0][:, LAST_SLOT * QUART : (LAST_SLOT + 2) * QUART])
         widen(1, 0, SCALAR, (2, 3))
         widen(0, 1, SCALAR, (2, 3))
         widen(1, 1, SCALAR, (0, 1))
@@ -299,17 +301,18 @@ def tile_sonar_ping_coherence_s13_kernel(tc, echo, steer_bytes, steer_scale, ref
         for k in range(SLOTS):
             turn(k, k)
             if k == LAST_SLOT:
-                widen(1, 1, SCALAR, (2, 3))
+                widen(1, 1, SCALAR, (2,))
             empty(k)
-            if 0 < k < LAST_SLOT:
-                q = k - 1
-                nc.tensor.matmul(out=gbank[:, q * P : (q + 1) * P].bitcast(BF16), lhsT=ones[:, 0:P], rhs=gains[:, q * QUART : (q + 1) * QUART], start=True, stop=True)
+            if k == 1:
+                nc.tensor.matmul(out=gbank[:, 0:QUART].bitcast(BF16), lhsT=ones[:, 0:P], rhs=gains[:, 0:HALF], start=True, stop=True)
+            if k == 2:
+                warm(1, 7, ones[:, 0:HALF])
         nc.scalar.copy(out=cgain[:, 0:HALF], in_=gbank[:, 0:QUART].bitcast(BF16))
-        nc.scalar.copy(out=idb[:], in_=idf[:, 0:BANDS])
         quant_echo(0)
         quant_echo(1)
-        quant_echo(2)
+        widen(1, 1, VECTOR, (3,))
         quant_steer(1, 0, 1)
+        quant_echo(2)
         interleave(1, 1, 2, VECTOR)
         quant_echo(3)
         first_two(0, 0, 0, 4)
@@ -352,8 +355,8 @@ def tile_sonar_ping_coherence_s13_kernel(tc, echo, steer_bytes, steer_scale, ref
         for k, kb in zip(range(10, 14), (2, 0, 3, 1)):
             turn(k, kb)
             empty(k)
-        gain_two(1, 0, 1)
         quant_d(0, 0, HALF)
+        gain_two(1, 0, 1)
         gain_two(1, 1, 1)
         quant_echo(10)
         quant_echo(11)
@@ -363,7 +366,7 @@ def tile_sonar_ping_coherence_s13_kernel(tc, echo, steer_bytes, steer_scale, ref
         join(1, 0)
         join(1, 1)
         sort_words(15, SCALAR)
-        widen(0, 2, SCALAR)
+        widen(0, 2, SCALAR, range(LAST_SLOT))
         gain_two(2, 0, 0)
         gain_two(2, 1, 0)
         first_two(2, 0, 1, 3)
@@ -378,6 +381,7 @@ def tile_sonar_ping_coherence_s13_kernel(tc, echo, steer_bytes, steer_scale, ref
         second_open(1, 0)
         join(2, 0)
         join(2, 1)
+        widen(0, 2, SCALAR, (LAST_SLOT,))
         quant_echo(14)
         for u in range(2):
             first_two(3, 0, u, 3 + u)

@@ -243,9 +243,9 @@ def tile_sonar_ping_coherence_s13_kernel(tc, echo, steer_bytes, steer_scale, ref
                 nc.tensor.matmul(out=scratch[:], lhsT=ones[:, 0:P], rhs=moving, start=True, stop=True)
 
         nc.scalar.dma_start(out=sscl[:], in_=steer_scale.rearrange("(c p t) o -> p c (t o)", p=P, t=SLOTS))
-        nc.vector.memset(ones[:].bitcast(I32), TWO_ONES)
         nc.vector.memset(gains[:].bitcast(I32), 0)
-        nc.scalar.activation(out=table_warm[:], in_=ones[:, 0:1], func=SQUARE)
+        nc.vector.memset(ones[:].bitcast(I32), TWO_ONES)
+        nc.scalar.activation(out=table_warm[:], in_=gains[:, HALF + P : HALF + P + 1], func=SQUARE)
         make_identity(nc, idf[:])
         nc.vector.memset(pscl[:].rearrange("p g n -> p (g n)").bitcast(I32), 0)
 
@@ -268,7 +268,7 @@ def tile_sonar_ping_coherence_s13_kernel(tc, echo, steer_bytes, steer_scale, ref
         nc.sync.dma_start(out=cgain[:, HALF:N], in_=col_gain[HALF:N].partition_broadcast(P))
         load_words(3)
 
-        sums = (2, 0, 6, 7)
+        sums = (0, 3, 6, 2)
 
         def second_open(g, n0):
             for i in range(OPEN):
@@ -287,12 +287,13 @@ def tile_sonar_ping_coherence_s13_kernel(tc, echo, steer_bytes, steer_scale, ref
         widen(0, 0, VECTOR)
         warm(1, 7, swide[0][:, 0:HALF])
         nc.scalar.copy(out=idb[:], in_=idf[:, 0:BANDS])
-        widen(0, 1, SCALAR, (0, 1))
+        widen(0, 1, VECTOR, (0,))
+        widen(0, 1, SCALAR, (1, 2))
         widen(1, 0, VECTOR, (0, 1))
         warm(1, 7, swide[0][:, LAST_SLOT * QUART : (LAST_SLOT + 2) * QUART])
         widen(1, 0, SCALAR, (2, 3))
-        widen(0, 1, SCALAR, (2, 3))
-        widen(1, 1, SCALAR, (0, 1))
+        widen(0, 1, SCALAR, (3,))
+        widen(1, 1, SCALAR, (0, 1, 2))
         interleave(0, 0, 1, VECTOR)
         interleave(0, 1, 2, VECTOR)
         interleave(1, 0, 1, VECTOR)
@@ -301,28 +302,26 @@ def tile_sonar_ping_coherence_s13_kernel(tc, echo, steer_bytes, steer_scale, ref
         for k in range(SLOTS):
             turn(k, k)
             if k == LAST_SLOT:
-                widen(1, 1, SCALAR, (2,))
+                widen(1, 1, SCALAR, (3,))
             empty(k)
             if k == 1:
                 nc.tensor.matmul(out=gbank[:, 0:QUART].bitcast(BF16), lhsT=ones[:, 0:P], rhs=gains[:, 0:HALF], start=True, stop=True)
             if k == 2:
                 warm(1, 7, ones[:, 0:HALF])
-        nc.scalar.copy(out=cgain[:, 0:HALF], in_=gbank[:, 0:QUART].bitcast(BF16))
         quant_echo(0)
         quant_echo(1)
-        widen(1, 1, VECTOR, (3,))
         quant_steer(1, 0, 1)
         quant_echo(2)
         interleave(1, 1, 2, VECTOR)
         quant_echo(3)
         first_two(0, 0, 0, 4)
+        nc.tensor.matmul(out=gbank[:, QUART : QUART + BANDS], lhsT=gains[:, HALF : HALF + P], rhs=idb[:], start=True, stop=True)
+        nc.scalar.copy(out=cgain[:, 0:HALF], in_=gbank[:, 0:QUART].bitcast(BF16))
+        nc.scalar.copy(out=rgain[:], in_=gbank[:, QUART : QUART + BANDS])
         for k in (4, 5):
             turn(k, k - 4)
             empty(k)
-        rbank = bank(7)
-        nc.tensor.matmul(out=rbank[:, 0:BANDS], lhsT=gains[:, HALF : HALF + P], rhs=idb[:], start=True, stop=True)
         quant_steer(1, 1, 2)
-        nc.vector.tensor_copy(out=rgain[:], in_=rbank[:, 0:BANDS])
         gain_two(0, 0, 0)
         first_two(0, 0, 1, 5)
         first_two(0, 1, 0, 6)
@@ -334,25 +333,25 @@ def tile_sonar_ping_coherence_s13_kernel(tc, echo, steer_bytes, steer_scale, ref
         quant_echo(4)
         gain_two(0, 0, 1)
         gain_two(0, 1, 0)
-        gain_two(0, 1, 1)
+        join(0, 0, VECTOR)
         for k, kb in zip((6, 8, 7, 9), (2, 3, 0, 1)):
             turn(k, kb)
         for k in range(6, 10):
             empty(k)
         quant_echo(6)
-        quant_echo(7)
         sort_words(11, VECTOR)
+        quant_echo(7)
+        gain_two(0, 1, 1)
         for u in range(2):
             for q in range(2):
-                first_two(1, q, u, 4 + 2 * u + q)
+                first_two(1, q, u, (4, 5, 6, 2)[2 * u + q])
         sort_words(12, SCALAR)
         sort_words(13, SCALAR)
         join(0, 1)
-        join(0, 0, VECTOR)
         gain_two(1, 0, 0)
         quant_echo(8)
         gain_two(1, 1, 0)
-        for k, kb in zip(range(10, 14), (2, 0, 3, 1)):
+        for k, kb in zip(range(10, 14), (0, 3, 1, 7)):
             turn(k, kb)
             empty(k)
         quant_d(0, 0, HALF)
@@ -369,8 +368,8 @@ def tile_sonar_ping_coherence_s13_kernel(tc, echo, steer_bytes, steer_scale, ref
         widen(0, 2, SCALAR, range(LAST_SLOT))
         gain_two(2, 0, 0)
         gain_two(2, 1, 0)
-        first_two(2, 0, 1, 3)
-        first_two(2, 1, 1, 1)
+        first_two(2, 0, 1, 1)
+        first_two(2, 1, 1, 7)
         quant_d(1, 0, HALF)
         quant_echo(12)
         for k in (14, 15):
@@ -384,26 +383,29 @@ def tile_sonar_ping_coherence_s13_kernel(tc, echo, steer_bytes, steer_scale, ref
         widen(0, 2, SCALAR, (LAST_SLOT,))
         quant_echo(14)
         for u in range(2):
-            first_two(3, 0, u, 3 + u)
-            for b in (2, 3):
-                for t in (2 * u, 2 * u + 1):
-                    first_slot(3, b, t, (1, 5)[b - 2])
+            for q in range(2):
+                first_two(3, q, u, (1, 7, 4, 5)[2 * u + q])
         widen(1, 2, SCALAR)
         interleave(2, 0, 1, SCALAR)
         gain_two(3, 0, 0)
         quant_d(2, 0, HALF)
+        for g in range(2):
+            second(4, g, 0, HALF, 1)
         second_open(2, 0)
+        second(4, 2, 0, HALF, None)
+        gain_two(3, 1, 0)
         gain_two(3, 0, 1)
         join(3, 0)
-        gain(3, 2)
-        gain(3, 3)
+        gain_two(3, 1, 1)
         interleave(2, 1, 2, VECTOR)
+        join(3, 1, VECTOR)
         quant_d(3, 0, HALF)
         quant_steer(2, 0, CP)
         widen(0, 3, SCALAR)
-        widen(1, 3, SCALAR)
+        widen(1, 3, SCALAR, (0, 1))
+        widen(1, 3, VECTOR, (2, 3))
 
-        for i, k in ((4, 3), (5, 4), (6, 1)):
+        for i, k in ((5, 7), (6, 4)):
             for g in range(G - 1):
                 second(i, g, 0, HALF, k)
 
@@ -416,7 +418,7 @@ def tile_sonar_ping_coherence_s13_kernel(tc, echo, steer_bytes, steer_scale, ref
         interleave(3, 0, CP, VECTOR)
         steps = [(0, 2), (1, 2), (2, 2), (0, 3), (1, 3), (2, 3), (3, 2), (3, 3)]
         held = [(i, g) for g in range(G - 1) for i in range(OPEN)]
-        work = (5, 3, 4, 1)
+        work = (5, 1, 7, 4)
         for n, (g, q) in enumerate(steps):
             ka, kb = work[2 * (n % 2)], work[2 * (n % 2) + 1]
             if n == len(steps) - 1:

@@ -326,44 +326,46 @@ def tile_sonar_ping_coherence_s13_kernel(tc, echo, steer_bytes, steer_scale, ref
         first_two(0, 0, 1, 5)
         first_two(0, 1, 0, 6)
         first_two(0, 1, 1, 7)
-        sort_words(6, SCALAR)
-        sort_words(7, SCALAR)
-        sort_words(8, VECTOR, 2)
-        sort_words(10, SCALAR)
-        quant_echo(4)
+        sort_words(6, VECTOR)
+        for k in range(7, 10):
+            sort_words(k, SCALAR)
         gain_two(0, 0, 1)
+        quant_echo(4)
         gain_two(0, 1, 0)
-        join(0, 0, VECTOR)
-        for k, kb in zip((6, 8, 7, 9), (2, 3, 0, 1)):
+        for k, kb in zip(range(6, 10), (2, 0, 3, 1)):
             turn(k, kb)
         for k in range(6, 10):
             empty(k)
+        sort_words(10, VECTOR)
         quant_echo(6)
         sort_words(11, VECTOR)
         quant_echo(7)
         gain_two(0, 1, 1)
+        join(0, 0, VECTOR)
         for u in range(2):
-            for q in range(2):
-                first_two(1, q, u, (4, 5, 6, 2)[2 * u + q])
+            first_two(1, 0, u, (4, 6)[u])
+            for b in (2, 3):
+                for t in (2 * u, 2 * u + 1):
+                    first_slot(1, b, t, (5, 2)[b - 2])
         sort_words(12, SCALAR)
         sort_words(13, SCALAR)
         join(0, 1)
         gain_two(1, 0, 0)
         quant_echo(8)
-        gain_two(1, 1, 0)
+        gain(1, 2)
         for k, kb in zip(range(10, 14), (0, 3, 1, 7)):
             turn(k, kb)
             empty(k)
         quant_d(0, 0, HALF)
         gain_two(1, 0, 1)
-        gain_two(1, 1, 1)
+        gain(1, 3)
         quant_echo(10)
         quant_echo(11)
         first_two(2, 0, 0, 4)
         first_two(2, 1, 0, 5)
         second_open(0, 0)
         join(1, 0)
-        join(1, 1)
+        sort_words(14, SCALAR)
         sort_words(15, SCALAR)
         widen(0, 2, SCALAR, range(LAST_SLOT))
         gain_two(2, 0, 0)
@@ -399,7 +401,8 @@ def tile_sonar_ping_coherence_s13_kernel(tc, echo, steer_bytes, steer_scale, ref
         gain_two(3, 1, 1)
         interleave(2, 1, 2, VECTOR)
         join(3, 1, VECTOR)
-        quant_d(3, 0, HALF)
+        quant_d(3, 0, QUART)
+        quant_d(3, QUART, HALF)
         quant_steer(2, 0, CP)
         widen(0, 3, SCALAR)
         widen(1, 3, SCALAR, (0, 1))

@@ -61,10 +61,10 @@ def tile_sonar_ping_coherence_s13_kernel(tc, echo, steer_bytes, steer_scale, ref
         dscl = [kept([P, N], U8, "dscl%d" % g) for g in range(G)]
         pcod = [kept([P, 2 * R], U8, "pcod%d" % g) for g in range(G)]
         pscl = kept([P, G, R], U8, "pscl")
-        gains = kept([P, HALF + P + 2], BF16, "gains")
+        gains = kept([P, HALF + 2], BF16, "gains")
         ones = kept([P, HALF + 2], BF16, "ones")
         idf = kept([P, P], F32, "idf")
-        idb = kept([P, BANDS], BF16, "idb")
+        rraw = kept([P, BANDS, 2], BF16, "rraw")
         cgain = kept([P, N], BF16, "cgain")
         table_warm = kept([P, 1], F32, "table_warm")
         rgain = kept([P, BANDS], F32, "rgain")
@@ -245,7 +245,7 @@ def tile_sonar_ping_coherence_s13_kernel(tc, echo, steer_bytes, steer_scale, ref
         nc.scalar.dma_start(out=sscl[:], in_=steer_scale.rearrange("(c p t) o -> p c (t o)", p=P, t=SLOTS))
         nc.vector.memset(gains[:].bitcast(I32), 0)
         nc.vector.memset(ones[:].bitcast(I32), TWO_ONES)
-        nc.scalar.activation(out=table_warm[:], in_=gains[:, HALF + P : HALF + P + 1], func=SQUARE)
+        nc.scalar.activation(out=table_warm[:], in_=gains[:, HALF : HALF + 1], func=SQUARE)
         make_identity(nc, idf[:])
         nc.vector.memset(pscl[:].rearrange("p g n -> p (g n)").bitcast(I32), 0)
 
@@ -256,7 +256,6 @@ def tile_sonar_ping_coherence_s13_kernel(tc, echo, steer_bytes, steer_scale, ref
             load_echo(k, k + 1)
             if k == 1:
                 nc.sync.dma_start(out=gains[0:1, 0:HALF], in_=col_gain[0:HALF].unsqueeze(0))
-        nc.scalar.dma_start(out=gains[0:BANDS, HALF : HALF + P], in_=row_gain.rearrange("(i m) -> i m", m=P))
         for k in range(4, 16, 2):
             load_echo(k, k + 2)
         load_scales(0, G)
@@ -267,6 +266,8 @@ def tile_sonar_ping_coherence_s13_kernel(tc, echo, steer_bytes, steer_scale, ref
         load_words(2)
         nc.sync.dma_start(out=cgain[:, HALF:N], in_=col_gain[HALF:N].partition_broadcast(P))
         load_words(3)
+        with nc.allow_non_contiguous_dma(reason="one gain for each partition and band"):
+            nc.sync.dma_start(out=rraw[:, :, 0:1], in_=row_gain.rearrange("(i p o) -> p i o", p=P, o=1))
 
         sums = (0, 3, 6, 2)
 
@@ -286,48 +287,44 @@ def tile_sonar_ping_coherence_s13_kernel(tc, echo, steer_bytes, steer_scale, ref
         warm(3, 7, ones[:, 0:HALF])
         widen(0, 0, VECTOR)
         warm(1, 7, swide[0][:, 0:HALF])
-        nc.scalar.copy(out=idb[:], in_=idf[:, 0:BANDS])
         widen(0, 1, VECTOR, (0,))
-        widen(0, 1, SCALAR, (1, 2))
+        widen(0, 1, SCALAR, (1, 2, 3))
         widen(1, 0, VECTOR, (0, 1))
         warm(1, 7, swide[0][:, LAST_SLOT * QUART : (LAST_SLOT + 2) * QUART])
         widen(1, 0, SCALAR, (2, 3))
-        widen(0, 1, SCALAR, (3,))
-        widen(1, 1, SCALAR, (0, 1, 2))
+        interleave(1, 0, 1, SCALAR)
         interleave(0, 0, 1, VECTOR)
         interleave(0, 1, 2, VECTOR)
-        interleave(1, 0, 1, VECTOR)
+        widen(1, 1, VECTOR, (0, 1, 2))
         quant_steer(0, 0, CP)
         gbank = bank(6)
         for k in range(SLOTS):
             turn(k, k)
-            if k == LAST_SLOT:
+            if k == 2:
                 widen(1, 1, SCALAR, (3,))
             empty(k)
             if k == 1:
                 nc.tensor.matmul(out=gbank[:, 0:QUART].bitcast(BF16), lhsT=ones[:, 0:P], rhs=gains[:, 0:HALF], start=True, stop=True)
             if k == 2:
                 warm(1, 7, ones[:, 0:HALF])
+        nc.scalar.copy(out=cgain[:, 0:HALF], in_=gbank[:, 0:QUART].bitcast(BF16))
         quant_echo(0)
         quant_echo(1)
-        quant_steer(1, 0, 1)
-        quant_echo(2)
         interleave(1, 1, 2, VECTOR)
+        quant_echo(2)
         quant_echo(3)
         first_two(0, 0, 0, 4)
-        nc.tensor.matmul(out=gbank[:, QUART : QUART + BANDS], lhsT=gains[:, HALF : HALF + P], rhs=idb[:], start=True, stop=True)
-        nc.scalar.copy(out=cgain[:, 0:HALF], in_=gbank[:, 0:QUART].bitcast(BF16))
-        nc.scalar.copy(out=rgain[:], in_=gbank[:, QUART : QUART + BANDS])
+        sort_words(7, SCALAR)
         for k in (4, 5):
             turn(k, k - 4)
             empty(k)
-        quant_steer(1, 1, 2)
+        quant_steer(1, 0, CP)
         gain_two(0, 0, 0)
         first_two(0, 0, 1, 5)
         first_two(0, 1, 0, 6)
         first_two(0, 1, 1, 7)
         sort_words(6, VECTOR)
-        for k in range(7, 10):
+        for k in (8, 9):
             sort_words(k, SCALAR)
         gain_two(0, 0, 1)
         quant_echo(4)
@@ -404,9 +401,9 @@ def tile_sonar_ping_coherence_s13_kernel(tc, echo, steer_bytes, steer_scale, ref
         quant_d(3, 0, QUART)
         quant_d(3, QUART, HALF)
         quant_steer(2, 0, CP)
+        nc.scalar.copy(out=rgain[:], in_=rraw[:, :, 0])
         widen(0, 3, SCALAR)
-        widen(1, 3, SCALAR, (0, 1))
-        widen(1, 3, VECTOR, (2, 3))
+        widen(1, 3, VECTOR)
 
         for i, k in ((5, 7), (6, 4)):
             for g in range(G - 1):
@@ -418,7 +415,7 @@ def tile_sonar_ping_coherence_s13_kernel(tc, echo, steer_bytes, steer_scale, ref
                 finish(i, 0, HALF, HALF)
 
         close((4, 5, 6))
-        interleave(3, 0, CP, VECTOR)
+        interleave(3, 0, 1, VECTOR)
         steps = [(0, 2), (1, 2), (2, 2), (0, 3), (1, 3), (2, 3), (3, 2), (3, 3)]
         held = [(i, g) for g in range(G - 1) for i in range(OPEN)]
         work = (5, 1, 7, 4)
@@ -435,27 +432,29 @@ def tile_sonar_ping_coherence_s13_kernel(tc, echo, steer_bytes, steer_scale, ref
                 first_two(g, q, 0, ka)
                 if n == 0:
                     close((0,))
+                    interleave(3, 1, 2, SCALAR)
                 first_two(g, q, 1, kb)
-                gain_two(g, q, 0)
-                if n == 0:
+                gains_two(g, q)
+                if n == 1:
                     quant_steer(3, 0, CP)
-                gain_two(g, q, 1)
                 if n > 0:
                     last_g, last_q = steps[n - 1]
                     quant_d(last_g, last_q * QUART, (last_q + 1) * QUART)
                 join(g, q)
             if n < 3:
                 close((n + 1,))
-            elif n == 3:
-                whole_band(BANDS - 1, 0, HALF, sums[0])
-            elif n == len(steps) - 2:
+            if 2 <= n < 2 + G:
+                second(BANDS - 1, n - 2, 0, HALF, sums[0])
+            if n == 1 + G:
+                finish(BANDS - 1, 0, HALF, HALF)
+            if n == len(steps) - 2:
                 for j in range(2):
                     i, held_g = held.pop(0)
                     second(i, held_g, HALF, N, sums[(i + 1) % OPEN])
-        for i, held_g in held[:-2]:
+        for i, held_g in held[:-1]:
             second(i, held_g, HALF, N, sums[(i + 1) % OPEN])
         for i in range(OPEN):
-            if (i, G - 2) in held[-2:]:
+            if (i, G - 2) in held[-1:]:
                 second(i, G - 2, HALF, N, None)
             second(i, G - 1, HALF, N, None)
             finish(i, HALF, N, HALF)

@@ -52,7 +52,7 @@ def tile_sonar_ping_coherence_s13_kernel(tc, echo, steer_bytes, steer_scale, ref
 
         ecod = [kept([P, SLOTS * CP * P], U32, "ecod%d" % g) for g in range(G)]
         escl = [kept([P, SLOTS * CP * P], U8, "escl%d" % g) for g in range(G)]
-        sscl = kept([P, CP, SLOTS], F32, "sscl")
+        sscl = kept([P, CP, 2 * SLOTS], F32, "sscl")
         swide = [kept([P, CP * SLOTS * QUART], BF16, "swide%d" % q) for q in range(N // QUART)]
         sgrp = [kept([P, CP * QUART * SLOTS], BF16, "sgrp%d" % q) for q in range(N // QUART)]
         scod = [kept([P, CP * QUART], U32, "scod%d" % q) for q in range(N // QUART)]
@@ -242,7 +242,7 @@ def tile_sonar_ping_coherence_s13_kernel(tc, echo, steer_bytes, steer_scale, ref
             for j in range(n):
                 nc.tensor.matmul(out=scratch[:], lhsT=ones[:, 0:P], rhs=moving, start=True, stop=True)
 
-        nc.scalar.dma_start(out=sscl[:], in_=steer_scale.rearrange("(c p t) o -> p c (t o)", p=P, t=SLOTS))
+        nc.scalar.dma_start(out=sscl[:, :, 0:SLOTS], in_=steer_scale.rearrange("(c p t) o -> p c (t o)", p=P, t=SLOTS))
         nc.vector.memset(gains[:].bitcast(I32), 0)
         nc.vector.memset(ones[:].bitcast(I32), TWO_ONES)
         nc.scalar.activation(out=table_warm[:], in_=gains[:, HALF : HALF + 1], func=SQUARE)

@@ -237,11 +237,6 @@ def tile_sonar_ping_coherence_s13_kernel(tc, echo, steer_bytes, steer_scale, ref
                 nc.scalar.activation(out=o[:, 0:piece], in_=band_sum[(i, n0)][:, a : a + piece], func=SQUARE, scale=rgain[:, i : i + 1])
                 nc.sync.dma_start(out=out[i * P : (i + 1) * P, n0 + a : n0 + a + piece], in_=o[:, 0:piece])
 
-        def warm(n, k, moving):
-            scratch = bank(k)
-            for j in range(n):
-                nc.tensor.matmul(out=scratch[:], lhsT=ones[:, 0:P], rhs=moving, start=True, stop=True)
-
         nc.scalar.dma_start(out=sscl[:, :, 0:SLOTS], in_=steer_scale.rearrange("(c p t) o -> p c (t o)", p=P, t=SLOTS))
         nc.vector.memset(gains[:].bitcast(I32), 0)
         nc.vector.memset(ones[:].bitcast(I32), TWO_ONES)
@@ -284,13 +279,10 @@ def tile_sonar_ping_coherence_s13_kernel(tc, echo, steer_bytes, steer_scale, ref
             gain_two(g, q, 0)
             gain_two(g, q, 1)
 
-        warm(3, 7, ones[:, 0:HALF])
         widen(0, 0, VECTOR)
-        warm(1, 7, swide[0][:, 0:HALF])
         widen(0, 1, VECTOR, (0,))
         widen(0, 1, SCALAR, (1, 2, 3))
         widen(1, 0, VECTOR, (0, 1))
-        warm(1, 7, swide[0][:, LAST_SLOT * QUART : (LAST_SLOT + 2) * QUART])
         widen(1, 0, SCALAR, (2, 3))
         interleave(1, 0, 1, SCALAR)
         interleave(0, 0, 1, VECTOR)
@@ -305,8 +297,6 @@ def tile_sonar_ping_coherence_s13_kernel(tc, echo, steer_bytes, steer_scale, ref
             empty(k)
             if k == 1:
                 nc.tensor.matmul(out=gbank[:, 0:QUART].bitcast(BF16), lhsT=ones[:, 0:P], rhs=gains[:, 0:HALF], start=True, stop=True)
-            if k == 2:
-                warm(1, 7, ones[:, 0:HALF])
         nc.scalar.copy(out=cgain[:, 0:HALF], in_=gbank[:, 0:QUART].bitcast(BF16))
         quant_echo(0)
         quant_echo(1)

@@ -26,7 +26,9 @@ HALF = 512
 QUART = 256
 BANDS = R // P
 OPEN = 4
-LAST_SLOT = SLOTS - 1
+LAST_T = SLOTS - 1
+LAST_G = G - 1
+LAST_BAND = BANDS - 1
 TWO_ONES = 0x3F803F80
 VECTOR, SCALAR = True, False
 ALONE = (0, 1, 2, 3, 6, 7, 10, 11)
@@ -44,8 +46,8 @@ def tile_sonar_ping_coherence_s13_kernel(tc, echo, steer_bytes, steer_scale, ref
         def kept(shape, dtype, name):
             return keep.tile(shape, dtype, name=name, align_bytes=256)
 
-        def bank(k):
-            return psum.tile([P, 512], F32, name="bank%d" % k, tag="bank%d" % k)
+        def bank(kb):
+            return psum.tile([P, 512], F32, name="bank%d" % kb, tag="bank%d" % kb)
 
         def copier(on_vector):
             return nc.vector.tensor_copy if on_vector else nc.scalar.copy
@@ -62,7 +64,7 @@ def tile_sonar_ping_coherence_s13_kernel(tc, echo, steer_bytes, steer_scale, ref
         pcod = [kept([P, 2 * R], U8, "pcod%d" % g) for g in range(G)]
         pscl = kept([P, G, R], U8, "pscl")
         gains = kept([P, HALF + 2], BF16, "gains")
-        ones = kept([P, HALF + 2], BF16, "ones")
+        ones = kept([P, P + 2], BF16, "ones")
         idf = kept([P, P], F32, "idf")
         rraw = kept([P, BANDS, 2], BF16, "rraw")
         cgain = kept([P, N], BF16, "cgain")
@@ -71,92 +73,85 @@ def tile_sonar_ping_coherence_s13_kernel(tc, echo, steer_bytes, steer_scale, ref
 
         echo_g = echo.rearrange("(g p t) k -> g p t k", p=P, t=SLOTS)
         steer_c = steer_bytes.rearrange("(c p t) n -> c p t n", p=P, t=SLOTS)
-        eraw, epiece, esort, xbank, egrp, epair, sraw = {}, {}, {}, {}, {}, {}, {}
-        ybank, ytwo, dgrp, dtwo, band_sum = {}, {}, {}, {}, {}
+        eraw, esort, xbank, egrp, epair, sraw = {}, {}, {}, {}, {}, {}
+        yfour, ytwo, dgrp, dtwo, band_sum = {}, {}, {}, {}, {}
 
-        def load_echo(k0, k1):
-            epiece[k0] = kept([P, (k1 - k0) * C], BF16, "eraw%d" % k0)
-            nc.sync.dma_start(out=epiece[k0][:], in_=echo_g[k0 // SLOTS][:, k0 % SLOTS : k0 % SLOTS + k1 - k0, :].rearrange("p t k -> p (t k)"))
-            for k in range(k0, k1):
-                eraw[k] = epiece[k0][:, (k - k0) * C : (k - k0 + 1) * C]
+        def load_echo(s0, s1):
+            tile = kept([P, (s1 - s0) * C], BF16, "eraw%d" % s0)
+            nc.sync.dma_start(out=tile[:], in_=echo_g[s0 // SLOTS][:, s0 % SLOTS : s0 % SLOTS + s1 - s0, :].rearrange("p t k -> p (t k)"))
+            for s in range(s0, s1):
+                eraw[s] = tile[:, (s - s0) * C : (s - s0 + 1) * C]
 
-        def load_steer(c, n0, n1):
-            tile = kept([P, SLOTS, n1 - n0], U8, "sraw%d_%d" % (c, n0))
-            nc.sync.dma_start(out=tile[:], in_=steer_c[c][:, :, n0:n1])
-            for b in range(n0 // P, n1 // P):
-                sraw[(c, b)] = (tile, n0)
+        def load_steer(c, h):
+            sraw[(c, h)] = kept([P, SLOTS, HALF], U8, "sraw%d_%d" % (c, h * HALF))
+            nc.sync.dma_start(out=sraw[(c, h)][:], in_=steer_c[c][:, :, h * HALF : (h + 1) * HALF])
 
         def load_words(g):
             nc.sync.dma_start(out=pcod[g][:].bitcast(I32), in_=ref_words[g].bitcast(I32))
 
-        def load_scales(g0, g1):
-            for r in range(4):
+        def load_scales():
+            for m in range(4):
                 nc.sync.dma_start(
-                    out=pscl[r:P:32, g0:g1, :].bitcast(I32),
-                    in_=ref_scales[g0:g1, r:16:4, :].rearrange("g a n -> a g n").bitcast(I32),
+                    out=pscl[m:P:32, :, :].bitcast(I32),
+                    in_=ref_scales[:, m:16:4, :].rearrange("g a n -> a g n").bitcast(I32),
                 )
 
-        def widen(c, q, on_vector, slots=range(SLOTS)):
-            raw, base = sraw[(c, 2 * q)]
-            for t in slots:
-                src = raw[:, t, q * QUART - base : (q + 1) * QUART - base].bitcast(FP8)
+        def widen(c, q, on_vector, rows=range(SLOTS)):
+            for t in rows:
+                src = sraw[(c, q // 2)][:, t, q % 2 * QUART : (q % 2 + 1) * QUART].bitcast(FP8)
                 dst = swide[q][:, (c * SLOTS + t) * QUART : (c * SLOTS + t + 1) * QUART]
                 if on_vector:
                     nc.vector.tensor_scalar(out=dst, in0=src, scalar1=sscl[:, c, t : t + 1], scalar2=None, op0=MULT)
                 else:
                     nc.scalar.activation(out=dst, in_=src, func=COPY, scale=sscl[:, c, t : t + 1])
 
-        def interleave(q, c0, c1, on_vector):
-            part = slice(c0 * SLOTS * QUART, c1 * SLOTS * QUART)
+        def interleave(c, q, on_vector):
+            part = slice(c * SLOTS * QUART, (c + 1) * SLOTS * QUART)
             copier(on_vector)(
-                out=sgrp[q][:, part].rearrange("p (c n i t) -> p c n t i", c=c1 - c0, i=4, t=SLOTS),
-                in_=swide[q][:, part].rearrange("p (c t n i) -> p c n t i", c=c1 - c0, i=4, t=SLOTS),
+                out=sgrp[q][:, part].rearrange("p (c n w t) -> p c n t w", c=1, w=4, t=SLOTS),
+                in_=swide[q][:, part].rearrange("p (c t n w) -> p c n t w", c=1, w=4, t=SLOTS),
             )
 
-        def quant_steer(q, c0, c1):
-            cols = slice(c0 * QUART, c1 * QUART)
-            nc.vector.quantize_mx(out=scod[q][:, cols].bitcast(FP8X4), scales=sqsc[q][:, cols], in_=sgrp[q][:, c0 * SLOTS * QUART : c1 * SLOTS * QUART])
+        def quant_steer(q):
+            nc.vector.quantize_mx(out=scod[q][:].bitcast(FP8X4), scales=sqsc[q][:], in_=sgrp[q][:])
 
-        def sort_words(k, on_vector, count=1):
-            tile = ring.tile([P, count * C // 2], F32, name="esort%d" % count, tag="esort%d" % count, align_bytes=256, bufs=4 // count)
-            src = eraw[k] if count == 1 else epiece[k][:]
+        def sort_words(s, on_vector):
+            esort[s] = ring.tile([P, C // 2], F32, name="esort1", tag="esort1", align_bytes=256, bufs=4)
             copier(on_vector)(
-                out=tile[:].rearrange("p (c u m) -> p c u m", c=count * CP, u=2),
-                in_=src.bitcast(F32).rearrange("p (c m u) -> p c u m", c=count * CP, u=2),
+                out=esort[s][:].rearrange("p (c odd x) -> p c odd x", c=CP, odd=2),
+                in_=eraw[s].bitcast(F32).rearrange("p (c x odd) -> p c odd x", c=CP, odd=2),
             )
-            for j in range(count):
-                esort[k + j] = tile[:, j * C // 2 : (j + 1) * C // 2]
 
-        def turn(k, kb):
-            xbank[k] = bank(kb)
-            words = eraw[k].bitcast(F32)
+        def turn(s, kb):
+            xbank[s] = bank(kb)
+            words = eraw[s].bitcast(F32)
             for c in range(CP):
-                for u in range(2):
-                    j = 2 * c + u
-                    src = esort[k][:, j * P : (j + 1) * P] if k in esort else words[:, 2 * P * c + u : 2 * P * (c + 1) : 2]
-                    nc.tensor.transpose(xbank[k][:, j * P : (j + 1) * P], src, idf[:])
+                for odd in range(2):
+                    cols = slice((2 * c + odd) * P, (2 * c + odd + 1) * P)
+                    src = esort[s][:, cols] if s in esort else words[:, 2 * P * c + odd : 2 * P * (c + 1) : 2]
+                    nc.tensor.transpose(xbank[s][:, cols], src, idf[:])
 
-        def empty(k):
-            if k in ALONE:
-                egrp[k] = ring.tile([P, C], BF16, name="egrp", tag="egrp", align_bytes=256, bufs=4)[:]
+        def empty(s):
+            if s in ALONE:
+                egrp[s] = ring.tile([P, C], BF16, name="egrp", tag="egrp", align_bytes=256, bufs=4)[:]
             else:
-                if k % 2 == 0:
-                    epair[k] = ring.tile([P, 2 * C], BF16, name="epair", tag="epair", align_bytes=256, bufs=3)
-                egrp[k] = epair[k - k % 2][:, k % 2 * C : (k % 2 + 1) * C]
+                if s % 2 == 0:
+                    epair[s] = ring.tile([P, 2 * C], BF16, name="epair", tag="epair", align_bytes=256, bufs=3)
+                egrp[s] = epair[s - s % 2][:, s % 2 * C : (s % 2 + 1) * C]
             nc.scalar.copy(
-                out=egrp[k].bitcast(F32).rearrange("p (c r u) -> p c r u", c=CP, u=2),
-                in_=xbank[k][:].rearrange("p (c u r) -> p c r u", c=CP, u=2),
+                out=egrp[s].bitcast(F32).rearrange("p (c r odd) -> p c r odd", c=CP, odd=2),
+                in_=xbank[s][:].rearrange("p (c odd r) -> p c r odd", c=CP, odd=2),
             )
 
-        def quant_echo(k):
-            src, count = (egrp[k], 1) if k in ALONE else (epair[k][:], 2)
-            cols = slice(k % SLOTS * CP * P, (k % SLOTS + count) * CP * P)
-            nc.vector.quantize_mx(out=ecod[k // SLOTS][:, cols].bitcast(FP8X4), scales=escl[k // SLOTS][:, cols], in_=src)
+        def quant_echo(s):
+            src, count = (egrp[s], 1) if s in ALONE else (epair[s][:], 2)
+            cols = slice(s % SLOTS * CP * P, (s % SLOTS + count) * CP * P)
+            nc.vector.quantize_mx(out=ecod[s // SLOTS][:, cols].bitcast(FP8X4), scales=escl[s // SLOTS][:, cols], in_=src)
 
         def first_sum(dst, g, t, n0, n1):
+            q = n0 // QUART
             for c in range(CP):
                 ecols = slice((t * CP + c) * P, (t * CP + c + 1) * P)
-                q = n0 // QUART
                 scols = slice((c - q) * QUART + n0, (c - q) * QUART + n1)
                 nc.tensor.matmul_mx(
                     out=dst,
@@ -168,161 +163,144 @@ def tile_sonar_ping_coherence_s13_kernel(tc, echo, steer_bytes, steer_scale, ref
                     stop=(c == CP - 1),
                 )
 
-        def first_slot(g, b, t, k):
-            if t == 0:
-                ybank[(g, b)] = bank(k)
-            first_sum(ybank[(g, b)][:, t * P : (t + 1) * P], g, t, b * P, (b + 1) * P)
-
-        def first(g, b, k):
-            for t in range(SLOTS):
-                first_slot(g, b, t, k)
-
         def d_cols(g, n0, n1):
             h = n0 // HALF
             if (g, h) not in dgrp:
                 dgrp[(g, h)] = ring.tile([P, HALF * SLOTS], BF16, name="dgrp", tag="dgrp", align_bytes=256, bufs=4)
             return dgrp[(g, h)][:, (n0 - h * HALF) * SLOTS : (n1 - h * HALF) * SLOTS]
 
-        def gain(g, b):
-            nc.vector.tensor_tensor(
-                out=d_cols(g, b * P, (b + 1) * P).rearrange("p (n i t) -> p n t i", i=4, t=SLOTS),
-                in0=ybank[(g, b)][:].rearrange("p (t n i) -> p n t i", t=SLOTS, i=4),
-                in1=cgain[:, b * P : (b + 1) * P].rearrange("p (n i) -> p n i", i=4).unsqueeze(2).to_broadcast([P, P // 4, SLOTS, 4]),
-                op=MULT,
-            )
-
-        def first_two(g, q, u, k):
-            ytwo[(g, q, u)] = bank(k)
-            for e in range(2):
-                first_sum(ytwo[(g, q, u)][:, e * QUART : (e + 1) * QUART], g, 2 * u + e, q * QUART, (q + 1) * QUART)
+        def first_two(g, q, u, kb):
+            ytwo[(g, q, u)] = bank(kb)
+            for v in range(2):
+                first_sum(ytwo[(g, q, u)][:, v * QUART : (v + 1) * QUART], g, 2 * u + v, q * QUART, (q + 1) * QUART)
 
         def gain_two(g, q, u):
             if u == 0:
                 dtwo[(g, q)] = ring.tile([P, 2, QUART, 2], BF16, name="dtwo", tag="dtwo", align_bytes=256)
             nc.vector.tensor_tensor(
                 out=dtwo[(g, q)][:, u, :, :],
-                in0=ytwo[(g, q, u)][:].rearrange("p (e n) -> p n e", e=2),
+                in0=ytwo[(g, q, u)][:].rearrange("p (v n) -> p n v", v=2),
                 in1=cgain[:, q * QUART : (q + 1) * QUART].unsqueeze(2).to_broadcast([P, QUART, 2]),
                 op=MULT,
             )
 
-        def join(g, q, on_vector=False):
+        def join(g, q, on_vector):
             copier(on_vector)(
                 out=d_cols(g, q * QUART, (q + 1) * QUART).bitcast(F32).rearrange("p (n u) -> p n u", u=2),
-                in_=dtwo[(g, q)][:].rearrange("p u n e -> p (u n e)").bitcast(F32).rearrange("p (u n) -> p n u", u=2),
+                in_=dtwo[(g, q)][:].rearrange("p u n v -> p (u n v)").bitcast(F32).rearrange("p (u n) -> p n u", u=2),
+            )
+
+        def first_four(g, e, rows, kb):
+            for t in rows:
+                if t == 0:
+                    yfour[(g, e)] = bank(kb)
+                first_sum(yfour[(g, e)][:, t * P : (t + 1) * P], g, t, e * P, (e + 1) * P)
+
+        def gain_four(g, e):
+            nc.vector.tensor_tensor(
+                out=d_cols(g, e * P, (e + 1) * P).rearrange("p (n w t) -> p n t w", w=4, t=SLOTS),
+                in0=yfour[(g, e)][:].rearrange("p (t n w) -> p n t w", t=SLOTS, w=4),
+                in1=cgain[:, e * P : (e + 1) * P].rearrange("p (n w) -> p n w", w=4).unsqueeze(2).to_broadcast([P, P // 4, SLOTS, 4]),
+                op=MULT,
             )
 
         def quant_d(g, n0, n1):
             nc.vector.quantize_mx(out=dcod[g][:, n0:n1].bitcast(FP8X4), scales=dscl[g][:, n0:n1], in_=d_cols(g, n0, n1))
 
-        def second_pass(dst, i, g, n0, n1, start, stop):
+        def second(i, g, n0, n1, kb=None):
+            if g == 0:
+                band_sum[(i, n0)] = bank(kb)
             nc.tensor.matmul_mx(
-                out=dst,
+                out=band_sum[(i, n0)][:, 0 : n1 - n0],
                 lhsT=pcod[g][:, i * 2 * P : (i + 1) * 2 * P].bitcast(FP4X4),
                 lhsT_scale=pscl[:, g, i * P : (i + 1) * P],
                 rhs=dcod[g][:, n0:n1].bitcast(FP8X4),
                 rhs_scale=dscl[g][:, n0:n1],
-                start=start,
-                stop=stop,
+                start=(g == 0),
+                stop=(g == LAST_G),
             )
 
-        def second(i, g, n0, n1, k):
-            if g == 0:
-                band_sum[(i, n0)] = bank(k)
-            second_pass(band_sum[(i, n0)][:, 0 : n1 - n0], i, g, n0, n1, g == 0, g == G - 1)
+        def finish(i, n0, n1):
+            done = stage.tile([P, HALF], F32, name="o", tag="o", align_bytes=256)
+            nc.scalar.activation(out=done[:, 0 : n1 - n0], in_=band_sum[(i, n0)][:, 0 : n1 - n0], func=SQUARE, scale=rgain[:, i : i + 1])
+            nc.sync.dma_start(out=out[i * P : (i + 1) * P, n0:n1], in_=done[:, 0 : n1 - n0])
 
-        def finish(i, n0, n1, piece):
-            for a in range(0, n1 - n0, piece):
-                o = stage.tile([P, HALF], F32, name="o", tag="o", align_bytes=256)
-                nc.scalar.activation(out=o[:, 0:piece], in_=band_sum[(i, n0)][:, a : a + piece], func=SQUARE, scale=rgain[:, i : i + 1])
-                nc.sync.dma_start(out=out[i * P : (i + 1) * P, n0 + a : n0 + a + piece], in_=o[:, 0:piece])
+        def close(i, n0):
+            second(i, LAST_G, n0, n0 + HALF)
+            finish(i, n0, n0 + HALF)
 
-        nc.scalar.dma_start(out=sscl[:, :, 0:SLOTS], in_=steer_scale.rearrange("(c p t) o -> p c (t o)", p=P, t=SLOTS))
+        nc.scalar.dma_start(out=sscl[:, :, 0:SLOTS], in_=steer_scale.rearrange("(c p t) one -> p c (t one)", p=P, t=SLOTS))
         nc.vector.memset(gains[:].bitcast(I32), 0)
         nc.vector.memset(ones[:].bitcast(I32), TWO_ONES)
         nc.scalar.activation(out=table_warm[:], in_=gains[:, HALF : HALF + 1], func=SQUARE)
         make_identity(nc, idf[:])
         nc.vector.memset(pscl[:].rearrange("p g n -> p (g n)").bitcast(I32), 0)
 
-
         for c in range(CP):
-            load_steer(c, 0, HALF)
-        for k in range(4):
-            load_echo(k, k + 1)
-            if k == 1:
+            load_steer(c, 0)
+        for s in range(SLOTS):
+            load_echo(s, s + 1)
+            if s == 1:
                 nc.sync.dma_start(out=gains[0:1, 0:HALF], in_=col_gain[0:HALF].unsqueeze(0))
-        for k in range(4, 16, 2):
-            load_echo(k, k + 2)
-        load_scales(0, G)
+        for s in range(SLOTS, G * SLOTS, 2):
+            load_echo(s, s + 2)
+        load_scales()
         load_words(0)
         load_words(1)
         for c in range(CP):
-            load_steer(c, HALF, N)
+            load_steer(c, 1)
         load_words(2)
         nc.sync.dma_start(out=cgain[:, HALF:N], in_=col_gain[HALF:N].partition_broadcast(P))
         load_words(3)
         with nc.allow_non_contiguous_dma(reason="one gain for each partition and band"):
-            nc.sync.dma_start(out=rraw[:, :, 0:1], in_=row_gain.rearrange("(i p o) -> p i o", p=P, o=1))
+            nc.sync.dma_start(out=rraw[:, :, 0:1], in_=row_gain.rearrange("(i p one) -> p i one", p=P, one=1))
 
-        sums = (0, 3, 6, 2)
-
-        def second_open(g, n0):
-            for i in range(OPEN):
-                second(i, g, n0, n0 + HALF, sums[i])
-
-        def whole_band(i, n0, n1, k):
-            for g in range(G):
-                second(i, g, n0, n1, k)
-            finish(i, n0, n1, n1 - n0)
-
-        def gains_two(g, q):
-            gain_two(g, q, 0)
-            gain_two(g, q, 1)
 
         widen(0, 0, VECTOR)
         widen(0, 1, VECTOR, (0,))
         widen(0, 1, SCALAR, (1, 2, 3))
         widen(1, 0, VECTOR, (0, 1))
         widen(1, 0, SCALAR, (2, 3))
-        interleave(1, 0, 1, SCALAR)
-        interleave(0, 0, 1, VECTOR)
-        interleave(0, 1, 2, VECTOR)
+        interleave(0, 1, SCALAR)
+        interleave(0, 0, VECTOR)
+        interleave(1, 0, VECTOR)
         widen(1, 1, VECTOR, (0, 1, 2))
-        quant_steer(0, 0, CP)
+        quant_steer(0)
         gbank = bank(6)
-        for k in range(SLOTS):
-            turn(k, k)
-            if k == 2:
-                widen(1, 1, SCALAR, (3,))
-            empty(k)
-            if k == 1:
+        for s in range(SLOTS):
+            turn(s, s)
+            if s == 2:
+                widen(1, 1, SCALAR, (LAST_T,))
+            empty(s)
+            if s == 1:
                 nc.tensor.matmul(out=gbank[:, 0:QUART].bitcast(BF16), lhsT=ones[:, 0:P], rhs=gains[:, 0:HALF], start=True, stop=True)
         nc.scalar.copy(out=cgain[:, 0:HALF], in_=gbank[:, 0:QUART].bitcast(BF16))
         quant_echo(0)
         quant_echo(1)
-        interleave(1, 1, 2, VECTOR)
+        interleave(1, 1, VECTOR)
         quant_echo(2)
         quant_echo(3)
         first_two(0, 0, 0, 4)
         sort_words(7, SCALAR)
-        for k in (4, 5):
-            turn(k, k - 4)
-            empty(k)
-        quant_steer(1, 0, CP)
+        for s, kb in ((4, 0), (5, 1)):
+            turn(s, kb)
+            empty(s)
+        quant_steer(1)
         gain_two(0, 0, 0)
         first_two(0, 0, 1, 5)
         first_two(0, 1, 0, 6)
         first_two(0, 1, 1, 7)
+
         sort_words(6, VECTOR)
-        for k in (8, 9):
-            sort_words(k, SCALAR)
+        for s in (8, 9):
+            sort_words(s, SCALAR)
         gain_two(0, 0, 1)
         quant_echo(4)
         gain_two(0, 1, 0)
-        for k, kb in zip(range(6, 10), (2, 0, 3, 1)):
-            turn(k, kb)
-        for k in range(6, 10):
-            empty(k)
+        for s, kb in zip(range(6, 10), (2, 0, 3, 1)):
+            turn(s, kb)
+        for s in range(6, 10):
+            empty(s)
         sort_words(10, VECTOR)
         quant_echo(6)
         sort_words(11, VECTOR)
@@ -331,124 +309,126 @@ def tile_sonar_ping_coherence_s13_kernel(tc, echo, steer_bytes, steer_scale, ref
         join(0, 0, VECTOR)
         for u in range(2):
             first_two(1, 0, u, (4, 6)[u])
-            for b in (2, 3):
-                for t in (2 * u, 2 * u + 1):
-                    first_slot(1, b, t, (5, 2)[b - 2])
+            for e, kb in ((2, 5), (3, 2)):
+                first_four(1, e, (2 * u, 2 * u + 1), kb)
+
+        sums = (0, 3, 6, 2)
         sort_words(12, SCALAR)
         sort_words(13, SCALAR)
-        join(0, 1)
+        join(0, 1, SCALAR)
         gain_two(1, 0, 0)
         quant_echo(8)
-        gain(1, 2)
-        for k, kb in zip(range(10, 14), (0, 3, 1, 7)):
-            turn(k, kb)
-            empty(k)
+        gain_four(1, 2)
+        for s, kb in zip(range(10, 14), (0, 3, 1, 7)):
+            turn(s, kb)
+            empty(s)
         quant_d(0, 0, HALF)
         gain_two(1, 0, 1)
-        gain(1, 3)
+        gain_four(1, 3)
         quant_echo(10)
         quant_echo(11)
         first_two(2, 0, 0, 4)
         first_two(2, 1, 0, 5)
-        second_open(0, 0)
-        join(1, 0)
+        for i in range(OPEN):
+            second(i, 0, 0, HALF, sums[i])
+        join(1, 0, SCALAR)
         sort_words(14, SCALAR)
         sort_words(15, SCALAR)
-        widen(0, 2, SCALAR, range(LAST_SLOT))
+        widen(0, 2, SCALAR, range(LAST_T))
         gain_two(2, 0, 0)
         gain_two(2, 1, 0)
         first_two(2, 0, 1, 1)
         first_two(2, 1, 1, 7)
+
         quant_d(1, 0, HALF)
         quant_echo(12)
-        for k in (14, 15):
-            turn(k, k - 10)
-            empty(k)
+        for s, kb in ((14, 4), (15, 5)):
+            turn(s, kb)
+            empty(s)
         gain_two(2, 0, 1)
         gain_two(2, 1, 1)
-        second_open(1, 0)
-        join(2, 0)
-        join(2, 1)
-        widen(0, 2, SCALAR, (LAST_SLOT,))
+        for i in range(OPEN):
+            second(i, 1, 0, HALF)
+        join(2, 0, SCALAR)
+        join(2, 1, SCALAR)
+        widen(0, 2, SCALAR, (LAST_T,))
         quant_echo(14)
+        work = (1, 7, 4, 5)
         for u in range(2):
             for q in range(2):
-                first_two(3, q, u, (1, 7, 4, 5)[2 * u + q])
+                first_two(3, q, u, work[2 * u + q])
         widen(1, 2, SCALAR)
-        interleave(2, 0, 1, SCALAR)
+        interleave(0, 2, SCALAR)
         gain_two(3, 0, 0)
         quant_d(2, 0, HALF)
         for g in range(2):
-            second(4, g, 0, HALF, 1)
-        second_open(2, 0)
-        second(4, 2, 0, HALF, None)
+            second(OPEN, g, 0, HALF, work[0])
+        for i in range(OPEN + 1):
+            second(i, 2, 0, HALF)
         gain_two(3, 1, 0)
         gain_two(3, 0, 1)
-        join(3, 0)
+        join(3, 0, SCALAR)
         gain_two(3, 1, 1)
-        interleave(2, 1, 2, VECTOR)
+        interleave(1, 2, VECTOR)
         join(3, 1, VECTOR)
         quant_d(3, 0, QUART)
         quant_d(3, QUART, HALF)
-        quant_steer(2, 0, CP)
+        quant_steer(2)
         nc.scalar.copy(out=rgain[:], in_=rraw[:, :, 0])
         widen(0, 3, SCALAR)
         widen(1, 3, VECTOR)
+        for i in (OPEN + 1, OPEN + 2):
+            for g in range(LAST_G):
+                second(i, g, 0, HALF, work[i - OPEN])
+        for i in range(OPEN, LAST_BAND):
+            close(i, 0)
+        interleave(0, 3, VECTOR)
 
-        for i, k in ((5, 7), (6, 4)):
-            for g in range(G - 1):
-                second(i, g, 0, HALF, k)
+        steps = [(g, q) for q in (2, 3) for g in range(LAST_G)] + [(LAST_G, 2), (LAST_G, 3)]
+        step_banks = (work[3], work[0], work[1], work[2])
+        held = [(i, g) for g in range(LAST_G) for i in range(OPEN)]
 
-        def close(bands):
-            for i in bands:
-                second(i, G - 1, 0, HALF, None)
-                finish(i, 0, HALF, HALF)
+        def run_held(passes):
+            for i, g in passes:
+                second(i, g, HALF, N, sums[(i + 1) % OPEN])
 
-        close((4, 5, 6))
-        interleave(3, 0, 1, VECTOR)
-        steps = [(0, 2), (1, 2), (2, 2), (0, 3), (1, 3), (2, 3), (3, 2), (3, 3)]
-        held = [(i, g) for g in range(G - 1) for i in range(OPEN)]
-        work = (5, 1, 7, 4)
-        for n, (g, q) in enumerate(steps):
-            ka, kb = work[2 * (n % 2)], work[2 * (n % 2) + 1]
-            if n == len(steps) - 1:
-                first(g, 2 * q, ka)
-                first(g, 2 * q + 1, kb)
-                gain(g, 2 * q)
-                gain(g, 2 * q + 1)
-                quant_d(g, HALF, HALF + QUART)
-                quant_d(g, HALF + QUART, N)
-            else:
-                first_two(g, q, 0, ka)
-                if n == 0:
-                    close((0,))
-                    interleave(3, 1, 2, SCALAR)
-                first_two(g, q, 1, kb)
-                gains_two(g, q)
-                if n == 1:
-                    quant_steer(3, 0, CP)
-                if n > 0:
-                    last_g, last_q = steps[n - 1]
-                    quant_d(last_g, last_q * QUART, (last_q + 1) * QUART)
-                join(g, q)
-            if n < 3:
-                close((n + 1,))
-            if 2 <= n < 2 + G:
-                second(BANDS - 1, n - 2, 0, HALF, sums[0])
-            if n == 1 + G:
-                finish(BANDS - 1, 0, HALF, HALF)
-            if n == len(steps) - 2:
-                for j in range(2):
-                    i, held_g = held.pop(0)
-                    second(i, held_g, HALF, N, sums[(i + 1) % OPEN])
-        for i, held_g in held[:-1]:
-            second(i, held_g, HALF, N, sums[(i + 1) % OPEN])
+        for step, (g, q) in enumerate(steps[:-1]):
+            first_two(g, q, 0, step_banks[2 * (step % 2)])
+            if step == 0:
+                close(0, 0)
+                interleave(1, 3, SCALAR)
+            first_two(g, q, 1, step_banks[2 * (step % 2) + 1])
+            gain_two(g, q, 0)
+            gain_two(g, q, 1)
+            if step == 1:
+                quant_steer(3)
+            if step > 0:
+                before_g, before_q = steps[step - 1]
+                quant_d(before_g, before_q * QUART, (before_q + 1) * QUART)
+            join(g, q, SCALAR)
+            if step + 1 < OPEN:
+                close(step + 1, 0)
+            band7_g = step - 2
+            if 0 <= band7_g < G:
+                second(LAST_BAND, band7_g, 0, HALF, sums[0])
+            if band7_g == LAST_G:
+                finish(LAST_BAND, 0, HALF)
+        run_held(held[:2])
+        for e, kb in zip((6, 7), step_banks[2:]):
+            first_four(LAST_G, e, range(SLOTS), kb)
+        for e in (6, 7):
+            gain_four(LAST_G, e)
+        quant_d(LAST_G, HALF, HALF + QUART)
+        quant_d(LAST_G, HALF + QUART, N)
+        run_held(held[2:-1])
         for i in range(OPEN):
-            if (i, G - 2) in held[-1:]:
-                second(i, G - 2, HALF, N, None)
-            second(i, G - 1, HALF, N, None)
-            finish(i, HALF, N, HALF)
-        pieces = [(i, HALF, N) for i in range(OPEN, BANDS - 2)]
-        pieces += [(BANDS - 2, HALF, HALF + QUART), (BANDS - 2, HALF + QUART, N), (BANDS - 1, HALF, HALF + QUART), (BANDS - 1, HALF + QUART, N - P), (BANDS - 1, N - P, N)]
-        for (i, n0, n1), k in zip(pieces, work + sums[1:]):
-            whole_band(i, n0, n1, k)
+            if i == OPEN - 1:
+                run_held(held[-1:])
+            close(i, HALF)
+        pieces = [(i, HALF, N) for i in range(OPEN, LAST_BAND - 1)]
+        pieces += [(LAST_BAND - 1, HALF, HALF + QUART), (LAST_BAND - 1, HALF + QUART, N)]
+        pieces += [(LAST_BAND, HALF, HALF + QUART), (LAST_BAND, HALF + QUART, N - P), (LAST_BAND, N - P, N)]
+        for (i, n0, n1), kb in zip(pieces, step_banks + sums[1:]):
+            for g in range(G):
+                second(i, g, n0, n1, kb)
+            finish(i, n0, n1)

from contextlib import ExitStack

import concourse.mybir as mybir
from concourse.masks import make_identity

T, C, N, R = 2048, 1024, 1024, 1024
FLOPS = 2 * T * C * N + 2 * T * R * N

F32 = mybir.dt.float32
BF16 = mybir.dt.bfloat16
U32 = mybir.dt.uint32
I32 = mybir.dt.int32
U8 = mybir.dt.uint8
FP8 = mybir.dt.float8_e4m3fn
FP8X4 = mybir.dt.float8_e4m3fn_x4
FP4X4 = mybir.dt.float4_e2m1fn_x4
COPY = mybir.ActivationFunctionType.Copy
SQUARE = mybir.ActivationFunctionType.Square
MULT = mybir.AluOpType.mult

P = 128
SLOTS = 4
G = T // 512
CP = C // 512
HALF = 512
QUART = 256
BANDS = R // P
OPEN = 4
LAST_T = SLOTS - 1
LAST_G = G - 1
LAST_BAND = BANDS - 1
TWO_ONES = 0x3F803F80
VECTOR, SCALAR = True, False
ALONE = (0, 1, 2, 3, 6, 7, 10, 11)


def tile_sonar_ping_coherence_s13_kernel(tc, echo, steer_bytes, steer_scale, ref_words, ref_scales, col_gain, row_gain, out):
    nc = tc.nc
    with ExitStack() as ctx:
        keep = ctx.enter_context(tc.tile_pool(name="keep", bufs=1))
        ring = ctx.enter_context(tc.tile_pool(name="ring", bufs=6))
        stage = ctx.enter_context(tc.tile_pool(name="stage", bufs=8))
        psum = ctx.enter_context(tc.psum_pool(name="psum", bufs=1))
        ctx.enter_context(tc.manual_schedule())

        def kept(shape, dtype, name):
            return keep.tile(shape, dtype, name=name, align_bytes=256)

        def bank(kb):
            return psum.tile([P, 512], F32, name="bank%d" % kb, tag="bank%d" % kb)

        def copier(on_vector):
            return nc.vector.tensor_copy if on_vector else nc.scalar.copy

        ecod = [kept([P, SLOTS * CP * P], U32, "ecod%d" % g) for g in range(G)]
        escl = [kept([P, SLOTS * CP * P], U8, "escl%d" % g) for g in range(G)]
        sscl = kept([P, CP, 2 * SLOTS], F32, "sscl")
        swide = [kept([P, CP * SLOTS * QUART], BF16, "swide%d" % q) for q in range(N // QUART)]
        sgrp = [kept([P, CP * QUART * SLOTS], BF16, "sgrp%d" % q) for q in range(N // QUART)]
        scod = [kept([P, CP * QUART], U32, "scod%d" % q) for q in range(N // QUART)]
        sqsc = [kept([P, CP * QUART], U8, "sqsc%d" % q) for q in range(N // QUART)]
        dcod = [kept([P, N], U32, "dcod%d" % g) for g in range(G)]
        dscl = [kept([P, N], U8, "dscl%d" % g) for g in range(G)]
        pcod = [kept([P, 2 * R], U8, "pcod%d" % g) for g in range(G)]
        pscl = kept([P, G, R], U8, "pscl")
        gains = kept([P, HALF + 2], BF16, "gains")
        ones = kept([P, P + 2], BF16, "ones")
        idf = kept([P, P], F32, "idf")
        rraw = kept([P, BANDS, 2], BF16, "rraw")
        cgain = kept([P, N], BF16, "cgain")
        table_warm = kept([P, 1], F32, "table_warm")
        rgain = kept([P, BANDS], F32, "rgain")

        echo_g = echo.rearrange("(g p t) k -> g p t k", p=P, t=SLOTS)
        steer_c = steer_bytes.rearrange("(c p t) n -> c p t n", p=P, t=SLOTS)
        eraw, esort, xbank, egrp, epair, sraw = {}, {}, {}, {}, {}, {}
        yfour, ytwo, dgrp, dtwo, band_sum = {}, {}, {}, {}, {}

        def load_echo(s0, s1):
            tile = kept([P, (s1 - s0) * C], BF16, "eraw%d" % s0)
            nc.sync.dma_start(out=tile[:], in_=echo_g[s0 // SLOTS][:, s0 % SLOTS : s0 % SLOTS + s1 - s0, :].rearrange("p t k -> p (t k)"))
            for s in range(s0, s1):
                eraw[s] = tile[:, (s - s0) * C : (s - s0 + 1) * C]

        def load_steer(c, h):
            sraw[(c, h)] = kept([P, SLOTS, HALF], U8, "sraw%d_%d" % (c, h * HALF))
            nc.sync.dma_start(out=sraw[(c, h)][:], in_=steer_c[c][:, :, h * HALF : (h + 1) * HALF])

        def load_words(g):
            nc.sync.dma_start(out=pcod[g][:].bitcast(I32), in_=ref_words[g].bitcast(I32))

        def load_scales():
            for m in range(4):
                nc.sync.dma_start(
                    out=pscl[m:P:32, :, :].bitcast(I32),
                    in_=ref_scales[:, m:16:4, :].rearrange("g a n -> a g n").bitcast(I32),
                )

        def widen(c, q, on_vector, rows=range(SLOTS)):
            for t in rows:
                src = sraw[(c, q // 2)][:, t, q % 2 * QUART : (q % 2 + 1) * QUART].bitcast(FP8)
                dst = swide[q][:, (c * SLOTS + t) * QUART : (c * SLOTS + t + 1) * QUART]
                if on_vector:
                    nc.vector.tensor_scalar(out=dst, in0=src, scalar1=sscl[:, c, t : t + 1], scalar2=None, op0=MULT)
                else:
                    nc.scalar.activation(out=dst, in_=src, func=COPY, scale=sscl[:, c, t : t + 1])

        def interleave(c, q, on_vector):
            part = slice(c * SLOTS * QUART, (c + 1) * SLOTS * QUART)
            copier(on_vector)(
                out=sgrp[q][:, part].rearrange("p (c n w t) -> p c n t w", c=1, w=4, t=SLOTS),
                in_=swide[q][:, part].rearrange("p (c t n w) -> p c n t w", c=1, w=4, t=SLOTS),
            )

        def quant_steer(q):
            nc.vector.quantize_mx(out=scod[q][:].bitcast(FP8X4), scales=sqsc[q][:], in_=sgrp[q][:])

        def sort_words(s, on_vector):
            esort[s] = ring.tile([P, C // 2], F32, name="esort1", tag="esort1", align_bytes=256, bufs=4)
            copier(on_vector)(
                out=esort[s][:].rearrange("p (c odd x) -> p c odd x", c=CP, odd=2),
                in_=eraw[s].bitcast(F32).rearrange("p (c x odd) -> p c odd x", c=CP, odd=2),
            )

        def turn(s, kb):
            xbank[s] = bank(kb)
            words = eraw[s].bitcast(F32)
            for c in range(CP):
                for odd in range(2):
                    cols = slice((2 * c + odd) * P, (2 * c + odd + 1) * P)
                    src = esort[s][:, cols] if s in esort else words[:, 2 * P * c + odd : 2 * P * (c + 1) : 2]
                    nc.tensor.transpose(xbank[s][:, cols], src, idf[:])

        def empty(s):
            if s in ALONE:
                egrp[s] = ring.tile([P, C], BF16, name="egrp", tag="egrp", align_bytes=256, bufs=4)[:]
            else:
                if s % 2 == 0:
                    epair[s] = ring.tile([P, 2 * C], BF16, name="epair", tag="epair", align_bytes=256, bufs=3)
                egrp[s] = epair[s - s % 2][:, s % 2 * C : (s % 2 + 1) * C]
            nc.scalar.copy(
                out=egrp[s].bitcast(F32).rearrange("p (c r odd) -> p c r odd", c=CP, odd=2),
                in_=xbank[s][:].rearrange("p (c odd r) -> p c r odd", c=CP, odd=2),
            )

        def quant_echo(s):
            src, count = (egrp[s], 1) if s in ALONE else (epair[s][:], 2)
            cols = slice(s % SLOTS * CP * P, (s % SLOTS + count) * CP * P)
            nc.vector.quantize_mx(out=ecod[s // SLOTS][:, cols].bitcast(FP8X4), scales=escl[s // SLOTS][:, cols], in_=src)

        def first_sum(dst, g, t, n0, n1):
            q = n0 // QUART
            for c in range(CP):
                ecols = slice((t * CP + c) * P, (t * CP + c + 1) * P)
                scols = slice((c - q) * QUART + n0, (c - q) * QUART + n1)
                nc.tensor.matmul_mx(
                    out=dst,
                    lhsT=ecod[g][:, ecols].bitcast(FP8X4),
                    lhsT_scale=escl[g][:, ecols],
                    rhs=scod[q][:, scols].bitcast(FP8X4),
                    rhs_scale=sqsc[q][:, scols],
                    start=(c == 0),
                    stop=(c == CP - 1),
                )

        def d_cols(g, n0, n1):
            h = n0 // HALF
            if (g, h) not in dgrp:
                dgrp[(g, h)] = ring.tile([P, HALF * SLOTS], BF16, name="dgrp", tag="dgrp", align_bytes=256, bufs=4)
            return dgrp[(g, h)][:, (n0 - h * HALF) * SLOTS : (n1 - h * HALF) * SLOTS]

        def first_two(g, q, u, kb):
            ytwo[(g, q, u)] = bank(kb)
            for v in range(2):
                first_sum(ytwo[(g, q, u)][:, v * QUART : (v + 1) * QUART], g, 2 * u + v, q * QUART, (q + 1) * QUART)

        def gain_two(g, q, u):
            if u == 0:
                dtwo[(g, q)] = ring.tile([P, 2, QUART, 2], BF16, name="dtwo", tag="dtwo", align_bytes=256)
            nc.vector.tensor_tensor(
                out=dtwo[(g, q)][:, u, :, :],
                in0=ytwo[(g, q, u)][:].rearrange("p (v n) -> p n v", v=2),
                in1=cgain[:, q * QUART : (q + 1) * QUART].unsqueeze(2).to_broadcast([P, QUART, 2]),
                op=MULT,
            )

        def join(g, q, on_vector):
            copier(on_vector)(
                out=d_cols(g, q * QUART, (q + 1) * QUART).bitcast(F32).rearrange("p (n u) -> p n u", u=2),
                in_=dtwo[(g, q)][:].rearrange("p u n v -> p (u n v)").bitcast(F32).rearrange("p (u n) -> p n u", u=2),
            )

        def first_four(g, e, rows, kb):
            for t in rows:
                if t == 0:
                    yfour[(g, e)] = bank(kb)
                first_sum(yfour[(g, e)][:, t * P : (t + 1) * P], g, t, e * P, (e + 1) * P)

        def gain_four(g, e):
            nc.vector.tensor_tensor(
                out=d_cols(g, e * P, (e + 1) * P).rearrange("p (n w t) -> p n t w", w=4, t=SLOTS),
                in0=yfour[(g, e)][:].rearrange("p (t n w) -> p n t w", t=SLOTS, w=4),
                in1=cgain[:, e * P : (e + 1) * P].rearrange("p (n w) -> p n w", w=4).unsqueeze(2).to_broadcast([P, P // 4, SLOTS, 4]),
                op=MULT,
            )

        def quant_d(g, n0, n1):
            nc.vector.quantize_mx(out=dcod[g][:, n0:n1].bitcast(FP8X4), scales=dscl[g][:, n0:n1], in_=d_cols(g, n0, n1))

        def second(i, g, n0, n1, kb=None):
            if g == 0:
                band_sum[(i, n0)] = bank(kb)
            nc.tensor.matmul_mx(
                out=band_sum[(i, n0)][:, 0 : n1 - n0],
                lhsT=pcod[g][:, i * 2 * P : (i + 1) * 2 * P].bitcast(FP4X4),
                lhsT_scale=pscl[:, g, i * P : (i + 1) * P],
                rhs=dcod[g][:, n0:n1].bitcast(FP8X4),
                rhs_scale=dscl[g][:, n0:n1],
                start=(g == 0),
                stop=(g == LAST_G),
            )

        def finish(i, n0, n1):
            done = stage.tile([P, HALF], F32, name="o", tag="o", align_bytes=256)
            nc.scalar.activation(out=done[:, 0 : n1 - n0], in_=band_sum[(i, n0)][:, 0 : n1 - n0], func=SQUARE, scale=rgain[:, i : i + 1])
            nc.sync.dma_start(out=out[i * P : (i + 1) * P, n0:n1], in_=done[:, 0 : n1 - n0])

        def close(i, n0):
            second(i, LAST_G, n0, n0 + HALF)
            finish(i, n0, n0 + HALF)

        nc.scalar.dma_start(out=sscl[:, :, 0:SLOTS], in_=steer_scale.rearrange("(c p t) one -> p c (t one)", p=P, t=SLOTS))
        nc.vector.memset(gains[:].bitcast(I32), 0)
        nc.vector.memset(ones[:].bitcast(I32), TWO_ONES)
        nc.scalar.activation(out=table_warm[:], in_=gains[:, HALF : HALF + 1], func=SQUARE)
        make_identity(nc, idf[:])
        nc.vector.memset(pscl[:].rearrange("p g n -> p (g n)").bitcast(I32), 0)

        for c in range(CP):
            load_steer(c, 0)
        for s in range(SLOTS):
            load_echo(s, s + 1)
            if s == 1:
                nc.sync.dma_start(out=gains[0:1, 0:HALF], in_=col_gain[0:HALF].unsqueeze(0))
        for s in range(SLOTS, G * SLOTS, 2):
            load_echo(s, s + 2)
        load_scales()
        load_words(0)
        load_words(1)
        for c in range(CP):
            load_steer(c, 1)
        load_words(2)
        nc.sync.dma_start(out=cgain[:, HALF:N], in_=col_gain[HALF:N].partition_broadcast(P))
        load_words(3)
        with nc.allow_non_contiguous_dma(reason="one gain for each partition and band"):
            nc.sync.dma_start(out=rraw[:, :, 0:1], in_=row_gain.rearrange("(i p one) -> p i one", p=P, one=1))


        widen(0, 0, VECTOR)
        widen(0, 1, VECTOR, (0,))
        widen(0, 1, SCALAR, (1, 2, 3))
        widen(1, 0, VECTOR, (0, 1))
        widen(1, 0, SCALAR, (2, 3))
        interleave(0, 1, SCALAR)
        interleave(0, 0, VECTOR)
        interleave(1, 0, VECTOR)
        widen(1, 1, VECTOR, (0, 1, 2))
        quant_steer(0)
        gbank = bank(6)
        for s in range(SLOTS):
            turn(s, s)
            if s == 2:
                widen(1, 1, SCALAR, (LAST_T,))
            empty(s)
            if s == 1:
                nc.tensor.matmul(out=gbank[:, 0:QUART].bitcast(BF16), lhsT=ones[:, 0:P], rhs=gains[:, 0:HALF], start=True, stop=True)
        nc.scalar.copy(out=cgain[:, 0:HALF], in_=gbank[:, 0:QUART].bitcast(BF16))
        quant_echo(0)
        quant_echo(1)
        interleave(1, 1, VECTOR)
        quant_echo(2)
        quant_echo(3)
        first_two(0, 0, 0, 4)
        sort_words(7, SCALAR)
        for s, kb in ((4, 0), (5, 1)):
            turn(s, kb)
            empty(s)
        quant_steer(1)
        gain_two(0, 0, 0)
        first_two(0, 0, 1, 5)
        first_two(0, 1, 0, 6)
        first_two(0, 1, 1, 7)

        sort_words(6, VECTOR)
        for s in (8, 9):
            sort_words(s, SCALAR)
        gain_two(0, 0, 1)
        quant_echo(4)
        gain_two(0, 1, 0)
        for s, kb in zip(range(6, 10), (2, 0, 3, 1)):
            turn(s, kb)
        for s in range(6, 10):
            empty(s)
        sort_words(10, VECTOR)
        quant_echo(6)
        sort_words(11, VECTOR)
        quant_echo(7)
        gain_two(0, 1, 1)
        join(0, 0, VECTOR)
        for u in range(2):
            first_two(1, 0, u, (4, 6)[u])
            for e, kb in ((2, 5), (3, 2)):
                first_four(1, e, (2 * u, 2 * u + 1), kb)

        sums = (0, 3, 6, 2)
        sort_words(12, SCALAR)
        sort_words(13, SCALAR)
        join(0, 1, SCALAR)
        gain_two(1, 0, 0)
        quant_echo(8)
        gain_four(1, 2)
        for s, kb in zip(range(10, 14), (0, 3, 1, 7)):
            turn(s, kb)
            empty(s)
        quant_d(0, 0, HALF)
        gain_two(1, 0, 1)
        gain_four(1, 3)
        quant_echo(10)
        quant_echo(11)
        first_two(2, 0, 0, 4)
        first_two(2, 1, 0, 5)
        for i in range(OPEN):
            second(i, 0, 0, HALF, sums[i])
        join(1, 0, SCALAR)
        sort_words(14, SCALAR)
        sort_words(15, SCALAR)
        widen(0, 2, SCALAR, range(LAST_T))
        gain_two(2, 0, 0)
        gain_two(2, 1, 0)
        first_two(2, 0, 1, 1)
        first_two(2, 1, 1, 7)

        quant_d(1, 0, HALF)
        quant_echo(12)
        for s, kb in ((14, 4), (15, 5)):
            turn(s, kb)
            empty(s)
        gain_two(2, 0, 1)
        gain_two(2, 1, 1)
        for i in range(OPEN):
            second(i, 1, 0, HALF)
        join(2, 0, SCALAR)
        join(2, 1, SCALAR)
        widen(0, 2, SCALAR, (LAST_T,))
        quant_echo(14)
        work = (1, 7, 4, 5)
        for u in range(2):
            for q in range(2):
                first_two(3, q, u, work[2 * u + q])
        widen(1, 2, SCALAR)
        interleave(0, 2, SCALAR)
        gain_two(3, 0, 0)
        quant_d(2, 0, HALF)
        for g in range(2):
            second(OPEN, g, 0, HALF, work[0])
        for i in range(OPEN + 1):
            second(i, 2, 0, HALF)
        gain_two(3, 1, 0)
        gain_two(3, 0, 1)
        join(3, 0, SCALAR)
        gain_two(3, 1, 1)
        interleave(1, 2, VECTOR)
        join(3, 1, VECTOR)
        quant_d(3, 0, QUART)
        quant_d(3, QUART, HALF)
        quant_steer(2)
        nc.scalar.copy(out=rgain[:], in_=rraw[:, :, 0])
        widen(0, 3, SCALAR)
        widen(1, 3, VECTOR)
        for i in (OPEN + 1, OPEN + 2):
            for g in range(LAST_G):
                second(i, g, 0, HALF, work[i - OPEN])
        for i in range(OPEN, LAST_BAND):
            close(i, 0)
        interleave(0, 3, VECTOR)

        steps = [(g, q) for q in (2, 3) for g in range(LAST_G)] + [(LAST_G, 2), (LAST_G, 3)]
        step_banks = (work[3], work[0], work[1], work[2])
        held = [(i, g) for g in range(LAST_G) for i in range(OPEN)]

        def run_held(passes):
            for i, g in passes:
                second(i, g, HALF, N, sums[(i + 1) % OPEN])

        for step, (g, q) in enumerate(steps[:-1]):
            first_two(g, q, 0, step_banks[2 * (step % 2)])
            if step == 0:
                close(0, 0)
                interleave(1, 3, SCALAR)
            first_two(g, q, 1, step_banks[2 * (step % 2) + 1])
            gain_two(g, q, 0)
            gain_two(g, q, 1)
            if step == 1:
                quant_steer(3)
            if step > 0:
                before_g, before_q = steps[step - 1]
                quant_d(before_g, before_q * QUART, (before_q + 1) * QUART)
            join(g, q, SCALAR)
            if step + 1 < OPEN:
                close(step + 1, 0)
            band7_g = step - 2
            if 0 <= band7_g < G:
                second(LAST_BAND, band7_g, 0, HALF, sums[0])
            if band7_g == LAST_G:
                finish(LAST_BAND, 0, HALF)
        run_held(held[:2])
        for e, kb in zip((6, 7), step_banks[2:]):
            first_four(LAST_G, e, range(SLOTS), kb)
        for e in (6, 7):
            gain_four(LAST_G, e)
        quant_d(LAST_G, HALF, HALF + QUART)
        quant_d(LAST_G, HALF + QUART, N)
        run_held(held[2:-1])
        for i in range(OPEN):
            if i == OPEN - 1:
                run_held(held[-1:])
            close(i, HALF)
        pieces = [(i, HALF, N) for i in range(OPEN, LAST_BAND - 1)]
        pieces += [(LAST_BAND - 1, HALF, HALF + QUART), (LAST_BAND - 1, HALF + QUART, N)]
        pieces += [(LAST_BAND, HALF, HALF + QUART), (LAST_BAND, HALF + QUART, N - P), (LAST_BAND, N - P, N)]
        for (i, n0, n1), kb in zip(pieces, step_banks + sums[1:]):
            for g in range(G):
                second(i, g, n0, n1, kb)
            finish(i, n0, n1)
